import numpy as np
import ml_dtypes


def mxq(x, axis, fmt="e4m3"):
    dtype, down = {"e4m3": (ml_dtypes.float8_e4m3fn, 7), "e5m2": (ml_dtypes.float8_e5m2, 14)}[fmt]
    v = np.moveaxis(np.asarray(x, np.float32).astype(ml_dtypes.bfloat16).astype(np.float64), axis, -1)
    blocks = v.reshape(v.shape[:-1] + (-1, 32))
    amax = np.abs(blocks).max(-1, keepdims=True)
    byte = np.maximum(np.where(amax > 0, np.frexp(amax)[1] - 1 + 127, 0) - down, 1)
    scale = np.exp2(byte - 127.0)
    codes = (blocks / scale).astype(np.float32).astype(dtype).astype(np.float64)
    return np.moveaxis((codes * scale).reshape(v.shape), -1, axis)


WIDE = False


def mx_kscale(k):
    if not WIDE:
        return np.ones(k)
    levels = np.array([10, -10, 5, -5, 0])
    if k % 512:
        return np.exp2(np.random.permutation(np.resize(levels, k // 32))).repeat(32)
    a = np.empty((k // 512, 16))
    for p in range(k // 512):
        a[p, :8] = np.random.permutation(np.resize(levels, 8))
        for g in range(8):
            far = levels[np.abs(levels - a[p, g]) >= 10]
            a[p, g + 8] = far[np.random.randint(len(far))]
    return np.exp2(a.ravel()).repeat(32)


def f64(x):
    return np.asarray(x).astype(np.float64)


def striped(idx):
    return np.tile(idx.reshape(-1, 16).T, (8, 1)).astype(np.uint16)


def unstriped(offs):
    return offs[:16].T.reshape(-1).astype(np.int64)


E2M1 = np.array([0.0, 0.5, 1.0, 1.5, 2.0, 3.0, 4.0, 6.0, -0.0, -0.5, -1.0, -1.5, -2.0, -3.0, -4.0, -6.0])


def pack_weight(w, fmt):
    k, n = w.shape
    w = f64(np.asarray(w, np.float32).astype(ml_dtypes.bfloat16)).reshape(k // 32, 32, n)
    amax = np.abs(w).max(1)
    if fmt == "e4m3":
        byte = np.frexp(amax)[1] - 1 + 127 - 7
    else:
        mant, ex = np.frexp(amax / 6.0)
        byte = np.where(mant > 0.5, ex, ex - 1) + 127
    byte = np.clip(np.where(amax > 0, byte, 1), 1, 254)
    scaled = (w * np.exp2(127.0 - byte)[:, None, :]).reshape(k, n).astype(np.float32)
    by_word = np.ascontiguousarray(scaled.reshape(k // 512, 128, 4, n).transpose(0, 1, 3, 2))
    if fmt == "e4m3":
        words = by_word.astype(ml_dtypes.float8_e4m3fn).view(np.uint8)
    else:
        c = by_word.astype(ml_dtypes.float4_e2m1fn).view(np.uint8) & 0xF
        words = (c[..., 0::2] | (c[..., 1::2] << 4)).reshape(k // 512, 128, 2 * n)
    return np.ascontiguousarray(words), np.ascontiguousarray(byte.astype(np.uint8).reshape(k // 512, 16, n))


def unpack_weight(words, scales, fmt):
    g, _, n = scales.shape
    words = np.ascontiguousarray(words).reshape(g, 128, n, -1)
    if fmt == "e4m3":
        vals = words.view(ml_dtypes.float8_e4m3fn).astype(np.float64)
    else:
        nib = np.empty((g, 128, n, 4), np.uint8)
        nib[..., 0::2] = words & 0xF
        nib[..., 1::2] = words >> 4
        vals = E2M1[nib]
    vals = vals * np.repeat(np.exp2(scales.astype(np.float64) - 127.0), 8, axis=1)[..., None]
    return vals.transpose(0, 1, 3, 2).reshape(g * 512, n)


def gelu(v):
    return 0.5 * v * (1.0 + np.tanh(np.sqrt(2.0 / np.pi) * (v + 0.044715 * v**3)))


K, T, Q, E, C, D, H = 512, 1024, 512, 8, 128, 128, 0
N = 512


def by_expert(wq, xq, C):
    return np.concatenate([wq[e].T @ xq[:, e * C:(e + 1) * C] for e in range(E)], axis=1)


def setup_inputs():
    n = np.random.standard_normal
    s = mx_kscale(K)
    slot_token = np.random.permutation(T)[:E * C]
    slots2 = np.concatenate([np.random.permutation(Q)[:D] for e in range(E)])
    x = pack_weight(n((K, Q)) * s[:, None], "e4m3")
    w = [pack_weight(m, "e4m3") for m in n((E, K, N)) / np.sqrt(K) / s[None, :, None]]
    return {
        "x_words": x[0],
        "x_scales": x[1],
        "xo": (n((K, T)) * s[:, None]).astype(np.float32),
        "w_words": np.stack([m[0] for m in w]),
        "w_scales": np.stack([m[1] for m in w]),
        "gate": np.tile(np.random.uniform(0.2, 1.0, E * C), (128, 1)).astype(np.float32),
        "offs": striped(slot_token),
        "offs2": striped(slots2),
    }


def reference(x_words, x_scales, xo, w_words, w_scales, gate, offs, offs2):
    w = np.stack([unpack_weight(w_words[e], w_scales[e], "e4m3") for e in range(E)])
    idx, idx2 = unstriped(offs), unstriped(offs2)
    xq = mxq(f64(xo)[:, idx], 0, "e4m3")
    rq = unpack_weight(x_words, x_scales, "e4m3")[:, idx2]
    y = gelu(by_expert(w, xq, C))
    z = gelu(by_expert(w, rq, D))
    own = np.zeros((N, T))
    own[:, idx] = f64(gate[:1]) * y
    return np.concatenate([own, z], axis=1)

@@ -1,0 +1,175 @@
+from contextlib import ExitStack
+
+import concourse.mybir as mybir
+
+K, T, Q, E, C, N = 512, 1024, 512, 8, 128, 512
+FLOPS = 2 * K * N * 2 * E * C
+
+F32 = mybir.dt.float32
+BF16 = mybir.dt.bfloat16
+I32 = mybir.dt.int32
+U32 = mybir.dt.uint32
+U16 = mybir.dt.uint16
+U8 = mybir.dt.uint8
+FP8X4 = mybir.dt.float8_e4m3fn_x4
+GELU = mybir.ActivationFunctionType.Gelu_apprx_tanh
+COPY = mybir.ActivationFunctionType.Copy
+MULT = mybir.AluOpType.mult
+
+P = 128
+PACK = 4
+NT = N // P
+OWN_CHUNKS = ((0,), (1,), (2,), (3,), (4, 5), (6, 7))
+W_LOADS = ((0,), (1,), (2, 3), (4, 5), (6, 7))
+
+
+def tile_moe_loc_lin_gelu_kernel(tc, x_words, x_scales, xo, w_words, w_scales, gate, offs, offs2, out):
+    nc = tc.nc
+    with ExitStack() as ctx:
+        keep = ctx.enter_context(tc.tile_pool(name="keep", bufs=1))
+        own_psum = ctx.enter_context(tc.psum_pool(name="own_psum", bufs=4))
+        far_psum = ctx.enter_context(tc.psum_pool(name="far_psum", bufs=4))
+
+        own_list = keep.tile([P, E * C // 16], U16, name="own_list")
+        far_list = keep.tile([P, E * C // 16], U16, name="far_list")
+        far_words = keep.tile([P, Q], I32, name="far_words", align_bytes=64)
+        far_bytes = keep.tile([P, Q], U8, name="far_bytes", align_bytes=64)
+        w_planes = [keep.tile([P, N], U8, name="w_plane%d" % g, align_bytes=64) for g in range(2)]
+        x_f32 = [keep.tile([P, T], F32, name="x_f32_%d" % j, align_bytes=64) for j in range(PACK)]
+        x_bf16 = [keep.tile([P, T], BF16, name="x_bf16_%d" % j, align_bytes=64) for j in range(PACK)]
+        gate_first = keep.tile([P, 2 * C], F32, name="gate_first")
+        gate_rest = keep.tile([P, (E - 2) * C], F32, name="gate_rest")
+
+        warm = keep.tile([P, 16], F32, name="warm")
+        warm_out = keep.tile([P, 16], F32, name="warm_out")
+        nc.vector.memset(far_bytes[:].bitcast(I32), 0)
+        for plane in w_planes:
+            nc.vector.memset(plane[:].bitcast(I32), 0)
+        nc.vector.memset(warm[:], 0.0)
+        nc.scalar.activation(warm_out[:], warm[:], GELU)
+
+        w_tiles = {}
+
+        def load_w(experts):
+            tile = keep.tile([P, len(experts), N], I32, name="w_codes%d" % experts[0], align_bytes=64)
+            src = w_words[experts[0] : experts[-1] + 1, 0].rearrange("e p n d -> p e (n d)").bitcast(I32)
+            nc.sync.dma_start(tile[:], src)
+            for i, e in enumerate(experts):
+                w_tiles[e] = tile[:, i, :]
+
+        def load_w_scales(g):
+            for quad in range(4):
+                nc.sync.dma_start(
+                    w_planes[g][32 * quad : 32 * quad + 16, :].bitcast(I32),
+                    w_scales[4 * g : 4 * g + 4, 0, 4 * quad : 4 * quad + 4, :].bitcast(I32),
+                )
+
+        nc.sync.dma_start(far_list[:], offs2)
+        nc.sync.dma_start(own_list[:], offs)
+        nc.sync.dma_start(far_words[:], x_words[0].rearrange("p t d -> p (t d)").bitcast(I32))
+        for quad in range(4):
+            nc.gpsimd.dma_start(
+                far_bytes[32 * quad : 32 * quad + 4, :].bitcast(I32),
+                x_scales[0, 4 * quad : 4 * quad + 4, :].bitcast(I32),
+            )
+        xo_planes = xo.rearrange("(p j) t -> p j t", j=PACK)
+        for j in range(PACK):
+            nc.sync.dma_start(x_f32[j][:], xo_planes[:, j, :])
+        load_w(W_LOADS[0])
+        load_w_scales(0)
+        nc.sync.dma_start(gate_first[:], gate[:, : 2 * C])
+        load_w(W_LOADS[1])
+        load_w(W_LOADS[2])
+        nc.sync.dma_start(gate_rest[:], gate[:, 2 * C :])
+        load_w_scales(1)
+        load_w(W_LOADS[3])
+        load_w(W_LOADS[4])
+
+        def gate_of(s0, n):
+            return gate_first[:, s0 : s0 + n] if s0 < 2 * C else gate_rest[:, s0 - 2 * C : s0 - 2 * C + n]
+
+        def multiply(acc, e, t, codes, scales):
+            cols = slice(t * P, (t + 1) * P)
+            nc.tensor.matmul_mx(
+                out=acc,
+                lhsT=w_tiles[e][:, cols].bitcast(FP8X4),
+                lhsT_scale=w_planes[e // 4][4 * (e % 4) :, cols],
+                rhs=codes.bitcast(FP8X4),
+                rhs_scale=scales,
+                start=True,
+                stop=True,
+            )
+
+        far_codes = [keep.tile([P, 2 * C], U32, name="far_codes%d" % h, align_bytes=64) for h in range(4)]
+        far_scales = [keep.tile([P, 2 * C], U8, name="far_scales%d" % h, align_bytes=64) for h in range(4)]
+        for h in range(4):
+            nc.vector.tensor_copy(far_codes[h][:], far_words[:].bitcast(U32).indirect(far_list[:, 16 * h : 16 * h + 16]))
+
+        for j in range(PACK):
+            nc.scalar.copy(x_bf16[j][:], x_f32[j][:])
+
+        own_out = [keep.tile([P, T], F32, name="own_out%d" % t) for t in range(NT)]
+        state = {}
+
+        def gather(c):
+            experts = OWN_CHUNKS[c]
+            s0, n = experts[0] * C, len(experts) * C
+            grouped = keep.tile([P, n, PACK], BF16, name="grouped%d" % c, align_bytes=64)
+            offsets = own_list[:, s0 // 16 : (s0 + n) // 16]
+            for j in range(PACK):
+                if c == 0:
+                    nc.vector.tensor_copy(grouped[:, :, j], x_f32[j][:].indirect(offsets))
+                else:
+                    nc.scalar.activation(grouped[:, :, j], x_bf16[j][:].indirect(offsets), COPY)
+            state[c] = grouped
+
+        def compute(c):
+            experts = OWN_CHUNKS[c]
+            n = len(experts) * C
+            codes = keep.tile([P, n], U32, name="codes%d" % c, align_bytes=64)
+            scales = keep.tile([P, n], U8, name="scales%d" % c, align_bytes=64)
+            nc.vector.quantize_mx(out=codes[:].bitcast(FP8X4), scales=scales[:], in_=state[c][:].rearrange("p s j -> p (s j)"))
+            halves = []
+            for half in range(2):
+                acc = own_psum.tile([P, 2, n], F32, name="own_acc", tag="own_acc")
+                for u in range(2):
+                    for i, e in enumerate(experts):
+                        slots = slice(i * C, (i + 1) * C)
+                        multiply(acc[:, u, slots], e, 2 * half + u, codes[:, slots], scales[:, slots])
+                y = keep.tile([P, 2, n], F32, name="y%d_%d" % (c, half))
+                nc.scalar.activation(y[:], acc[:], GELU)
+                halves.append(y)
+            state[c] = halves
+
+        def scatter(c):
+            experts = OWN_CHUNKS[c]
+            s0, n = experts[0] * C, len(experts) * C
+            offsets = own_list[:, s0 // 16 : (s0 + n) // 16]
+            for t in range(NT):
+                nc.vector.tensor_tensor(own_out[t][:].indirect(offsets), state[c][t // 2][:, t % 2, :], gate_of(s0, n), MULT)
+                if c == len(OWN_CHUNKS) - 1:
+                    nc.sync.dma_start(out[t * P : (t + 1) * P, :T], own_out[t][:])
+
+        def far(g):
+            for t in range(NT):
+                acc = far_psum.tile([P, 4 * C], F32, name="far_acc", tag="far_acc")
+                for i in range(4):
+                    e = 4 * g + i
+                    slots = slice((e % 2) * C, (e % 2 + 1) * C)
+                    multiply(acc[:, i * C : (i + 1) * C], e, t, far_codes[e // 2][:, slots], far_scales[e // 2][:, slots])
+                z = keep.tile([P, 4 * C], F32, name="z%d_%d" % (g, t))
+                nc.scalar.activation(z[:], acc[:], GELU)
+                nc.sync.dma_start(out[t * P : (t + 1) * P, T + g * 4 * C : T + (g + 1) * 4 * C], z[:])
+
+        last = len(OWN_CHUNKS) - 1
+        gather(0)
+        compute(0)
+        for h in range(4):
+            nc.vector.tensor_copy(far_scales[h][:], far_bytes[:].indirect(far_list[:, 16 * h : 16 * h + 16]))
+        for c in range(last):
+            gather(c + 1)
+            compute(c + 1)
+            scatter(c)
+        far(0)
+        far(1)
+        scatter(last)

@@ -19,7 +19,6 @@ MULT = mybir.AluOpType.mult
 P = 128
 PACK = 4
 NT = N // P
-OWN_CHUNKS = ((0,), (1,), (2,), (3,), (4, 5), (6, 7))
 W_LOADS = ((0,), (1,), (2, 3), (4, 5), (6, 7))
 
 
@@ -35,17 +34,18 @@ def tile_moe_loc_lin_gelu_kernel(tc, x_words, x_scales, xo, w_words, w_scales, g
         far_words = keep.tile([P, Q], I32, name="far_words", align_bytes=64)
         far_bytes = keep.tile([P, Q], U8, name="far_bytes", align_bytes=64)
         w_planes = [keep.tile([P, N], U8, name="w_plane%d" % g, align_bytes=64) for g in range(2)]
-        x_f32 = [keep.tile([P, T], F32, name="x_f32_%d" % j, align_bytes=64) for j in range(PACK)]
+        x_f32 = [
+            keep.tile([P, T], F32, name="x_f32_%d" % j, align_bytes=64, tag="stage" if j == PACK - 1 else "x_f32_%d" % j)
+            for j in range(PACK)
+        ]
         x_bf16 = [keep.tile([P, T], BF16, name="x_bf16_%d" % j, align_bytes=64) for j in range(PACK)]
         gate_first = keep.tile([P, 2 * C], F32, name="gate_first")
         gate_rest = keep.tile([P, (E - 2) * C], F32, name="gate_rest")
 
         warm = keep.tile([P, 16], F32, name="warm")
         warm_out = keep.tile([P, 16], F32, name="warm_out")
-        nc.vector.memset(far_bytes[:].bitcast(I32), 0)
-        for plane in w_planes:
-            nc.vector.memset(plane[:].bitcast(I32), 0)
         nc.vector.memset(warm[:], 0.0)
+        nc.vector.memset(w_planes[1][:].bitcast(I32), 0)
         nc.scalar.activation(warm_out[:], warm[:], GELU)
 
         w_tiles = {}
@@ -60,17 +60,17 @@ def tile_moe_loc_lin_gelu_kernel(tc, x_words, x_scales, xo, w_words, w_scales, g
         def load_w_scales(g):
             for quad in range(4):
                 nc.sync.dma_start(
-                    w_planes[g][32 * quad : 32 * quad + 16, :].bitcast(I32),
-                    w_scales[4 * g : 4 * g + 4, 0, 4 * quad : 4 * quad + 4, :].bitcast(I32),
+                    w_planes[g][32 * quad : 32 * quad + 4 * (E - 4 * g), :].bitcast(I32),
+                    w_scales[4 * g :, 0, 4 * quad : 4 * quad + 4, :].bitcast(I32),
                 )
 
         nc.sync.dma_start(far_list[:], offs2)
         nc.sync.dma_start(own_list[:], offs)
         nc.sync.dma_start(far_words[:], x_words[0].rearrange("p t d -> p (t d)").bitcast(I32))
         for quad in range(4):
-            nc.gpsimd.dma_start(
-                far_bytes[32 * quad : 32 * quad + 4, :].bitcast(I32),
-                x_scales[0, 4 * quad : 4 * quad + 4, :].bitcast(I32),
+            nc.sync.dma_start(
+                far_bytes[32 * quad : 32 * quad + 32, :].bitcast(I32),
+                x_scales[0, 4 * quad : 4 * quad + 4, :].bitcast(I32).unsqueeze(0).broadcast_to([8, 4, Q // 4]),
             )
         xo_planes = xo.rearrange("(p j) t -> p j t", j=PACK)
         for j in range(PACK):
@@ -101,75 +101,84 @@ def tile_moe_loc_lin_gelu_kernel(tc, x_words, x_scales, xo, w_words, w_scales, g
             )
 
         far_codes = [keep.tile([P, 2 * C], U32, name="far_codes%d" % h, align_bytes=64) for h in range(4)]
-        far_scales = [keep.tile([P, 2 * C], U8, name="far_scales%d" % h, align_bytes=64) for h in range(4)]
+        far_scales = {}
+
+        def gather_far_bytes(g, tag):
+            far_scales[g] = keep.tile([P, 4 * C], U8, name="far_scales%d" % g, align_bytes=64, tag=tag)
+            for h in range(2):
+                col = 32 * g + 16 * h
+                nc.vector.tensor_copy(
+                    far_scales[g][:, 2 * C * h : 2 * C * (h + 1)], far_bytes[:].indirect(far_list[:, col : col + 16])
+                )
+
         for h in range(4):
             nc.vector.tensor_copy(far_codes[h][:], far_words[:].bitcast(U32).indirect(far_list[:, 16 * h : 16 * h + 16]))
+        gather_far_bytes(0, "far_scales0")
 
         for j in range(PACK):
             nc.scalar.copy(x_bf16[j][:], x_f32[j][:])
 
         own_out = [keep.tile([P, T], F32, name="own_out%d" % t) for t in range(NT)]
-        state = {}
+        grouped, results = {}, {}
 
-        def gather(c):
-            experts = OWN_CHUNKS[c]
-            s0, n = experts[0] * C, len(experts) * C
-            grouped = keep.tile([P, n, PACK], BF16, name="grouped%d" % c, align_bytes=64)
-            offsets = own_list[:, s0 // 16 : (s0 + n) // 16]
+        def gather(e):
+            grouped[e] = keep.tile([P, C, PACK], BF16, name="grouped%d" % e, align_bytes=64, tag="first" if e == 0 else "stage")
+            offsets = own_list[:, e * C // 16 : (e + 1) * C // 16]
             for j in range(PACK):
-                if c == 0:
-                    nc.vector.tensor_copy(grouped[:, :, j], x_f32[j][:].indirect(offsets))
+                if e == 0:
+                    nc.vector.tensor_copy(grouped[e][:, :, j], x_f32[j][:].indirect(offsets))
                 else:
-                    nc.scalar.activation(grouped[:, :, j], x_bf16[j][:].indirect(offsets), COPY)
-            state[c] = grouped
+                    nc.scalar.activation(grouped[e][:, :, j], x_bf16[j][:].indirect(offsets), COPY)
 
-        def compute(c):
-            experts = OWN_CHUNKS[c]
-            n = len(experts) * C
-            codes = keep.tile([P, n], U32, name="codes%d" % c, align_bytes=64)
-            scales = keep.tile([P, n], U8, name="scales%d" % c, align_bytes=64)
-            nc.vector.quantize_mx(out=codes[:].bitcast(FP8X4), scales=scales[:], in_=state[c][:].rearrange("p s j -> p (s j)"))
-            halves = []
-            for half in range(2):
-                acc = own_psum.tile([P, 2, n], F32, name="own_acc", tag="own_acc")
-                for u in range(2):
-                    for i, e in enumerate(experts):
-                        slots = slice(i * C, (i + 1) * C)
-                        multiply(acc[:, u, slots], e, 2 * half + u, codes[:, slots], scales[:, slots])
-                y = keep.tile([P, 2, n], F32, name="y%d_%d" % (c, half))
+        def compute(e):
+            codes = keep.tile([P, C], U32, name="codes%d" % e, align_bytes=64, tag="lead%d" % (e - 1))
+            scales = keep.tile([P, C], U8, name="scales%d" % e, align_bytes=64, tag="scales%d" % e)
+            nc.vector.quantize_mx(out=codes[:].bitcast(FP8X4), scales=scales[:], in_=grouped[e][:].rearrange("p s j -> p (s j)"))
+            lead = 2 if e == 0 else 1
+            for tiles, tag in ((range(lead), "lead%d" % e), (range(lead, NT), "rest%d" % e)):
+                acc = own_psum.tile([P, len(tiles), C], F32, name="own_acc", tag="own_acc")
+                for u, t in enumerate(tiles):
+                    multiply(acc[:, u, :], e, t, codes[:], scales[:])
+                y = keep.tile([P, len(tiles), C], F32, name="y_" + tag, align_bytes=64, tag=tag)
                 nc.scalar.activation(y[:], acc[:], GELU)
-                halves.append(y)
-            state[c] = halves
+                for u, t in enumerate(tiles):
+                    results[e, t] = y[:, u, :]
+                if tiles[0] == 0 and e + 1 < E:
+                    gather(e + 1)
 
-        def scatter(c):
-            experts = OWN_CHUNKS[c]
-            s0, n = experts[0] * C, len(experts) * C
-            offsets = own_list[:, s0 // 16 : (s0 + n) // 16]
-            for t in range(NT):
-                nc.vector.tensor_tensor(own_out[t][:].indirect(offsets), state[c][t // 2][:, t % 2, :], gate_of(s0, n), MULT)
-                if c == len(OWN_CHUNKS) - 1:
-                    nc.sync.dma_start(out[t * P : (t + 1) * P, :T], own_out[t][:])
+        done = [0] * NT
 
-        def far(g):
-            for t in range(NT):
-                acc = far_psum.tile([P, 4 * C], F32, name="far_acc", tag="far_acc")
-                for i in range(4):
-                    e = 4 * g + i
-                    slots = slice((e % 2) * C, (e % 2 + 1) * C)
-                    multiply(acc[:, i * C : (i + 1) * C], e, t, far_codes[e // 2][:, slots], far_scales[e // 2][:, slots])
-                z = keep.tile([P, 4 * C], F32, name="z%d_%d" % (g, t))
-                nc.scalar.activation(z[:], acc[:], GELU)
-                nc.sync.dma_start(out[t * P : (t + 1) * P, T + g * 4 * C : T + (g + 1) * 4 * C], z[:])
+        def scatter(e, t):
+            offsets = own_list[:, e * C // 16 : (e + 1) * C // 16]
+            nc.vector.tensor_tensor(own_out[t][:].indirect(offsets), results[e, t], gate_of(e * C, C), MULT)
+            done[t] += 1
+            if done[t] == E:
+                nc.sync.dma_start(out[t * P : (t + 1) * P, :T], own_out[t][:])
 
-        last = len(OWN_CHUNKS) - 1
+        def far(k, tag):
+            g, t = divmod(k, NT)
+            acc = far_psum.tile([P, 4 * C], F32, name="far_acc", tag="far_acc")
+            for i in range(4):
+                e = 4 * g + i
+                slots = slice((e % 2) * C, (e % 2 + 1) * C)
+                multiply(acc[:, i * C : (i + 1) * C], e, t, far_codes[e // 2][:, slots], far_scales[g][:, i * C : (i + 1) * C])
+            z = keep.tile([P, 4 * C], F32, name="z%d" % k, align_bytes=64, tag=tag)
+            nc.scalar.activation(z[:], acc[:], GELU)
+            nc.sync.dma_start(out[t * P : (t + 1) * P, T + g * 4 * C : T + (g + 1) * 4 * C], z[:])
+
         gather(0)
         compute(0)
-        for h in range(4):
-            nc.vector.tensor_copy(far_scales[h][:], far_bytes[:].indirect(far_list[:, 16 * h : 16 * h + 16]))
-        for c in range(last):
-            gather(c + 1)
-            compute(c + 1)
-            scatter(c)
-        far(0)
-        far(1)
-        scatter(last)
+        gather_far_bytes(1, "first")
+        for e in range(E - 1):
+            lead = 2 if e == 0 else 1
+            for t in range(lead):
+                scatter(e, t)
+            compute(e + 1)
+            far(e, "scales%d" % (e + 1))
+            if e == E - 2:
+                far(E - 1, "lead%d" % e)
+            for t in range(lead, NT - 1 if e == E - 2 else NT):
+                scatter(e, t)
+        for t in (0, 1, 3, 2):
+            scatter(E - 1, t)
+        scatter(E - 2, NT - 1)

@@ -15,10 +15,12 @@ FP8X4 = mybir.dt.float8_e4m3fn_x4
 GELU = mybir.ActivationFunctionType.Gelu_apprx_tanh
 COPY = mybir.ActivationFunctionType.Copy
 MULT = mybir.AluOpType.mult
+ADD = mybir.AluOpType.add
 
 P = 128
 PACK = 4
 NT = N // P
+OWN_CHUNKS = ((0,), (1,), (2, 3), (4, 5), (6, 7))
 W_LOADS = ((0,), (1,), (2, 3), (4, 5), (6, 7))
 
 
@@ -34,10 +36,7 @@ def tile_moe_loc_lin_gelu_kernel(tc, x_words, x_scales, xo, w_words, w_scales, g
         far_words = keep.tile([P, Q], I32, name="far_words", align_bytes=64)
         far_bytes = keep.tile([P, Q], U8, name="far_bytes", align_bytes=64)
         w_planes = [keep.tile([P, N], U8, name="w_plane%d" % g, align_bytes=64) for g in range(2)]
-        x_f32 = [
-            keep.tile([P, T], F32, name="x_f32_%d" % j, align_bytes=64, tag="stage" if j == PACK - 1 else "x_f32_%d" % j)
-            for j in range(PACK)
-        ]
+        x_f32 = [keep.tile([P, T], F32, name="x_f32_%d" % j, align_bytes=64) for j in range(PACK)]
         x_bf16 = [keep.tile([P, T], BF16, name="x_bf16_%d" % j, align_bytes=64) for j in range(PACK)]
         gate_first = keep.tile([P, 2 * C], F32, name="gate_first")
         gate_rest = keep.tile([P, (E - 2) * C], F32, name="gate_rest")
@@ -65,15 +64,17 @@ def tile_moe_loc_lin_gelu_kernel(tc, x_words, x_scales, xo, w_words, w_scales, g
                 )
 
         nc.sync.dma_start(far_list[:], offs2)
-        nc.sync.dma_start(own_list[:], offs)
         nc.sync.dma_start(far_words[:], x_words[0].rearrange("p t d -> p (t d)").bitcast(I32))
+        nc.sync.dma_start(own_list[:], offs)
+        xo_planes = xo.rearrange("(p j) t -> p j t", j=PACK)
+        for j in range(2):
+            nc.sync.dma_start(x_f32[j][:], xo_planes[:, j, :])
         for quad in range(4):
             nc.sync.dma_start(
                 far_bytes[32 * quad : 32 * quad + 32, :].bitcast(I32),
                 x_scales[0, 4 * quad : 4 * quad + 4, :].bitcast(I32).unsqueeze(0).broadcast_to([8, 4, Q // 4]),
             )
-        xo_planes = xo.rearrange("(p j) t -> p j t", j=PACK)
-        for j in range(PACK):
+        for j in range(2, PACK):
             nc.sync.dma_start(x_f32[j][:], xo_planes[:, j, :])
         load_w(W_LOADS[0])
         load_w_scales(0)
@@ -103,56 +104,64 @@ def tile_moe_loc_lin_gelu_kernel(tc, x_words, x_scales, xo, w_words, w_scales, g
         far_codes = [keep.tile([P, 2 * C], U32, name="far_codes%d" % h, align_bytes=64) for h in range(4)]
         far_scales = {}
 
-        def gather_far_bytes(g, tag):
-            far_scales[g] = keep.tile([P, 4 * C], U8, name="far_scales%d" % g, align_bytes=64, tag=tag)
-            for h in range(2):
-                col = 32 * g + 16 * h
-                nc.vector.tensor_copy(
-                    far_scales[g][:, 2 * C * h : 2 * C * (h + 1)], far_bytes[:].indirect(far_list[:, col : col + 16])
-                )
+        def gather_far_bytes(h, tag):
+            far_scales[h] = keep.tile([P, 2 * C], U8, name="far_scales%d" % h, align_bytes=64, tag=tag)
+            nc.vector.tensor_copy(far_scales[h][:], far_bytes[:].indirect(far_list[:, 16 * h : 16 * h + 16]))
 
         for h in range(4):
             nc.vector.tensor_copy(far_codes[h][:], far_words[:].bitcast(U32).indirect(far_list[:, 16 * h : 16 * h + 16]))
-        gather_far_bytes(0, "far_scales0")
+        for h in range(3):
+            gather_far_bytes(h, "far_scales%d" % h)
 
-        for j in range(PACK):
-            nc.scalar.copy(x_bf16[j][:], x_f32[j][:])
+        for j in range(PACK - 1):
+            nc.gpsimd.tensor_scalar(x_bf16[j][:], x_f32[j][:], 1.0, 0.0, MULT, ADD)
 
         own_out = [keep.tile([P, T], F32, name="own_out%d" % t) for t in range(NT)]
         grouped, results = {}, {}
 
-        def gather(e):
-            grouped[e] = keep.tile([P, C, PACK], BF16, name="grouped%d" % e, align_bytes=64, tag="first" if e == 0 else "stage")
-            offsets = own_list[:, e * C // 16 : (e + 1) * C // 16]
+        def span(c):
+            return OWN_CHUNKS[c][0] * C, len(OWN_CHUNKS[c]) * C
+
+        def gather(c):
+            s0, n = span(c)
+            tag = ("first", "second")[c] if c < 2 else "scales0"
+            grouped[c] = keep.tile([P, n, PACK], BF16, name="grouped%d" % c, align_bytes=64, tag=tag)
+            offsets = own_list[:, s0 // 16 : (s0 + n) // 16]
             for j in range(PACK):
-                if e == 0:
-                    nc.vector.tensor_copy(grouped[e][:, :, j], x_f32[j][:].indirect(offsets))
+                if c == 0 and j >= 2:
+                    nc.vector.tensor_copy(grouped[c][:, :, j], x_f32[j][:].indirect(offsets))
                 else:
-                    nc.scalar.activation(grouped[e][:, :, j], x_bf16[j][:].indirect(offsets), COPY)
+                    nc.scalar.activation(grouped[c][:, :, j], x_bf16[j][:].indirect(offsets), COPY)
 
-        def compute(e):
-            codes = keep.tile([P, C], U32, name="codes%d" % e, align_bytes=64, tag="lead%d" % (e - 1))
-            scales = keep.tile([P, C], U8, name="scales%d" % e, align_bytes=64, tag="scales%d" % e)
-            nc.vector.quantize_mx(out=codes[:].bitcast(FP8X4), scales=scales[:], in_=grouped[e][:].rearrange("p s j -> p (s j)"))
-            lead = 2 if e == 0 else 1
-            for tiles, tag in ((range(lead), "lead%d" % e), (range(lead, NT), "rest%d" % e)):
-                acc = own_psum.tile([P, len(tiles), C], F32, name="own_acc", tag="own_acc")
-                for u, t in enumerate(tiles):
-                    multiply(acc[:, u, :], e, t, codes[:], scales[:])
-                y = keep.tile([P, len(tiles), C], F32, name="y_" + tag, align_bytes=64, tag=tag)
-                nc.scalar.activation(y[:], acc[:], GELU)
-                for u, t in enumerate(tiles):
-                    results[e, t] = y[:, u, :]
-                if tiles[0] == 0 and e + 1 < E:
-                    gather(e + 1)
+        def activate(c, tiles, codes, scales):
+            n = span(c)[1]
+            acc = own_psum.tile([P, len(tiles), n], F32, name="own_acc", tag="own_acc")
+            for u, t in enumerate(tiles):
+                for i, e in enumerate(OWN_CHUNKS[c]):
+                    slots = slice(i * C, (i + 1) * C)
+                    multiply(acc[:, u, slots], e, t, codes[:, slots], scales[:, slots])
+            tag = "y%d_%d" % (c, tiles[0])
+            y = keep.tile([P, len(tiles), n], F32, name=tag, align_bytes=64, tag=tag)
+            nc.scalar.activation(y[:], acc[:], GELU)
+            for u, t in enumerate(tiles):
+                results[c, t] = y[:, u, :]
 
-        done = [0] * NT
+        def compute(c):
+            n = span(c)[1]
+            codes = keep.tile([P, n], U32, name="codes%d" % c, align_bytes=64, tag="y%d_0" % (c - 1))
+            scales = keep.tile([P, n], U8, name="scales%d" % c, align_bytes=64, tag="scales%d" % c)
+            nc.vector.quantize_mx(out=codes[:].bitcast(FP8X4), scales=scales[:], in_=grouped[c][:].rearrange("p s j -> p (s j)"))
+            activate(c, (0,), codes, scales)
+            activate(c, (1,), codes, scales)
+            if c + 1 < len(OWN_CHUNKS):
+                gather(c + 1)
+            activate(c, (2, 3), codes, scales)
 
-        def scatter(e, t):
-            offsets = own_list[:, e * C // 16 : (e + 1) * C // 16]
-            nc.vector.tensor_tensor(own_out[t][:].indirect(offsets), results[e, t], gate_of(e * C, C), MULT)
-            done[t] += 1
-            if done[t] == E:
+        def scatter(c, t):
+            s0, n = span(c)
+            offsets = own_list[:, s0 // 16 : (s0 + n) // 16]
+            nc.vector.tensor_tensor(own_out[t][:].indirect(offsets), results[c, t], gate_of(s0, n), MULT)
+            if s0 + n == E * C:
                 nc.sync.dma_start(out[t * P : (t + 1) * P, :T], own_out[t][:])
 
         def far(k, tag):
@@ -161,24 +170,24 @@ def tile_moe_loc_lin_gelu_kernel(tc, x_words, x_scales, xo, w_words, w_scales, g
             for i in range(4):
                 e = 4 * g + i
                 slots = slice((e % 2) * C, (e % 2 + 1) * C)
-                multiply(acc[:, i * C : (i + 1) * C], e, t, far_codes[e // 2][:, slots], far_scales[g][:, i * C : (i + 1) * C])
+                multiply(acc[:, i * C : (i + 1) * C], e, t, far_codes[e // 2][:, slots], far_scales[e // 2][:, slots])
             z = keep.tile([P, 4 * C], F32, name="z%d" % k, align_bytes=64, tag=tag)
             nc.scalar.activation(z[:], acc[:], GELU)
             nc.sync.dma_start(out[t * P : (t + 1) * P, T + g * 4 * C : T + (g + 1) * 4 * C], z[:])
 
+        far_slots = {2: ("scales2",), 3: ("scales3", "y2_0"), 4: ("y2_2", "y3_1", "scales0", "scales4", "y3_0")}
         gather(0)
+        nc.scalar.copy(x_bf16[PACK - 1][:], x_f32[PACK - 1][:])
         compute(0)
-        gather_far_bytes(1, "first")
-        for e in range(E - 1):
-            lead = 2 if e == 0 else 1
-            for t in range(lead):
-                scatter(e, t)
-            compute(e + 1)
-            far(e, "scales%d" % (e + 1))
-            if e == E - 2:
-                far(E - 1, "lead%d" % e)
-            for t in range(lead, NT - 1 if e == E - 2 else NT):
-                scatter(e, t)
-        for t in (0, 1, 3, 2):
-            scatter(E - 1, t)
-        scatter(E - 2, NT - 1)
+        gather_far_bytes(3, "first")
+        k = 0
+        for c in range(len(OWN_CHUNKS)):
+            scatter(c, 0)
+            scatter(c, 1)
+            if c + 1 < len(OWN_CHUNKS):
+                compute(c + 1)
+            for tag in far_slots.get(c + 1, ()):
+                far(k, tag)
+                k += 1
+            scatter(c, 2)
+            scatter(c, 3)

@@ -28,13 +28,12 @@ def tile_moe_loc_lin_gelu_kernel(tc, x_words, x_scales, xo, w_words, w_scales, g
     nc = tc.nc
     with ExitStack() as ctx:
         keep = ctx.enter_context(tc.tile_pool(name="keep", bufs=1))
-        own_psum = ctx.enter_context(tc.psum_pool(name="own_psum", bufs=4))
-        far_psum = ctx.enter_context(tc.psum_pool(name="far_psum", bufs=4))
+        psum = ctx.enter_context(tc.psum_pool(name="psum", bufs=1))
 
         own_list = keep.tile([P, E * C // 16], U16, name="own_list")
         far_list = keep.tile([P, E * C // 16], U16, name="far_list")
-        far_words = keep.tile([P, Q], I32, name="far_words", align_bytes=64)
-        far_bytes = keep.tile([P, Q], U8, name="far_bytes", align_bytes=64)
+        far_words = keep.tile([P, 4 * Q], I32, name="far_words", align_bytes=64)
+        far_bytes = keep.tile([P, 2 * Q], U8, name="far_bytes", align_bytes=64)
         w_planes = [keep.tile([P, N], U8, name="w_plane%d" % g, align_bytes=64) for g in range(2)]
         x_f32 = [keep.tile([P, T], F32, name="x_f32_%d" % j, align_bytes=64) for j in range(PACK)]
         x_bf16 = [keep.tile([P, T], BF16, name="x_bf16_%d" % j, align_bytes=64) for j in range(PACK)]
@@ -43,7 +42,9 @@ def tile_moe_loc_lin_gelu_kernel(tc, x_words, x_scales, xo, w_words, w_scales, g
 
         warm = keep.tile([P, 16], F32, name="warm")
         warm_out = keep.tile([P, 16], F32, name="warm_out")
+        nc.vector.memset(far_bytes[:].bitcast(I32), 0)
         nc.vector.memset(warm[:], 0.0)
+        nc.vector.memset(far_words[:, Q:], 0)
         nc.vector.memset(w_planes[1][:].bitcast(I32), 0)
         nc.scalar.activation(warm_out[:], warm[:], GELU)
 
@@ -52,9 +53,9 @@ def tile_moe_loc_lin_gelu_kernel(tc, x_words, x_scales, xo, w_words, w_scales, g
         def load_w(experts):
             tile = keep.tile([P, len(experts), N], I32, name="w_codes%d" % experts[0], align_bytes=64)
             src = w_words[experts[0] : experts[-1] + 1, 0].rearrange("e p n d -> p e (n d)").bitcast(I32)
-            nc.sync.dma_start(tile[:], src)
             for i, e in enumerate(experts):
                 w_tiles[e] = tile[:, i, :]
+            return tile, src
 
         def load_w_scales(g):
             for quad in range(4):
@@ -64,27 +65,29 @@ def tile_moe_loc_lin_gelu_kernel(tc, x_words, x_scales, xo, w_words, w_scales, g
                 )
 
         nc.sync.dma_start(far_list[:], offs2)
-        nc.sync.dma_start(far_words[:], x_words[0].rearrange("p t d -> p (t d)").bitcast(I32))
+        nc.sync.dma_start(far_words[:, :Q], x_words[0].rearrange("p t d -> p (t d)").bitcast(I32))
         nc.sync.dma_start(own_list[:], offs)
         xo_planes = xo.rearrange("(p j) t -> p j t", j=PACK)
         for j in range(2):
             nc.sync.dma_start(x_f32[j][:], xo_planes[:, j, :])
         for quad in range(4):
             nc.sync.dma_start(
-                far_bytes[32 * quad : 32 * quad + 32, :].bitcast(I32),
-                x_scales[0, 4 * quad : 4 * quad + 4, :].bitcast(I32).unsqueeze(0).broadcast_to([8, 4, Q // 4]),
+                far_bytes[32 * quad : 32 * quad + 4, :Q].bitcast(I32),
+                x_scales[0, 4 * quad : 4 * quad + 4, :].bitcast(I32),
             )
         for j in range(2, PACK):
             nc.sync.dma_start(x_f32[j][:], xo_planes[:, j, :])
-        load_w(W_LOADS[0])
+        loads = [load_w(experts) for experts in W_LOADS]
+        nc.sync.dma_start(loads[0][0][:, :, : N // 2], loads[0][1][:, :, : N // 2])
         load_w_scales(0)
         nc.sync.dma_start(gate_first[:], gate[:, : 2 * C])
-        load_w(W_LOADS[1])
-        load_w(W_LOADS[2])
+        nc.sync.dma_start(loads[0][0][:, :, N // 2 :], loads[0][1][:, :, N // 2 :])
+        nc.sync.dma_start(loads[1][0][:], loads[1][1])
+        nc.sync.dma_start(loads[2][0][:], loads[2][1])
         nc.sync.dma_start(gate_rest[:], gate[:, 2 * C :])
         load_w_scales(1)
-        load_w(W_LOADS[3])
-        load_w(W_LOADS[4])
+        nc.sync.dma_start(loads[3][0][:], loads[3][1])
+        nc.sync.dma_start(loads[4][0][:], loads[4][1])
 
         def gate_of(s0, n):
             return gate_first[:, s0 : s0 + n] if s0 < 2 * C else gate_rest[:, s0 - 2 * C : s0 - 2 * C + n]
@@ -101,17 +104,15 @@ def tile_moe_loc_lin_gelu_kernel(tc, x_words, x_scales, xo, w_words, w_scales, g
                 stop=True,
             )
 
-        far_codes = [keep.tile([P, 2 * C], U32, name="far_codes%d" % h, align_bytes=64) for h in range(4)]
+        far_codes = keep.tile([P, E * C], U32, name="far_codes", align_bytes=64)
         far_scales = {}
 
-        def gather_far_bytes(h, tag):
-            far_scales[h] = keep.tile([P, 2 * C], U8, name="far_scales%d" % h, align_bytes=64, tag=tag)
-            nc.vector.tensor_copy(far_scales[h][:], far_bytes[:].indirect(far_list[:, 16 * h : 16 * h + 16]))
+        def gather_far_bytes(g, tag):
+            far_scales[g] = keep.tile([P, 4 * C], U8, name="far_scales%d" % g, align_bytes=64, tag=tag)
+            nc.vector.tensor_copy(far_scales[g][:], far_bytes[:].indirect(far_list[:, 32 * g : 32 * g + 32]))
 
-        for h in range(4):
-            nc.vector.tensor_copy(far_codes[h][:], far_words[:].bitcast(U32).indirect(far_list[:, 16 * h : 16 * h + 16]))
-        for h in range(3):
-            gather_far_bytes(h, "far_scales%d" % h)
+        nc.vector.tensor_copy(far_codes[:], far_words[:].bitcast(U32).indirect(far_list[:]))
+        gather_far_bytes(0, "far_scales0")
 
         for j in range(PACK - 1):
             nc.gpsimd.tensor_scalar(x_bf16[j][:], x_f32[j][:], 1.0, 0.0, MULT, ADD)
@@ -124,7 +125,7 @@ def tile_moe_loc_lin_gelu_kernel(tc, x_words, x_scales, xo, w_words, w_scales, g
 
         def gather(c):
             s0, n = span(c)
-            tag = ("first", "second")[c] if c < 2 else "scales0"
+            tag = ("first", "second", "scales0", "scales2", "scales3")[c]
             grouped[c] = keep.tile([P, n, PACK], BF16, name="grouped%d" % c, align_bytes=64, tag=tag)
             offsets = own_list[:, s0 // 16 : (s0 + n) // 16]
             for j in range(PACK):
@@ -135,7 +136,7 @@ def tile_moe_loc_lin_gelu_kernel(tc, x_words, x_scales, xo, w_words, w_scales, g
 
         def activate(c, tiles, codes, scales):
             n = span(c)[1]
-            acc = own_psum.tile([P, len(tiles), n], F32, name="own_acc", tag="own_acc")
+            acc = psum.tile([P, len(tiles), n], F32, name="own_acc", tag="bank%d_%d" % (c % 2, tiles[0]))
             for u, t in enumerate(tiles):
                 for i, e in enumerate(OWN_CHUNKS[c]):
                     slots = slice(i * C, (i + 1) * C)
@@ -166,20 +167,20 @@ def tile_moe_loc_lin_gelu_kernel(tc, x_words, x_scales, xo, w_words, w_scales, g
 
         def far(k, tag):
             g, t = divmod(k, NT)
-            acc = far_psum.tile([P, 4 * C], F32, name="far_acc", tag="far_acc")
+            acc = psum.tile([P, 4 * C], F32, name="far_acc", tag=tag)
             for i in range(4):
                 e = 4 * g + i
-                slots = slice((e % 2) * C, (e % 2 + 1) * C)
-                multiply(acc[:, i * C : (i + 1) * C], e, t, far_codes[e // 2][:, slots], far_scales[e // 2][:, slots])
-            z = keep.tile([P, 4 * C], F32, name="z%d" % k, align_bytes=64, tag=tag)
+                slots = slice(i * C, (i + 1) * C)
+                multiply(acc[:, slots], e, t, far_codes[:, e * C : (e + 1) * C], far_scales[g][:, slots])
+            z = keep.tile([P, 4 * C], F32, name="z%d" % k)
             nc.scalar.activation(z[:], acc[:], GELU)
             nc.sync.dma_start(out[t * P : (t + 1) * P, T + g * 4 * C : T + (g + 1) * 4 * C], z[:])
 
-        far_slots = {2: ("scales2",), 3: ("scales3", "y2_0"), 4: ("y2_2", "y3_1", "scales0", "scales4", "y3_0")}
+        far_slots = {2: ("bank0_1", "bank0_2"), 3: ("bank1_0", "bank1_1", "bank1_2"), 4: ("bank0_0", "bank0_1", "bank0_2")}
         gather(0)
         nc.scalar.copy(x_bf16[PACK - 1][:], x_f32[PACK - 1][:])
         compute(0)
-        gather_far_bytes(3, "first")
+        gather_far_bytes(1, "first")
         k = 0
         for c in range(len(OWN_CHUNKS)):
             scatter(c, 0)

@@ -20,6 +20,7 @@ ADD = mybir.AluOpType.add
 P = 128
 PACK = 4
 NT = N // P
+SPLIT = 768
 OWN_CHUNKS = ((0,), (1,), (2, 3), (4, 5), (6, 7))
 W_LOADS = ((0,), (1,), (2, 3), (4, 5), (6, 7))
 
@@ -28,23 +29,30 @@ def tile_moe_loc_lin_gelu_kernel(tc, x_words, x_scales, xo, w_words, w_scales, g
     nc = tc.nc
     with ExitStack() as ctx:
         keep = ctx.enter_context(tc.tile_pool(name="keep", bufs=1))
+        turns = ctx.enter_context(tc.tile_pool(name="turns", bufs=1))
         psum = ctx.enter_context(tc.psum_pool(name="psum", bufs=1))
 
         own_list = keep.tile([P, E * C // 16], U16, name="own_list")
         far_list = keep.tile([P, E * C // 16], U16, name="far_list")
-        far_words = keep.tile([P, 4 * Q], I32, name="far_words", align_bytes=64)
-        far_bytes = keep.tile([P, 2 * Q], U8, name="far_bytes", align_bytes=64)
+        far_words = keep.tile([P, Q], I32, name="far_words", align_bytes=64)
+        far_bytes = keep.tile([P, Q], U8, name="far_bytes", align_bytes=64)
         w_planes = [keep.tile([P, N], U8, name="w_plane%d" % g, align_bytes=64) for g in range(2)]
-        x_f32 = [keep.tile([P, T], F32, name="x_f32_%d" % j, align_bytes=64) for j in range(PACK)]
-        x_bf16 = [keep.tile([P, T], BF16, name="x_bf16_%d" % j, align_bytes=64) for j in range(PACK)]
+        x_f32 = [keep.tile([P, T], F32, name="x_f32_%d" % j, tag="x_f32_%d" % j, align_bytes=64) for j in range(PACK)]
+        x_bf16 = [keep.tile([P, T], BF16, name="x_bf16_%d" % j, align_bytes=64) for j in range(PACK - 1)]
         gate_first = keep.tile([P, 2 * C], F32, name="gate_first")
         gate_rest = keep.tile([P, (E - 2) * C], F32, name="gate_rest")
 
         warm = keep.tile([P, 16], F32, name="warm")
         warm_out = keep.tile([P, 16], F32, name="warm_out")
+        third = keep.tile([P, 2 * C, PACK], BF16, name="third", align_bytes=64)
+        third_words = third[:].rearrange("p s j -> p (s j)").bitcast(F32)
+        nc.vector.memset(third_words[:, 1:2], 0.0)
+        second = keep.tile([P, C, PACK], BF16, name="second", align_bytes=64)
+        second_words = second[:].rearrange("p s j -> p (s j)").bitcast(F32)
+        nc.vector.memset(second_words[:, 1:2], 0.0)
+        bias_of = {(0, 0): second_words[:, 1:2], (0, 1): warm_out[:, 0:1], (0, 2): third_words[:, 1:2]}
         nc.vector.memset(far_bytes[:].bitcast(I32), 0)
         nc.vector.memset(warm[:], 0.0)
-        nc.vector.memset(far_words[:, Q:], 0)
         nc.vector.memset(w_planes[1][:].bitcast(I32), 0)
         nc.scalar.activation(warm_out[:], warm[:], GELU)
 
@@ -57,35 +65,35 @@ def tile_moe_loc_lin_gelu_kernel(tc, x_words, x_scales, xo, w_words, w_scales, g
                 w_tiles[e] = tile[:, i, :]
             return tile, src
 
-        def load_w_scales(g):
+        def load_w_scales(g, queue):
             for quad in range(4):
-                nc.sync.dma_start(
+                queue.dma_start(
                     w_planes[g][32 * quad : 32 * quad + 4 * (E - 4 * g), :].bitcast(I32),
                     w_scales[4 * g :, 0, 4 * quad : 4 * quad + 4, :].bitcast(I32),
                 )
 
         nc.sync.dma_start(far_list[:], offs2)
-        nc.sync.dma_start(far_words[:, :Q], x_words[0].rearrange("p t d -> p (t d)").bitcast(I32))
-        nc.sync.dma_start(own_list[:], offs)
+        nc.sync.dma_start(far_words[:], x_words[0].rearrange("p t d -> p (t d)").bitcast(I32))
         xo_planes = xo.rearrange("(p j) t -> p j t", j=PACK)
+        nc.sync.dma_start(own_list[:], offs)
         for j in range(2):
             nc.sync.dma_start(x_f32[j][:], xo_planes[:, j, :])
         for quad in range(4):
             nc.sync.dma_start(
-                far_bytes[32 * quad : 32 * quad + 4, :Q].bitcast(I32),
+                far_bytes[32 * quad : 32 * quad + 4, :].bitcast(I32),
                 x_scales[0, 4 * quad : 4 * quad + 4, :].bitcast(I32),
             )
         for j in range(2, PACK):
             nc.sync.dma_start(x_f32[j][:], xo_planes[:, j, :])
+        load_w_scales(0, nc.sync)
         loads = [load_w(experts) for experts in W_LOADS]
         nc.sync.dma_start(loads[0][0][:, :, : N // 2], loads[0][1][:, :, : N // 2])
-        load_w_scales(0)
         nc.sync.dma_start(gate_first[:], gate[:, : 2 * C])
         nc.sync.dma_start(loads[0][0][:, :, N // 2 :], loads[0][1][:, :, N // 2 :])
         nc.sync.dma_start(loads[1][0][:], loads[1][1])
         nc.sync.dma_start(loads[2][0][:], loads[2][1])
         nc.sync.dma_start(gate_rest[:], gate[:, 2 * C :])
-        load_w_scales(1)
+        load_w_scales(1, nc.sync)
         nc.sync.dma_start(loads[3][0][:], loads[3][1])
         nc.sync.dma_start(loads[4][0][:], loads[4][1])
 
@@ -107,12 +115,20 @@ def tile_moe_loc_lin_gelu_kernel(tc, x_words, x_scales, xo, w_words, w_scales, g
         far_codes = keep.tile([P, E * C], U32, name="far_codes", align_bytes=64)
         far_scales = {}
 
-        def gather_far_bytes(g, tag):
-            far_scales[g] = keep.tile([P, 4 * C], U8, name="far_scales%d" % g, align_bytes=64, tag=tag)
-            nc.vector.tensor_copy(far_scales[g][:], far_bytes[:].indirect(far_list[:, 32 * g : 32 * g + 32]))
+        def gather_far_bytes(g, offset):
+            far_scales[g] = turns.tile([P, 4 * C], U8, name="far_scales%d" % g, align_bytes=64, offset=offset)
+            for h in range(2):
+                nc.vector.tensor_copy(
+                    far_scales[g][:, 2 * C * h : 2 * C * (h + 1)],
+                    far_bytes[:].indirect(far_list[:, 32 * g + 16 * h : 32 * g + 16 * h + 16]),
+                )
 
-        nc.vector.tensor_copy(far_codes[:], far_words[:].bitcast(U32).indirect(far_list[:]))
-        gather_far_bytes(0, "far_scales0")
+        for g in range(E // 2):
+            nc.vector.tensor_copy(
+                far_codes[:, 2 * C * g : 2 * C * (g + 1)],
+                far_words[:].bitcast(U32).indirect(far_list[:, 16 * g : 16 * g + 16]),
+            )
+        gather_far_bytes(0, 2560)
 
         for j in range(PACK - 1):
             nc.gpsimd.tensor_scalar(x_bf16[j][:], x_f32[j][:], 1.0, 0.0, MULT, ADD)
@@ -123,12 +139,17 @@ def tile_moe_loc_lin_gelu_kernel(tc, x_words, x_scales, xo, w_words, w_scales, g
         def span(c):
             return OWN_CHUNKS[c][0] * C, len(OWN_CHUNKS[c]) * C
 
-        def gather(c):
+        def gather(c, planes):
             s0, n = span(c)
-            tag = ("first", "second", "scales0", "scales2", "scales3")[c]
-            grouped[c] = keep.tile([P, n, PACK], BF16, name="grouped%d" % c, align_bytes=64, tag=tag)
+            tag = ("first", "second", "third", "scales2", "scales3")[c]
+            if c == 0:
+                grouped[c] = turns.tile([P, n, PACK], BF16, name="first", align_bytes=64, offset=1536)
+            elif c in (1, 2):
+                grouped[c] = (second, third)[c - 1]
+            else:
+                grouped[c] = keep.tile([P, n, PACK], BF16, name="grouped%d" % c, align_bytes=64, tag=tag)
             offsets = own_list[:, s0 // 16 : (s0 + n) // 16]
-            for j in range(PACK):
+            for j in planes:
                 if c == 0 and j >= 2:
                     nc.vector.tensor_copy(grouped[c][:, :, j], x_f32[j][:].indirect(offsets))
                 else:
@@ -142,8 +163,8 @@ def tile_moe_loc_lin_gelu_kernel(tc, x_words, x_scales, xo, w_words, w_scales, g
                     slots = slice(i * C, (i + 1) * C)
                     multiply(acc[:, u, slots], e, t, codes[:, slots], scales[:, slots])
             tag = "y%d_%d" % (c, tiles[0])
-            y = keep.tile([P, len(tiles), n], F32, name=tag, align_bytes=64, tag=tag)
-            nc.scalar.activation(y[:], acc[:], GELU)
+            y = keep.tile([P, len(tiles), n], F32, name=tag, align_bytes=64, tag="x_f32_3" if tag == "y0_2" else tag)
+            nc.scalar.activation(y[:], acc[:], GELU, bias=bias_of.get((c, tiles[0]), 0.0))
             for u, t in enumerate(tiles):
                 results[c, t] = y[:, u, :]
 
@@ -152,11 +173,18 @@ def tile_moe_loc_lin_gelu_kernel(tc, x_words, x_scales, xo, w_words, w_scales, g
             codes = keep.tile([P, n], U32, name="codes%d" % c, align_bytes=64, tag="y%d_0" % (c - 1))
             scales = keep.tile([P, n], U8, name="scales%d" % c, align_bytes=64, tag="scales%d" % c)
             nc.vector.quantize_mx(out=codes[:].bitcast(FP8X4), scales=scales[:], in_=grouped[c][:].rearrange("p s j -> p (s j)"))
+            if c == 0:
+                x_bf16.append(turns.tile([P, T], BF16, name="x_bf16_3", align_bytes=64, offset=0))
+                nc.gpsimd.tensor_scalar(x_bf16[3][:, :SPLIT], x_f32[3][:, :SPLIT], 1.0, 0.0, MULT, ADD)
+                nc.scalar.copy(x_bf16[3][:, SPLIT:], x_f32[3][:, SPLIT:])
             activate(c, (0,), codes, scales)
             activate(c, (1,), codes, scales)
             if c + 1 < len(OWN_CHUNKS):
-                gather(c + 1)
+                if c != 1:
+                    gather(c + 1, range(2 if c == 0 else 0, PACK))
             activate(c, (2, 3), codes, scales)
+            if c == 0:
+                gather(2, range(2, PACK))
 
         def scatter(c, t):
             s0, n = span(c)
@@ -177,10 +205,11 @@ def tile_moe_loc_lin_gelu_kernel(tc, x_words, x_scales, xo, w_words, w_scales, g
             nc.sync.dma_start(out[t * P : (t + 1) * P, T + g * 4 * C : T + (g + 1) * 4 * C], z[:])
 
         far_slots = {2: ("bank0_1", "bank0_2"), 3: ("bank1_0", "bank1_1", "bank1_2"), 4: ("bank0_0", "bank0_1", "bank0_2")}
-        gather(0)
-        nc.scalar.copy(x_bf16[PACK - 1][:], x_f32[PACK - 1][:])
+        gather(0, range(PACK))
+        gather(1, range(2))
+        gather(2, range(2))
         compute(0)
-        gather_far_bytes(1, "first")
+        gather_far_bytes(1, 2048)
         k = 0
         for c in range(len(OWN_CHUNKS)):
             scatter(c, 0)

@@ -20,7 +20,8 @@ ADD = mybir.AluOpType.add
 P = 128
 PACK = 4
 NT = N // P
-SPLIT = 768
+SPLIT = 512
+EARLY = 5
 OWN_CHUNKS = ((0,), (1,), (2, 3), (4, 5), (6, 7))
 W_LOADS = ((0,), (1,), (2, 3), (4, 5), (6, 7))
 
@@ -50,7 +51,7 @@ def tile_moe_loc_lin_gelu_kernel(tc, x_words, x_scales, xo, w_words, w_scales, g
         second = keep.tile([P, C, PACK], BF16, name="second", align_bytes=64)
         second_words = second[:].rearrange("p s j -> p (s j)").bitcast(F32)
         nc.vector.memset(second_words[:, 1:2], 0.0)
-        bias_of = {(0, 0): second_words[:, 1:2], (0, 1): warm_out[:, 0:1], (0, 2): third_words[:, 1:2]}
+        bias_of = {(0, 0): second_words[:, 1:2], (0, 1): warm_out[:, 0:1], (0, 2): third[:, 0, 2:3], (1, 0): third[:, 0, 3:4]}
         nc.vector.memset(far_bytes[:].bitcast(I32), 0)
         nc.vector.memset(warm[:], 0.0)
         nc.vector.memset(w_planes[1][:].bitcast(I32), 0)
@@ -115,23 +116,29 @@ def tile_moe_loc_lin_gelu_kernel(tc, x_words, x_scales, xo, w_words, w_scales, g
         far_codes = keep.tile([P, E * C], U32, name="far_codes", align_bytes=64)
         far_scales = {}
 
-        def gather_far_bytes(g, offset):
-            far_scales[g] = turns.tile([P, 4 * C], U8, name="far_scales%d" % g, align_bytes=64, offset=offset)
-            for h in range(2):
-                nc.vector.tensor_copy(
-                    far_scales[g][:, 2 * C * h : 2 * C * (h + 1)],
-                    far_bytes[:].indirect(far_list[:, 32 * g + 16 * h : 32 * g + 16 * h + 16]),
-                )
+        def gather_far(dst, window, first, count):
+            for e0 in range(0, count, 3):
+                e1 = min(e0 + 3, count)
+                offsets = far_list[:, (first + e0) * C // 16 : (first + e1) * C // 16]
+                nc.vector.tensor_copy(dst[:, e0 * C : e1 * C], window.indirect(offsets))
 
-        for g in range(E // 2):
-            nc.vector.tensor_copy(
-                far_codes[:, 2 * C * g : 2 * C * (g + 1)],
-                far_words[:].bitcast(U32).indirect(far_list[:, 16 * g : 16 * g + 16]),
-            )
-        gather_far_bytes(0, 2560)
+        def gather_far_bytes(first, count, offset):
+            tile = turns.tile([P, count * C], U8, name="far_scales%d" % first, align_bytes=64, offset=offset)
+            gather_far(tile, far_bytes[:], first, count)
+            for i in range(count):
+                far_scales[first + i] = tile[:, i * C : (i + 1) * C]
 
-        for j in range(PACK - 1):
-            nc.gpsimd.tensor_scalar(x_bf16[j][:], x_f32[j][:], 1.0, 0.0, MULT, ADD)
+        gather_far(far_codes, far_words[:].bitcast(U32), 0, E)
+        gather_far_bytes(0, EARLY, 2560)
+
+        def cast(j, split):
+            nc.gpsimd.tensor_scalar(x_bf16[j][:, :split], x_f32[j][:, :split], 1.0, 0.0, MULT, ADD)
+            if split < T:
+                nc.scalar.copy(x_bf16[j][:, split:], x_f32[j][:, split:])
+
+        cast(0, SPLIT)
+        cast(1, T)
+        cast(2, T)
 
         own_out = [keep.tile([P, T], F32, name="own_out%d" % t) for t in range(NT)]
         grouped, results = {}, {}
@@ -175,16 +182,14 @@ def tile_moe_loc_lin_gelu_kernel(tc, x_words, x_scales, xo, w_words, w_scales, g
             nc.vector.quantize_mx(out=codes[:].bitcast(FP8X4), scales=scales[:], in_=grouped[c][:].rearrange("p s j -> p (s j)"))
             if c == 0:
                 x_bf16.append(turns.tile([P, T], BF16, name="x_bf16_3", align_bytes=64, offset=0))
-                nc.gpsimd.tensor_scalar(x_bf16[3][:, :SPLIT], x_f32[3][:, :SPLIT], 1.0, 0.0, MULT, ADD)
-                nc.scalar.copy(x_bf16[3][:, SPLIT:], x_f32[3][:, SPLIT:])
+                cast(3, SPLIT)
             activate(c, (0,), codes, scales)
             activate(c, (1,), codes, scales)
             if c + 1 < len(OWN_CHUNKS):
-                if c != 1:
-                    gather(c + 1, range(2 if c == 0 else 0, PACK))
+                gather(c + 1, range((2, 3, 0, 0)[c], PACK))
             activate(c, (2, 3), codes, scales)
             if c == 0:
-                gather(2, range(2, PACK))
+                gather(2, range(2, 3))
 
         def scatter(c, t):
             s0, n = span(c)
@@ -199,7 +204,7 @@ def tile_moe_loc_lin_gelu_kernel(tc, x_words, x_scales, xo, w_words, w_scales, g
             for i in range(4):
                 e = 4 * g + i
                 slots = slice(i * C, (i + 1) * C)
-                multiply(acc[:, slots], e, t, far_codes[:, e * C : (e + 1) * C], far_scales[g][:, slots])
+                multiply(acc[:, slots], e, t, far_codes[:, e * C : (e + 1) * C], far_scales[e])
             z = keep.tile([P, 4 * C], F32, name="z%d" % k)
             nc.scalar.activation(z[:], acc[:], GELU)
             nc.sync.dma_start(out[t * P : (t + 1) * P, T + g * 4 * C : T + (g + 1) * 4 * C], z[:])
@@ -209,7 +214,7 @@ def tile_moe_loc_lin_gelu_kernel(tc, x_words, x_scales, xo, w_words, w_scales, g
         gather(1, range(2))
         gather(2, range(2))
         compute(0)
-        gather_far_bytes(1, 2048)
+        gather_far_bytes(EARLY, E - EARLY, 2048)
         k = 0
         for c in range(len(OWN_CHUNKS)):
             scatter(c, 0)

@@ -20,8 +20,8 @@ ADD = mybir.AluOpType.add
 P = 128
 PACK = 4
 NT = N // P
-SPLIT = 512
-EARLY = 5
+SPLIT = 768
+EARLY = 4
 OWN_CHUNKS = ((0,), (1,), (2, 3), (4, 5), (6, 7))
 W_LOADS = ((0,), (1,), (2, 3), (4, 5), (6, 7))
 
@@ -48,10 +48,13 @@ def tile_moe_loc_lin_gelu_kernel(tc, x_words, x_scales, xo, w_words, w_scales, g
         third = keep.tile([P, 2 * C, PACK], BF16, name="third", align_bytes=64)
         third_words = third[:].rearrange("p s j -> p (s j)").bitcast(F32)
         nc.vector.memset(third_words[:, 1:2], 0.0)
+        fourth = keep.tile([P, 2 * C, PACK], BF16, name="fourth", align_bytes=64)
+        fourth_words = fourth[:].rearrange("p s j -> p (s j)").bitcast(F32)
+        nc.vector.memset(fourth_words[:, 0:2], 0.0)
         second = keep.tile([P, C, PACK], BF16, name="second", align_bytes=64)
         second_words = second[:].rearrange("p s j -> p (s j)").bitcast(F32)
         nc.vector.memset(second_words[:, 1:2], 0.0)
-        bias_of = {(0, 0): second_words[:, 1:2], (0, 1): warm_out[:, 0:1], (0, 2): third[:, 0, 2:3], (1, 0): third[:, 0, 3:4]}
+        bias_of = {(0, 0): second_words[:, 1:2], (0, 1): warm_out[:, 0:1], (0, 2): third[:, 0, 2:3], (1, 0): third[:, 0, 3:4], (1, 1): fourth_words[:, 0:1], (2, 0): fourth_words[:, 1:2]}
         nc.vector.memset(far_bytes[:].bitcast(I32), 0)
         nc.vector.memset(warm[:], 0.0)
         nc.vector.memset(w_planes[1][:].bitcast(I32), 0)
@@ -117,8 +120,8 @@ def tile_moe_loc_lin_gelu_kernel(tc, x_words, x_scales, xo, w_words, w_scales, g
         far_scales = {}
 
         def gather_far(dst, window, first, count):
-            for e0 in range(0, count, 3):
-                e1 = min(e0 + 3, count)
+            for e0 in range(0, count, 2):
+                e1 = e0 + 2
                 offsets = far_list[:, (first + e0) * C // 16 : (first + e1) * C // 16]
                 nc.vector.tensor_copy(dst[:, e0 * C : e1 * C], window.indirect(offsets))
 
@@ -136,7 +139,7 @@ def tile_moe_loc_lin_gelu_kernel(tc, x_words, x_scales, xo, w_words, w_scales, g
             if split < T:
                 nc.scalar.copy(x_bf16[j][:, split:], x_f32[j][:, split:])
 
-        cast(0, SPLIT)
+        cast(0, T // 2)
         cast(1, T)
         cast(2, T)
 
@@ -151,8 +154,8 @@ def tile_moe_loc_lin_gelu_kernel(tc, x_words, x_scales, xo, w_words, w_scales, g
             tag = ("first", "second", "third", "scales2", "scales3")[c]
             if c == 0:
                 grouped[c] = turns.tile([P, n, PACK], BF16, name="first", align_bytes=64, offset=1536)
-            elif c in (1, 2):
-                grouped[c] = (second, third)[c - 1]
+            elif c in (1, 2, 3):
+                grouped[c] = (second, third, fourth)[c - 1]
             else:
                 grouped[c] = keep.tile([P, n, PACK], BF16, name="grouped%d" % c, align_bytes=64, tag=tag)
             offsets = own_list[:, s0 // 16 : (s0 + n) // 16]
@@ -164,7 +167,7 @@ def tile_moe_loc_lin_gelu_kernel(tc, x_words, x_scales, xo, w_words, w_scales, g
 
         def activate(c, tiles, codes, scales):
             n = span(c)[1]
-            acc = psum.tile([P, len(tiles), n], F32, name="own_acc", tag="bank%d_%d" % (c % 2, tiles[0]))
+            acc = psum.tile([P, len(tiles), n], F32, name="own_acc", tag="bank%d_%d" % (c % 2, min(tiles[0], 1) if c == 2 else tiles[0]))
             for u, t in enumerate(tiles):
                 for i, e in enumerate(OWN_CHUNKS[c]):
                     slots = slice(i * C, (i + 1) * C)
@@ -186,10 +189,12 @@ def tile_moe_loc_lin_gelu_kernel(tc, x_words, x_scales, xo, w_words, w_scales, g
             activate(c, (0,), codes, scales)
             activate(c, (1,), codes, scales)
             if c + 1 < len(OWN_CHUNKS):
-                gather(c + 1, range((2, 3, 0, 0)[c], PACK))
+                gather(c + 1, range((2, 3, 2, 0)[c], PACK))
             activate(c, (2, 3), codes, scales)
             if c == 0:
                 gather(2, range(2, 3))
+            if c == 1:
+                gather(3, range(2))
 
         def scatter(c, t):
             s0, n = span(c)
@@ -209,7 +214,7 @@ def tile_moe_loc_lin_gelu_kernel(tc, x_words, x_scales, xo, w_words, w_scales, g
             nc.scalar.activation(z[:], acc[:], GELU)
             nc.sync.dma_start(out[t * P : (t + 1) * P, T + g * 4 * C : T + (g + 1) * 4 * C], z[:])
 
-        far_slots = {2: ("bank0_1", "bank0_2"), 3: ("bank1_0", "bank1_1", "bank1_2"), 4: ("bank0_0", "bank0_1", "bank0_2")}
+        far_slots = {2: ("bank0_0", "bank0_1"), 3: ("bank1_0", "bank1_1", "bank1_2"), 4: ("bank0_0", "bank0_1", "bank0_2")}
         gather(0, range(PACK))
         gather(1, range(2))
         gather(2, range(2))

@@ -20,8 +20,8 @@ ADD = mybir.AluOpType.add
 P = 128
 PACK = 4
 NT = N // P
-SPLIT = 768
-EARLY = 4
+SPLIT = 384
+EARLY = 5
 OWN_CHUNKS = ((0,), (1,), (2, 3), (4, 5), (6, 7))
 W_LOADS = ((0,), (1,), (2, 3), (4, 5), (6, 7))
 
@@ -39,7 +39,7 @@ def tile_moe_loc_lin_gelu_kernel(tc, x_words, x_scales, xo, w_words, w_scales, g
         far_bytes = keep.tile([P, Q], U8, name="far_bytes", align_bytes=64)
         w_planes = [keep.tile([P, N], U8, name="w_plane%d" % g, align_bytes=64) for g in range(2)]
         x_f32 = [keep.tile([P, T], F32, name="x_f32_%d" % j, tag="x_f32_%d" % j, align_bytes=64) for j in range(PACK)]
-        x_bf16 = [keep.tile([P, T], BF16, name="x_bf16_%d" % j, align_bytes=64) for j in range(PACK - 1)]
+        x_bf16 = [keep.tile([P, T], BF16, name="x_bf16_%d" % j, align_bytes=64) for j in range(PACK)]
         gate_first = keep.tile([P, 2 * C], F32, name="gate_first")
         gate_rest = keep.tile([P, (E - 2) * C], F32, name="gate_rest")
 
@@ -121,7 +121,7 @@ def tile_moe_loc_lin_gelu_kernel(tc, x_words, x_scales, xo, w_words, w_scales, g
 
         def gather_far(dst, window, first, count):
             for e0 in range(0, count, 2):
-                e1 = e0 + 2
+                e1 = min(e0 + 2, count)
                 offsets = far_list[:, (first + e0) * C // 16 : (first + e1) * C // 16]
                 nc.vector.tensor_copy(dst[:, e0 * C : e1 * C], window.indirect(offsets))
 
@@ -134,14 +134,13 @@ def tile_moe_loc_lin_gelu_kernel(tc, x_words, x_scales, xo, w_words, w_scales, g
         gather_far(far_codes, far_words[:].bitcast(U32), 0, E)
         gather_far_bytes(0, EARLY, 2560)
 
-        def cast(j, split):
-            nc.gpsimd.tensor_scalar(x_bf16[j][:, :split], x_f32[j][:, :split], 1.0, 0.0, MULT, ADD)
-            if split < T:
-                nc.scalar.copy(x_bf16[j][:, split:], x_f32[j][:, split:])
+        def cast(j, cols, factor=1.0):
+            nc.gpsimd.tensor_scalar(x_bf16[j][:, cols], x_f32[j][:, cols], factor, 0.0, MULT, ADD)
 
-        cast(0, T // 2)
-        cast(1, T)
-        cast(2, T)
+        cast(0, slice(0, T // 2))
+        nc.scalar.copy(x_bf16[0][:, T // 2 :], x_f32[0][:, T // 2 :])
+        cast(1, slice(0, T))
+        cast(2, slice(0, T))
 
         own_out = [keep.tile([P, T], F32, name="own_out%d" % t) for t in range(NT)]
         grouped, results = {}, {}
@@ -184,8 +183,9 @@ def tile_moe_loc_lin_gelu_kernel(tc, x_words, x_scales, xo, w_words, w_scales, g
             scales = keep.tile([P, n], U8, name="scales%d" % c, align_bytes=64, tag="scales%d" % c)
             nc.vector.quantize_mx(out=codes[:].bitcast(FP8X4), scales=scales[:], in_=grouped[c][:].rearrange("p s j -> p (s j)"))
             if c == 0:
-                x_bf16.append(turns.tile([P, T], BF16, name="x_bf16_3", align_bytes=64, offset=0))
-                cast(3, SPLIT)
+                one = turns.tile([P, 1], F32, name="one", align_bytes=64, offset=1536)
+                nc.vector.memset(one[:], 1.0)
+                cast(3, slice(0, SPLIT), one[:])
             activate(c, (0,), codes, scales)
             activate(c, (1,), codes, scales)
             if c + 1 < len(OWN_CHUNKS):
@@ -218,6 +218,7 @@ def tile_moe_loc_lin_gelu_kernel(tc, x_words, x_scales, xo, w_words, w_scales, g
         gather(0, range(PACK))
         gather(1, range(2))
         gather(2, range(2))
+        nc.scalar.copy(x_bf16[3][:, SPLIT:], x_f32[3][:, SPLIT:])
         compute(0)
         gather_far_bytes(EARLY, E - EARLY, 2048)
         k = 0

@@ -20,7 +20,7 @@ ADD = mybir.AluOpType.add
 P = 128
 PACK = 4
 NT = N // P
-SPLIT = 384
+SPLIT = 256
 EARLY = 5
 OWN_CHUNKS = ((0,), (1,), (2, 3), (4, 5), (6, 7))
 W_LOADS = ((0,), (1,), (2, 3), (4, 5), (6, 7))
@@ -141,6 +141,7 @@ def tile_moe_loc_lin_gelu_kernel(tc, x_words, x_scales, xo, w_words, w_scales, g
         nc.scalar.copy(x_bf16[0][:, T // 2 :], x_f32[0][:, T // 2 :])
         cast(1, slice(0, T))
         cast(2, slice(0, T))
+        cast(3, slice(0, SPLIT))
 
         own_out = [keep.tile([P, T], F32, name="own_out%d" % t) for t in range(NT)]
         grouped, results = {}, {}
@@ -166,13 +167,13 @@ def tile_moe_loc_lin_gelu_kernel(tc, x_words, x_scales, xo, w_words, w_scales, g
 
         def activate(c, tiles, codes, scales):
             n = span(c)[1]
-            acc = psum.tile([P, len(tiles), n], F32, name="own_acc", tag="bank%d_%d" % (c % 2, min(tiles[0], 1) if c == 2 else tiles[0]))
+            acc = psum.tile([P, len(tiles), n], F32, name="own_acc", tag="bank%d_%d" % (c % 2, min(tiles[0], 1) if c in (0, 2) else tiles[0]))
             for u, t in enumerate(tiles):
                 for i, e in enumerate(OWN_CHUNKS[c]):
                     slots = slice(i * C, (i + 1) * C)
                     multiply(acc[:, u, slots], e, t, codes[:, slots], scales[:, slots])
             tag = "y%d_%d" % (c, tiles[0])
-            y = keep.tile([P, len(tiles), n], F32, name=tag, align_bytes=64, tag="x_f32_3" if tag == "y0_2" else tag)
+            y = keep.tile([P, len(tiles), n], F32, name=tag, align_bytes=64, tag=tag)
             nc.scalar.activation(y[:], acc[:], GELU, bias=bias_of.get((c, tiles[0]), 0.0))
             for u, t in enumerate(tiles):
                 results[c, t] = y[:, u, :]
@@ -182,10 +183,6 @@ def tile_moe_loc_lin_gelu_kernel(tc, x_words, x_scales, xo, w_words, w_scales, g
             codes = keep.tile([P, n], U32, name="codes%d" % c, align_bytes=64, tag="y%d_0" % (c - 1))
             scales = keep.tile([P, n], U8, name="scales%d" % c, align_bytes=64, tag="scales%d" % c)
             nc.vector.quantize_mx(out=codes[:].bitcast(FP8X4), scales=scales[:], in_=grouped[c][:].rearrange("p s j -> p (s j)"))
-            if c == 0:
-                one = turns.tile([P, 1], F32, name="one", align_bytes=64, offset=1536)
-                nc.vector.memset(one[:], 1.0)
-                cast(3, slice(0, SPLIT), one[:])
             activate(c, (0,), codes, scales)
             activate(c, (1,), codes, scales)
             if c + 1 < len(OWN_CHUNKS):

@@ -20,96 +20,110 @@ ADD = mybir.AluOpType.add
 P = 128
 PACK = 4
 NT = N // P
-SPLIT = 256
+PER_COL = 16
+SHARE = 4
+
+CHUNKS = ((0,), (1,), (2, 3), (4, 5), (6, 7))
+FIRST_HALF, SECOND_HALF = slice(0, T // 2), slice(T // 2, T)
 EARLY = 5
-OWN_CHUNKS = ((0,), (1,), (2, 3), (4, 5), (6, 7))
-W_LOADS = ((0,), (1,), (2, 3), (4, 5), (6, 7))
+FIRST_AT, LATE_AT, EARLY_AT = 0, 512, 1024
 
 
-def tile_moe_loc_lin_gelu_kernel(tc, x_words, x_scales, xo, w_words, w_scales, gate, offs, offs2, out):
+def tile_moe_loc_lin_gelu_kernel(
+    tc, x_words, x_scales, xo, w_words, w_scales, gate, offs, offs2, out
+):
     nc = tc.nc
     with ExitStack() as ctx:
         keep = ctx.enter_context(tc.tile_pool(name="keep", bufs=1))
         turns = ctx.enter_context(tc.tile_pool(name="turns", bufs=1))
         psum = ctx.enter_context(tc.psum_pool(name="psum", bufs=1))
 
-        own_list = keep.tile([P, E * C // 16], U16, name="own_list")
-        far_list = keep.tile([P, E * C // 16], U16, name="far_list")
+        own_list = keep.tile([P, E * C // PER_COL], U16, name="own_list")
+        far_list = keep.tile([P, E * C // PER_COL], U16, name="far_list")
         far_words = keep.tile([P, Q], I32, name="far_words", align_bytes=64)
         far_bytes = keep.tile([P, Q], U8, name="far_bytes", align_bytes=64)
-        w_planes = [keep.tile([P, N], U8, name="w_plane%d" % g, align_bytes=64) for g in range(2)]
-        x_f32 = [keep.tile([P, T], F32, name="x_f32_%d" % j, tag="x_f32_%d" % j, align_bytes=64) for j in range(PACK)]
+        w_scale_tiles = [keep.tile([P, N], U8, name="w_scales%d" % g, align_bytes=64) for g in range(E // SHARE)]
+        x_f32 = [keep.tile([P, T], F32, name="x_f32_%d" % j, align_bytes=64) for j in range(PACK)]
         x_bf16 = [keep.tile([P, T], BF16, name="x_bf16_%d" % j, align_bytes=64) for j in range(PACK)]
         gate_first = keep.tile([P, 2 * C], F32, name="gate_first")
         gate_rest = keep.tile([P, (E - 2) * C], F32, name="gate_rest")
 
-        warm = keep.tile([P, 16], F32, name="warm")
-        warm_out = keep.tile([P, 16], F32, name="warm_out")
-        third = keep.tile([P, 2 * C, PACK], BF16, name="third", align_bytes=64)
-        third_words = third[:].rearrange("p s j -> p (s j)").bitcast(F32)
-        nc.vector.memset(third_words[:, 1:2], 0.0)
-        fourth = keep.tile([P, 2 * C, PACK], BF16, name="fourth", align_bytes=64)
-        fourth_words = fourth[:].rearrange("p s j -> p (s j)").bitcast(F32)
-        nc.vector.memset(fourth_words[:, 0:2], 0.0)
-        second = keep.tile([P, C, PACK], BF16, name="second", align_bytes=64)
-        second_words = second[:].rearrange("p s j -> p (s j)").bitcast(F32)
-        nc.vector.memset(second_words[:, 1:2], 0.0)
-        bias_of = {(0, 0): second_words[:, 1:2], (0, 1): warm_out[:, 0:1], (0, 2): third[:, 0, 2:3], (1, 0): third[:, 0, 3:4], (1, 1): fourth_words[:, 0:1], (2, 0): fourth_words[:, 1:2]}
         nc.vector.memset(far_bytes[:].bitcast(I32), 0)
-        nc.vector.memset(warm[:], 0.0)
-        nc.vector.memset(w_planes[1][:].bitcast(I32), 0)
-        nc.scalar.activation(warm_out[:], warm[:], GELU)
+        for tile in w_scale_tiles:
+            nc.vector.memset(tile[:].bitcast(I32), 0)
 
-        w_tiles = {}
+        zeros = keep.tile([P, 16], F32, name="zeros")
+        gelu_of_zeros = keep.tile([P, 16], F32, name="gelu_of_zeros")
+        nc.vector.memset(zeros[:], 0.0)
+        nc.scalar.activation(gelu_of_zeros[:], zeros[:], GELU)
 
-        def load_w(experts):
-            tile = keep.tile([P, len(experts), N], I32, name="w_codes%d" % experts[0], align_bytes=64)
-            src = w_words[experts[0] : experts[-1] + 1, 0].rearrange("e p n d -> p e (n d)").bitcast(I32)
-            for i, e in enumerate(experts):
-                w_tiles[e] = tile[:, i, :]
-            return tile, src
+        grouped = {}
+        for c in (1, 2, 3):
+            grouped[c] = keep.tile([P, len(CHUNKS[c]) * C, PACK], BF16, name="grouped%d" % c, align_bytes=64)
 
-        def load_w_scales(g, queue):
+        def plane_pair(c, h):
+            return grouped[c][:].rearrange("p s j -> p (s j)").bitcast(F32)[:, h : h + 1]
+
+        nc.vector.memset(plane_pair(1, 1), 0.0)
+        nc.vector.memset(plane_pair(2, 1), 0.0)
+        nc.vector.memset(grouped[3][:, 0, :], 0.0)
+        bias_of = {
+            (0, 0): plane_pair(1, 1),
+            (0, 1): gelu_of_zeros[:, 0:1],
+            (0, 2): grouped[2][:, 0, 2:3],
+            (1, 0): grouped[2][:, 0, 3:4],
+            (1, 1): plane_pair(3, 0),
+            (2, 0): plane_pair(3, 1),
+        }
+
+        def load_w_scales(g):
             for quad in range(4):
-                queue.dma_start(
-                    w_planes[g][32 * quad : 32 * quad + 4 * (E - 4 * g), :].bitcast(I32),
-                    w_scales[4 * g :, 0, 4 * quad : 4 * quad + 4, :].bitcast(I32),
+                nc.sync.dma_start(
+                    w_scale_tiles[g][32 * quad : 32 * quad + 4 * SHARE, :].bitcast(I32),
+                    w_scales[SHARE * g : SHARE * (g + 1), 0, 4 * quad : 4 * quad + 4, :].bitcast(I32),
                 )
 
+        w_chunks, w_of = [], {}
+        for experts in CHUNKS:
+            tile = keep.tile([P, len(experts), N], I32, name="w_codes%d" % experts[0], align_bytes=64)
+            w_chunks.append(tile)
+            for i, e in enumerate(experts):
+                w_of[e] = tile[:, i, :]
+
+        def load_w(c, cols):
+            src = w_words[CHUNKS[c][0] : CHUNKS[c][-1] + 1, 0].rearrange("e p n d -> p e (n d)").bitcast(I32)
+            nc.sync.dma_start(w_chunks[c][:, :, cols], src[:, :, cols])
+
+        xo_planes = xo.rearrange("(p j) t -> p j t", j=PACK)
         nc.sync.dma_start(far_list[:], offs2)
         nc.sync.dma_start(far_words[:], x_words[0].rearrange("p t d -> p (t d)").bitcast(I32))
-        xo_planes = xo.rearrange("(p j) t -> p j t", j=PACK)
         nc.sync.dma_start(own_list[:], offs)
-        for j in range(2):
+        for j in (0, 1):
             nc.sync.dma_start(x_f32[j][:], xo_planes[:, j, :])
         for quad in range(4):
             nc.sync.dma_start(
                 far_bytes[32 * quad : 32 * quad + 4, :].bitcast(I32),
                 x_scales[0, 4 * quad : 4 * quad + 4, :].bitcast(I32),
             )
-        for j in range(2, PACK):
+        for j in (2, 3):
             nc.sync.dma_start(x_f32[j][:], xo_planes[:, j, :])
-        load_w_scales(0, nc.sync)
-        loads = [load_w(experts) for experts in W_LOADS]
-        nc.sync.dma_start(loads[0][0][:, :, : N // 2], loads[0][1][:, :, : N // 2])
+        load_w_scales(0)
+        load_w(0, slice(0, N // 2))
         nc.sync.dma_start(gate_first[:], gate[:, : 2 * C])
-        nc.sync.dma_start(loads[0][0][:, :, N // 2 :], loads[0][1][:, :, N // 2 :])
-        nc.sync.dma_start(loads[1][0][:], loads[1][1])
-        nc.sync.dma_start(loads[2][0][:], loads[2][1])
+        load_w(0, slice(N // 2, N))
+        load_w(1, slice(0, N))
+        load_w(2, slice(0, N))
         nc.sync.dma_start(gate_rest[:], gate[:, 2 * C :])
-        load_w_scales(1, nc.sync)
-        nc.sync.dma_start(loads[3][0][:], loads[3][1])
-        nc.sync.dma_start(loads[4][0][:], loads[4][1])
-
-        def gate_of(s0, n):
-            return gate_first[:, s0 : s0 + n] if s0 < 2 * C else gate_rest[:, s0 - 2 * C : s0 - 2 * C + n]
+        load_w_scales(1)
+        load_w(3, slice(0, N))
+        load_w(4, slice(0, N))
 
         def multiply(acc, e, t, codes, scales):
             cols = slice(t * P, (t + 1) * P)
             nc.tensor.matmul_mx(
                 out=acc,
-                lhsT=w_tiles[e][:, cols].bitcast(FP8X4),
-                lhsT_scale=w_planes[e // 4][4 * (e % 4) :, cols],
+                lhsT=w_of[e][:, cols].bitcast(FP8X4),
+                lhsT_scale=w_scale_tiles[e // SHARE][4 * (e % SHARE) :, cols],
                 rhs=codes.bitcast(FP8X4),
                 rhs_scale=scales,
                 start=True,
@@ -120,10 +134,10 @@ def tile_moe_loc_lin_gelu_kernel(tc, x_words, x_scales, xo, w_words, w_scales, g
         far_scales = {}
 
         def gather_far(dst, window, first, count):
-            for e0 in range(0, count, 2):
-                e1 = min(e0 + 2, count)
-                offsets = far_list[:, (first + e0) * C // 16 : (first + e1) * C // 16]
-                nc.vector.tensor_copy(dst[:, e0 * C : e1 * C], window.indirect(offsets))
+            for i0 in range(0, count, 2):
+                i1 = min(i0 + 2, count)
+                offsets = far_list[:, (first + i0) * C // PER_COL : (first + i1) * C // PER_COL]
+                nc.vector.tensor_copy(dst[:, i0 * C : i1 * C], window.indirect(offsets))
 
         def gather_far_bytes(first, count, offset):
             tile = turns.tile([P, count * C], U8, name="far_scales%d" % first, align_bytes=64, offset=offset)
@@ -132,44 +146,32 @@ def tile_moe_loc_lin_gelu_kernel(tc, x_words, x_scales, xo, w_words, w_scales, g
                 far_scales[first + i] = tile[:, i * C : (i + 1) * C]
 
         gather_far(far_codes, far_words[:].bitcast(U32), 0, E)
-        gather_far_bytes(0, EARLY, 2560)
+        gather_far_bytes(0, EARLY, EARLY_AT)
 
-        def cast(j, cols, factor=1.0):
-            nc.gpsimd.tensor_scalar(x_bf16[j][:, cols], x_f32[j][:, cols], factor, 0.0, MULT, ADD)
-
-        cast(0, slice(0, T // 2))
-        nc.scalar.copy(x_bf16[0][:, T // 2 :], x_f32[0][:, T // 2 :])
-        cast(1, slice(0, T))
-        cast(2, slice(0, T))
-        cast(3, slice(0, SPLIT))
+        nc.scalar.copy(x_bf16[0][:, SECOND_HALF], x_f32[0][:, SECOND_HALF])
+        for j, cols in ((0, FIRST_HALF), (1, slice(0, T)), (2, slice(0, T))):
+            nc.gpsimd.tensor_scalar(x_bf16[j][:, cols], x_f32[j][:, cols], 1.0, 0.0, MULT, ADD)
 
         own_out = [keep.tile([P, T], F32, name="own_out%d" % t) for t in range(NT)]
-        grouped, results = {}, {}
+        results = {}
+        last = len(CHUNKS) - 1
 
         def span(c):
-            return OWN_CHUNKS[c][0] * C, len(OWN_CHUNKS[c]) * C
+            return CHUNKS[c][0] * C, len(CHUNKS[c]) * C
+
+        def own_offsets(c):
+            s0, n = span(c)
+            return own_list[:, s0 // PER_COL : (s0 + n) // PER_COL]
 
         def gather(c, planes):
-            s0, n = span(c)
-            tag = ("first", "second", "third", "scales2", "scales3")[c]
-            if c == 0:
-                grouped[c] = turns.tile([P, n, PACK], BF16, name="first", align_bytes=64, offset=1536)
-            elif c in (1, 2, 3):
-                grouped[c] = (second, third, fourth)[c - 1]
-            else:
-                grouped[c] = keep.tile([P, n, PACK], BF16, name="grouped%d" % c, align_bytes=64, tag=tag)
-            offsets = own_list[:, s0 // 16 : (s0 + n) // 16]
             for j in planes:
-                if c == 0 and j >= 2:
-                    nc.vector.tensor_copy(grouped[c][:, :, j], x_f32[j][:].indirect(offsets))
-                else:
-                    nc.scalar.activation(grouped[c][:, :, j], x_bf16[j][:].indirect(offsets), COPY)
+                nc.scalar.activation(grouped[c][:, :, j], x_bf16[j][:].indirect(own_offsets(c)), COPY)
 
-        def activate(c, tiles, codes, scales):
+        def activate(c, tiles, bank, codes, scales):
             n = span(c)[1]
-            acc = psum.tile([P, len(tiles), n], F32, name="own_acc", tag="bank%d_%d" % (c % 2, min(tiles[0], 1) if c in (0, 2) else tiles[0]))
+            acc = psum.tile([P, len(tiles), n], F32, name="own_acc", tag=bank)
             for u, t in enumerate(tiles):
-                for i, e in enumerate(OWN_CHUNKS[c]):
+                for i, e in enumerate(CHUNKS[c]):
                     slots = slice(i * C, (i + 1) * C)
                     multiply(acc[:, u, slots], e, t, codes[:, slots], scales[:, slots])
             tag = "y%d_%d" % (c, tiles[0])
@@ -178,54 +180,70 @@ def tile_moe_loc_lin_gelu_kernel(tc, x_words, x_scales, xo, w_words, w_scales, g
             for u, t in enumerate(tiles):
                 results[c, t] = y[:, u, :]
 
+        planes_of_next = {0: (2, 3), 1: (3,), 2: (2, 3), 3: (0, 1, 2, 3)}
+        planes_of_next_but_one = {0: (2,), 1: (0, 1)}
+
         def compute(c):
             n = span(c)[1]
             codes = keep.tile([P, n], U32, name="codes%d" % c, align_bytes=64, tag="y%d_0" % (c - 1))
             scales = keep.tile([P, n], U8, name="scales%d" % c, align_bytes=64, tag="scales%d" % c)
-            nc.vector.quantize_mx(out=codes[:].bitcast(FP8X4), scales=scales[:], in_=grouped[c][:].rearrange("p s j -> p (s j)"))
-            activate(c, (0,), codes, scales)
-            activate(c, (1,), codes, scales)
-            if c + 1 < len(OWN_CHUNKS):
-                gather(c + 1, range((2, 3, 2, 0)[c], PACK))
-            activate(c, (2, 3), codes, scales)
-            if c == 0:
-                gather(2, range(2, 3))
-            if c == 1:
-                gather(3, range(2))
+            nc.vector.quantize_mx(
+                out=codes[:].bitcast(FP8X4), scales=scales[:], in_=grouped[c][:].rearrange("p s j -> p (s j)")
+            )
+            banks = ["bank%d_%d" % (c % 2, b) for b in range(3)]
+            activate(c, (0,), banks[0], codes, scales)
+            activate(c, (1,), banks[1], codes, scales)
+            if c + 1 == last:
+                grouped[last] = keep.tile(
+                    [P, span(last)[1], PACK], BF16, name="grouped%d" % last, align_bytes=64, tag="scales%d" % c
+                )
+            ahead = planes_of_next.get(c, ())
+            gather(c + 1, ahead)
+            activate(c, (2, 3), banks[1 if len(ahead) == 2 else 2], codes, scales)
+            gather(c + 2, planes_of_next_but_one.get(c, ()))
 
         def scatter(c, t):
             s0, n = span(c)
-            offsets = own_list[:, s0 // 16 : (s0 + n) // 16]
-            nc.vector.tensor_tensor(own_out[t][:].indirect(offsets), results[c, t], gate_of(s0, n), MULT)
-            if s0 + n == E * C:
+            weights = gate_first[:, s0 : s0 + n] if s0 < 2 * C else gate_rest[:, s0 - 2 * C : s0 - 2 * C + n]
+            nc.vector.tensor_tensor(own_out[t][:].indirect(own_offsets(c)), results[c, t], weights, MULT)
+            if c == last:
                 nc.sync.dma_start(out[t * P : (t + 1) * P, :T], own_out[t][:])
 
-        def far(k, tag):
-            g, t = divmod(k, NT)
-            acc = psum.tile([P, 4 * C], F32, name="far_acc", tag=tag)
-            for i in range(4):
-                e = 4 * g + i
-                slots = slice(i * C, (i + 1) * C)
-                multiply(acc[:, slots], e, t, far_codes[:, e * C : (e + 1) * C], far_scales[e])
-            z = keep.tile([P, 4 * C], F32, name="z%d" % k)
+        def far(unit, bank):
+            g, t = divmod(unit, NT)
+            acc = psum.tile([P, SHARE * C], F32, name="far_acc", tag=bank)
+            for i in range(SHARE):
+                e = SHARE * g + i
+                multiply(acc[:, i * C : (i + 1) * C], e, t, far_codes[:, e * C : (e + 1) * C], far_scales[e])
+            z = keep.tile([P, SHARE * C], F32, name="z%d" % unit)
             nc.scalar.activation(z[:], acc[:], GELU)
-            nc.sync.dma_start(out[t * P : (t + 1) * P, T + g * 4 * C : T + (g + 1) * 4 * C], z[:])
+            nc.sync.dma_start(out[t * P : (t + 1) * P, T + g * SHARE * C : T + (g + 1) * SHARE * C], z[:])
 
-        far_slots = {2: ("bank0_0", "bank0_1"), 3: ("bank1_0", "bank1_1", "bank1_2"), 4: ("bank0_0", "bank0_1", "bank0_2")}
-        gather(0, range(PACK))
-        gather(1, range(2))
-        gather(2, range(2))
-        nc.scalar.copy(x_bf16[3][:, SPLIT:], x_f32[3][:, SPLIT:])
+        far_banks = {
+            2: ("bank0_0", "bank0_1"),
+            3: ("bank1_0", "bank1_1", "bank1_2"),
+            4: ("bank0_0", "bank0_1", "bank0_2"),
+        }
+
+        grouped[0] = turns.tile([P, C, PACK], BF16, name="grouped0", align_bytes=64, offset=FIRST_AT)
+        gather(0, (0, 1))
+        for j in (2, 3):
+            nc.vector.tensor_copy(grouped[0][:, :, j], x_f32[j][:].indirect(own_offsets(0)))
+        nc.vector.tensor_copy(x_bf16[3][:, FIRST_HALF], x_f32[3][:, FIRST_HALF])
+        gather(1, (0, 1))
+        gather(2, (0, 1))
+        nc.scalar.copy(x_bf16[3][:, SECOND_HALF], x_f32[3][:, SECOND_HALF])
         compute(0)
-        gather_far_bytes(EARLY, E - EARLY, 2048)
-        k = 0
-        for c in range(len(OWN_CHUNKS)):
+        gather_far_bytes(EARLY, E - EARLY, LATE_AT)
+
+        unit = 0
+        for c in range(len(CHUNKS)):
             scatter(c, 0)
             scatter(c, 1)
-            if c + 1 < len(OWN_CHUNKS):
+            if c < last:
                 compute(c + 1)
-            for tag in far_slots.get(c + 1, ()):
-                far(k, tag)
-                k += 1
+            for bank in far_banks.get(c + 1, ()):
+                far(unit, bank)
+                unit += 1
             scatter(c, 2)
             scatter(c, 3)

@@ -95,11 +95,11 @@ def tile_moe_loc_lin_gelu_kernel(
             nc.sync.dma_start(w_chunks[c][:, :, cols], src[:, :, cols])
 
         xo_planes = xo.rearrange("(p j) t -> p j t", j=PACK)
-        nc.sync.dma_start(far_list[:], offs2)
         nc.sync.dma_start(far_words[:], x_words[0].rearrange("p t d -> p (t d)").bitcast(I32))
+        nc.sync.dma_start(far_list[:], offs2)
+        nc.sync.dma_start(x_f32[0][:], xo_planes[:, 0, :])
         nc.sync.dma_start(own_list[:], offs)
-        for j in (0, 1):
-            nc.sync.dma_start(x_f32[j][:], xo_planes[:, j, :])
+        nc.sync.dma_start(x_f32[1][:], xo_planes[:, 1, :])
         for quad in range(4):
             nc.sync.dma_start(
                 far_bytes[32 * quad : 32 * quad + 4, :].bitcast(I32),

@@ -58,7 +58,7 @@ def tile_moe_loc_lin_gelu_kernel(
         nc.scalar.activation(gelu_of_zeros[:], zeros[:], GELU)
 
         grouped = {}
-        for c in (1, 2, 3):
+        for c in (1, 2, 3, 4):
             grouped[c] = keep.tile([P, len(CHUNKS[c]) * C, PACK], BF16, name="grouped%d" % c, align_bytes=64)
 
         def plane_pair(c, h):
@@ -67,6 +67,7 @@ def tile_moe_loc_lin_gelu_kernel(
         nc.vector.memset(plane_pair(1, 1), 0.0)
         nc.vector.memset(plane_pair(2, 1), 0.0)
         nc.vector.memset(grouped[3][:, 0, :], 0.0)
+        nc.vector.memset(grouped[4][:, 0, :], 0.0)
         bias_of = {
             (0, 0): plane_pair(1, 1),
             (0, 1): gelu_of_zeros[:, 0:1],
@@ -74,6 +75,8 @@ def tile_moe_loc_lin_gelu_kernel(
             (1, 0): grouped[2][:, 0, 3:4],
             (1, 1): plane_pair(3, 0),
             (2, 0): plane_pair(3, 1),
+            (3, 0): plane_pair(4, 0),
+            (3, 1): plane_pair(4, 1),
         }
 
         def load_w_scales(g):
@@ -167,6 +170,8 @@ def tile_moe_loc_lin_gelu_kernel(
             for j in planes:
                 nc.scalar.activation(grouped[c][:, :, j], x_bf16[j][:].indirect(own_offsets(c)), COPY)
 
+        y_end = keep.tile([P, 2, span(last - 1)[1] + span(last)[1]], F32, name="y_end", align_bytes=64)
+
         def activate(c, tiles, bank, codes, scales):
             n = span(c)[1]
             acc = psum.tile([P, len(tiles), n], F32, name="own_acc", tag=bank)
@@ -175,8 +180,11 @@ def tile_moe_loc_lin_gelu_kernel(
                     slots = slice(i * C, (i + 1) * C)
                     multiply(acc[:, u, slots], e, t, codes[:, slots], scales[:, slots])
             tag = "y%d_%d" % (c, tiles[0])
-            y = keep.tile([P, len(tiles), n], F32, name=tag, align_bytes=64, tag=tag)
-            nc.scalar.activation(y[:], acc[:], GELU, bias=bias_of.get((c, tiles[0]), 0.0))
+            if c >= last - 1 and tiles == (2, 3):
+                y = y_end[:, :, (c - last + 1) * n : (c - last + 2) * n]
+            else:
+                y = keep.tile([P, len(tiles), n], F32, name=tag, align_bytes=64, tag=tag)[:]
+            nc.scalar.activation(y, acc[:], GELU, bias=bias_of.get((c, tiles[0]), 0.0))
             for u, t in enumerate(tiles):
                 results[c, t] = y[:, u, :]
 
@@ -193,13 +201,9 @@ def tile_moe_loc_lin_gelu_kernel(
             banks = ["bank%d_%d" % (c % 2, b) for b in range(3)]
             activate(c, (0,), banks[0], codes, scales)
             activate(c, (1,), banks[1], codes, scales)
-            if c + 1 == last:
-                grouped[last] = keep.tile(
-                    [P, span(last)[1], PACK], BF16, name="grouped%d" % last, align_bytes=64, tag="scales%d" % c
-                )
             ahead = planes_of_next.get(c, ())
             gather(c + 1, ahead)
-            activate(c, (2, 3), banks[1 if len(ahead) == 2 else 2], codes, scales)
+            activate(c, (2, 3), banks[1 if len(ahead) >= 2 else 2], codes, scales)
             gather(c + 2, planes_of_next_but_one.get(c, ()))
 
         def scatter(c, t):
@@ -220,9 +224,9 @@ def tile_moe_loc_lin_gelu_kernel(
             nc.sync.dma_start(out[t * P : (t + 1) * P, T + g * SHARE * C : T + (g + 1) * SHARE * C], z[:])
 
         far_banks = {
-            2: ("bank0_0", "bank0_1"),
-            3: ("bank1_0", "bank1_1", "bank1_2"),
-            4: ("bank0_0", "bank0_1", "bank0_2"),
+            2: ("bank0_0", "bank0_1", "bank0_0"),
+            3: ("bank1_0",),
+            4: ("bank0_0", "bank0_1", "bank0_2", "bank0_0"),
         }
 
         grouped[0] = turns.tile([P, C, PACK], BF16, name="grouped0", align_bytes=64, offset=FIRST_AT)
@@ -246,4 +250,10 @@ def tile_moe_loc_lin_gelu_kernel(
                 far(unit, bank)
                 unit += 1
             scatter(c, 2)
-            scatter(c, 3)
+            if c < last - 1:
+                scatter(c, 3)
+        s0 = span(last - 1)[0]
+        nc.vector.tensor_tensor(
+            own_out[3][:].indirect(own_list[:, s0 // PER_COL :]), y_end[:, 1, :], gate_rest[:, s0 - 2 * C :], MULT
+        )
+        nc.sync.dma_start(out[3 * P :, :T], own_out[3][:])

@@ -44,7 +44,7 @@ def tile_moe_loc_lin_gelu_kernel(
         far_bytes = keep.tile([P, Q], U8, name="far_bytes", align_bytes=64)
         w_scale_tiles = [keep.tile([P, N], U8, name="w_scales%d" % g, align_bytes=64) for g in range(E // SHARE)]
         x_f32 = [keep.tile([P, T], F32, name="x_f32_%d" % j, align_bytes=64) for j in range(PACK)]
-        x_bf16 = [keep.tile([P, T], BF16, name="x_bf16_%d" % j, align_bytes=64) for j in range(PACK)]
+        x_bf16 = [keep.tile([P, T], BF16, name="x_bf16_%d" % j, align_bytes=64, tag="plane%d" % j) for j in range(PACK)]
         gate_first = keep.tile([P, 2 * C], F32, name="gate_first")
         gate_rest = keep.tile([P, (E - 2) * C], F32, name="gate_rest")
 
@@ -213,20 +213,20 @@ def tile_moe_loc_lin_gelu_kernel(
             if c == last:
                 nc.sync.dma_start(out[t * P : (t + 1) * P, :T], own_out[t][:])
 
-        def far(unit, bank):
+        def far(unit, bank, buffer):
             g, t = divmod(unit, NT)
             acc = psum.tile([P, SHARE * C], F32, name="far_acc", tag=bank)
             for i in range(SHARE):
                 e = SHARE * g + i
                 multiply(acc[:, i * C : (i + 1) * C], e, t, far_codes[:, e * C : (e + 1) * C], far_scales[e])
-            z = keep.tile([P, SHARE * C], F32, name="z%d" % unit)
+            z = keep.tile([P, SHARE * C], F32, name="z%d" % unit, align_bytes=64, tag=buffer or "z%d" % unit)
             nc.scalar.activation(z[:], acc[:], GELU)
             nc.sync.dma_start(out[t * P : (t + 1) * P, T + g * SHARE * C : T + (g + 1) * SHARE * C], z[:])
 
         far_banks = {
-            2: ("bank0_0", "bank0_1", "bank0_0"),
-            3: ("bank1_0",),
-            4: ("bank0_0", "bank0_1", "bank0_2", "bank0_0"),
+            2: (("bank0_0", None), ("bank0_1", None), ("bank0_0", None)),
+            3: (("bank1_0", None), ("spare0", "plane2"), ("spare1", "plane3")),
+            4: (("bank0_0", None), ("bank0_1", None)),
         }
 
         grouped[0] = turns.tile([P, C, PACK], BF16, name="grouped0", align_bytes=64, offset=FIRST_AT)
@@ -246,8 +246,8 @@ def tile_moe_loc_lin_gelu_kernel(
             scatter(c, 1)
             if c < last:
                 compute(c + 1)
-            for bank in far_banks.get(c + 1, ()):
-                far(unit, bank)
+            for bank, buffer in far_banks.get(c + 1, ()):
+                far(unit, bank, buffer)
                 unit += 1
             scatter(c, 2)
             if c < last - 1:

@@ -73,8 +73,9 @@ def tile_moe_loc_lin_gelu_kernel(
             (0, 1): gelu_of_zeros[:, 0:1],
             (0, 2): grouped[2][:, 0, 2:3],
             (1, 0): grouped[2][:, 0, 3:4],
-            (1, 1): plane_pair(3, 0),
-            (2, 0): plane_pair(3, 1),
+            (1, 1): grouped[3][:, 0, 0:1],
+            (2, 0): grouped[3][:, 0, 1:2],
+            (2, 1): plane_pair(3, 1),
             (3, 0): plane_pair(4, 0),
             (3, 1): plane_pair(4, 1),
         }
@@ -188,8 +189,8 @@ def tile_moe_loc_lin_gelu_kernel(
             for u, t in enumerate(tiles):
                 results[c, t] = y[:, u, :]
 
-        planes_of_next = {0: (2, 3), 1: (3,), 2: (2, 3), 3: (0, 1, 2, 3)}
-        planes_of_next_but_one = {0: (2,), 1: (0, 1)}
+        planes_of_next = {0: (2, 3), 1: (3,), 2: (1, 2, 3), 3: (0, 1, 2, 3)}
+        planes_of_next_but_one = {0: (2,), 1: (0,)}
 
         def compute(c):
             n = span(c)[1]
@@ -198,7 +199,7 @@ def tile_moe_loc_lin_gelu_kernel(
             nc.vector.quantize_mx(
                 out=codes[:].bitcast(FP8X4), scales=scales[:], in_=grouped[c][:].rearrange("p s j -> p (s j)")
             )
-            banks = ["bank%d_%d" % (c % 2, b) for b in range(3)]
+            banks = ["bank%d_%d" % (c % 2, b) for b in range(3)] if c < last else ["spare0", "spare1", "bank0_2"]
             activate(c, (0,), banks[0], codes, scales)
             activate(c, (1,), banks[1], codes, scales)
             ahead = planes_of_next.get(c, ())
@@ -213,7 +214,7 @@ def tile_moe_loc_lin_gelu_kernel(
             if c == last:
                 nc.sync.dma_start(out[t * P : (t + 1) * P, :T], own_out[t][:])
 
-        def far(unit, bank, buffer):
+        def far(unit, bank, buffer, queue):
             g, t = divmod(unit, NT)
             acc = psum.tile([P, SHARE * C], F32, name="far_acc", tag=bank)
             for i in range(SHARE):
@@ -221,12 +222,12 @@ def tile_moe_loc_lin_gelu_kernel(
                 multiply(acc[:, i * C : (i + 1) * C], e, t, far_codes[:, e * C : (e + 1) * C], far_scales[e])
             z = keep.tile([P, SHARE * C], F32, name="z%d" % unit, align_bytes=64, tag=buffer or "z%d" % unit)
             nc.scalar.activation(z[:], acc[:], GELU)
-            nc.sync.dma_start(out[t * P : (t + 1) * P, T + g * SHARE * C : T + (g + 1) * SHARE * C], z[:])
+            queue.dma_start(out[t * P : (t + 1) * P, T + g * SHARE * C : T + (g + 1) * SHARE * C], z[:])
 
         far_banks = {
-            2: (("bank0_0", None), ("bank0_1", None), ("bank0_0", None)),
-            3: (("bank1_0", None), ("spare0", "plane2"), ("spare1", "plane3")),
-            4: (("bank0_0", None), ("bank0_1", None)),
+            2: (("bank0_0", None), ("bank0_1", None)),
+            3: (("bank1_0", None), ("bank0_0", "plane2"), ("bank0_1", "plane3")),
+            4: (("spare0", None), ("spare1", None), ("bank0_2", None)),
         }
 
         grouped[0] = turns.tile([P, C, PACK], BF16, name="grouped0", align_bytes=64, offset=FIRST_AT)
@@ -247,7 +248,7 @@ def tile_moe_loc_lin_gelu_kernel(
             if c < last:
                 compute(c + 1)
             for bank, buffer in far_banks.get(c + 1, ()):
-                far(unit, bank, buffer)
+                far(unit, bank, buffer, nc.scalar if c + 1 == last else nc.sync)
                 unit += 1
             scatter(c, 2)
             if c < last - 1:

@@ -22,11 +22,11 @@ PACK = 4
 NT = N // P
 PER_COL = 16
 SHARE = 4
+HALF = T // 2
 
 CHUNKS = ((0,), (1,), (2, 3), (4, 5), (6, 7))
-FIRST_HALF, SECOND_HALF = slice(0, T // 2), slice(T // 2, T)
-EARLY = 5
-FIRST_AT, LATE_AT, EARLY_AT = 0, 512, 1024
+EARLY = 4
+ON_SCALAR = 256
 
 
 def tile_moe_loc_lin_gelu_kernel(
@@ -35,50 +35,28 @@ def tile_moe_loc_lin_gelu_kernel(
     nc = tc.nc
     with ExitStack() as ctx:
         keep = ctx.enter_context(tc.tile_pool(name="keep", bufs=1))
-        turns = ctx.enter_context(tc.tile_pool(name="turns", bufs=1))
         psum = ctx.enter_context(tc.psum_pool(name="psum", bufs=1))
+
+        def sbuf(shape, dtype, name, tag=None):
+            return keep.tile(shape, dtype, name=name, align_bytes=64, tag=tag or name)
 
         own_list = keep.tile([P, E * C // PER_COL], U16, name="own_list")
         far_list = keep.tile([P, E * C // PER_COL], U16, name="far_list")
-        far_words = keep.tile([P, Q], I32, name="far_words", align_bytes=64)
-        far_bytes = keep.tile([P, Q], U8, name="far_bytes", align_bytes=64)
-        w_scale_tiles = [keep.tile([P, N], U8, name="w_scales%d" % g, align_bytes=64) for g in range(E // SHARE)]
-        x_f32 = [keep.tile([P, T], F32, name="x_f32_%d" % j, align_bytes=64) for j in range(PACK)]
-        x_bf16 = [keep.tile([P, T], BF16, name="x_bf16_%d" % j, align_bytes=64, tag="plane%d" % j) for j in range(PACK)]
-        gate_first = keep.tile([P, 2 * C], F32, name="gate_first")
-        gate_rest = keep.tile([P, (E - 2) * C], F32, name="gate_rest")
+        far_words = sbuf([P, Q], I32, "far_words")
+        far_bytes = sbuf([P, Q], U8, "far_bytes")
+        w_scale_tiles = [sbuf([P, N], U8, "w_scales%d" % g) for g in range(E // SHARE)]
+        x_f32 = [sbuf([P, 2, T], F32, "x_f32_%d" % h) for h in range(2)]
+        pairs = [sbuf([P, T, 2], BF16, "pairs%d" % h) for h in range(2)]
+        gates = sbuf([P, E * C], F32, "gates")
 
         nc.vector.memset(far_bytes[:].bitcast(I32), 0)
         for tile in w_scale_tiles:
             nc.vector.memset(tile[:].bitcast(I32), 0)
 
-        zeros = keep.tile([P, 16], F32, name="zeros")
-        gelu_of_zeros = keep.tile([P, 16], F32, name="gelu_of_zeros")
+        zeros = sbuf([P, 16], F32, "zeros")
+        gelu_of_zeros = sbuf([P, 16], F32, "gelu_of_zeros")
         nc.vector.memset(zeros[:], 0.0)
         nc.scalar.activation(gelu_of_zeros[:], zeros[:], GELU)
-
-        grouped = {}
-        for c in (1, 2, 3, 4):
-            grouped[c] = keep.tile([P, len(CHUNKS[c]) * C, PACK], BF16, name="grouped%d" % c, align_bytes=64)
-
-        def plane_pair(c, h):
-            return grouped[c][:].rearrange("p s j -> p (s j)").bitcast(F32)[:, h : h + 1]
-
-        nc.vector.memset(plane_pair(1, 1), 0.0)
-        nc.vector.memset(plane_pair(2, 1), 0.0)
-        nc.vector.memset(grouped[3][:, 0, :], 0.0)
-        nc.vector.memset(grouped[4][:, 0, :], 0.0)
-        bias_of = {
-            (0, 0): plane_pair(1, 1),
-            (0, 1): gelu_of_zeros[:, 0:1],
-            (0, 2): grouped[2][:, 0, 2:3],
-            (1, 0): grouped[2][:, 0, 3:4],
-            (1, 1): grouped[3][:, 0, 0:1],
-            (2, 0): grouped[3][:, 0, 1:2],
-            (2, 1): plane_pair(3, 1),
-            (3, 0): plane_pair(4, 0),
-            (3, 1): plane_pair(4, 1),
-        }
 
         def load_w_scales(g):
             for quad in range(4):
@@ -89,7 +67,7 @@ def tile_moe_loc_lin_gelu_kernel(
 
         w_chunks, w_of = [], {}
         for experts in CHUNKS:
-            tile = keep.tile([P, len(experts), N], I32, name="w_codes%d" % experts[0], align_bytes=64)
+            tile = sbuf([P, len(experts), N], I32, "w_codes%d" % experts[0])
             w_chunks.append(tile)
             for i, e in enumerate(experts):
                 w_of[e] = tile[:, i, :]
@@ -99,25 +77,30 @@ def tile_moe_loc_lin_gelu_kernel(
             nc.sync.dma_start(w_chunks[c][:, :, cols], src[:, :, cols])
 
         xo_planes = xo.rearrange("(p j) t -> p j t", j=PACK)
+
+        def load_x(h, s):
+            cols = slice(s * HALF, (s + 1) * HALF)
+            nc.sync.dma_start(x_f32[h][:, :, cols], xo_planes[:, 2 * h : 2 * h + 2, cols])
+
         nc.sync.dma_start(far_words[:], x_words[0].rearrange("p t d -> p (t d)").bitcast(I32))
         nc.sync.dma_start(far_list[:], offs2)
-        nc.sync.dma_start(x_f32[0][:], xo_planes[:, 0, :])
+        load_x(0, 0)
         nc.sync.dma_start(own_list[:], offs)
-        nc.sync.dma_start(x_f32[1][:], xo_planes[:, 1, :])
+        load_x(0, 1)
         for quad in range(4):
             nc.sync.dma_start(
                 far_bytes[32 * quad : 32 * quad + 4, :].bitcast(I32),
                 x_scales[0, 4 * quad : 4 * quad + 4, :].bitcast(I32),
             )
-        for j in (2, 3):
-            nc.sync.dma_start(x_f32[j][:], xo_planes[:, j, :])
+        load_x(1, 0)
+        load_x(1, 1)
         load_w_scales(0)
-        load_w(0, slice(0, N // 2))
-        nc.sync.dma_start(gate_first[:], gate[:, : 2 * C])
         load_w(0, slice(N // 2, N))
+        nc.sync.dma_start(gates[:, : 2 * C], gate[:, : 2 * C])
+        load_w(0, slice(0, N // 2))
         load_w(1, slice(0, N))
         load_w(2, slice(0, N))
-        nc.sync.dma_start(gate_rest[:], gate[:, 2 * C :])
+        nc.sync.dma_start(gates[:, 2 * C :], gate[:, 2 * C :])
         load_w_scales(1)
         load_w(3, slice(0, N))
         load_w(4, slice(0, N))
@@ -134,7 +117,7 @@ def tile_moe_loc_lin_gelu_kernel(
                 stop=True,
             )
 
-        far_codes = keep.tile([P, E * C], U32, name="far_codes", align_bytes=64)
+        far_codes = sbuf([P, E * C], U32, "far_codes")
         far_scales = {}
 
         def gather_far(dst, window, first, count):
@@ -143,118 +126,144 @@ def tile_moe_loc_lin_gelu_kernel(
                 offsets = far_list[:, (first + i0) * C // PER_COL : (first + i1) * C // PER_COL]
                 nc.vector.tensor_copy(dst[:, i0 * C : i1 * C], window.indirect(offsets))
 
-        def gather_far_bytes(first, count, offset):
-            tile = turns.tile([P, count * C], U8, name="far_scales%d" % first, align_bytes=64, offset=offset)
+        def gather_far_bytes(first, count, tag):
+            tile = sbuf([P, count * C], U8, "far_scales%d" % first, tag)
             gather_far(tile, far_bytes[:], first, count)
             for i in range(count):
                 far_scales[first + i] = tile[:, i * C : (i + 1) * C]
 
         gather_far(far_codes, far_words[:].bitcast(U32), 0, E)
-        gather_far_bytes(0, EARLY, EARLY_AT)
+        gather_far_bytes(0, EARLY, None)
 
-        nc.scalar.copy(x_bf16[0][:, SECOND_HALF], x_f32[0][:, SECOND_HALF])
-        for j, cols in ((0, FIRST_HALF), (1, slice(0, T)), (2, slice(0, T))):
-            nc.gpsimd.tensor_scalar(x_bf16[j][:, cols], x_f32[j][:, cols], 1.0, 0.0, MULT, ADD)
+        for h in range(2):
+            for s in range(2):
+                src = x_f32[h][:, :, s * HALF : (s + 1) * HALF].rearrange("p j t -> p t j")
+                dst = pairs[h][:, s * HALF : (s + 1) * HALF, :]
+                nc.scalar.copy(dst[:, :ON_SCALAR, :], src[:, :ON_SCALAR, :])
+                nc.gpsimd.tensor_scalar(dst[:, ON_SCALAR:, :], src[:, ON_SCALAR:, :], 1.0, 0.0, MULT, ADD)
 
-        own_out = [keep.tile([P, T], F32, name="own_out%d" % t) for t in range(NT)]
-        results = {}
         last = len(CHUNKS) - 1
 
         def span(c):
-            return CHUNKS[c][0] * C, len(CHUNKS[c]) * C
+            return slice(CHUNKS[c][0] * C, (CHUNKS[c][-1] + 1) * C)
 
-        def own_offsets(c):
-            s0, n = span(c)
-            return own_list[:, s0 // PER_COL : (s0 + n) // PER_COL]
+        def width(c):
+            return len(CHUNKS[c]) * C
 
-        def gather(c, planes):
-            for j in planes:
-                nc.scalar.activation(grouped[c][:, :, j], x_bf16[j][:].indirect(own_offsets(c)), COPY)
+        def own_offsets(slots):
+            return own_list[:, slots.start // PER_COL : slots.stop // PER_COL]
 
-        y_end = keep.tile([P, 2, span(last - 1)[1] + span(last)[1]], F32, name="y_end", align_bytes=64)
+        grouped = {}
 
-        def activate(c, tiles, bank, codes, scales):
-            n = span(c)[1]
-            acc = psum.tile([P, len(tiles), n], F32, name="own_acc", tag=bank)
+        def gather(c):
+            grouped[c] = sbuf([P, width(c), PACK], BF16, "grouped%d" % c, "b%d" % (c - 2))
+            words = grouped[c][:].rearrange("p s j -> p (s j)").bitcast(U32).rearrange("p (s h) -> p s h", h=2)
+            for h in range(2 if c else 1):
+                window = pairs[h][:].rearrange("p t j -> p (t j)").bitcast(U32)
+                nc.vector.tensor_copy(words[:, :, h], window.indirect(own_offsets(span(c))))
+            if c == 0:
+                for j in range(2):
+                    nc.vector.tensor_copy(grouped[c][:, :, 2 + j], x_f32[1][:, j, :].indirect(own_offsets(span(c))))
+
+        y_vector = sbuf([P, 2, E * C], F32, "y_vector")
+        gated = {t: sbuf([P, E * C], F32, "gated%d" % t) for t in (2, 3)}
+        y_scalar = {}
+
+        def products(c, tiles, bank, codes, scales):
+            acc = psum.tile([P, len(tiles), width(c)], F32, name="own_acc", tag=bank)
             for u, t in enumerate(tiles):
                 for i, e in enumerate(CHUNKS[c]):
                     slots = slice(i * C, (i + 1) * C)
                     multiply(acc[:, u, slots], e, t, codes[:, slots], scales[:, slots])
-            tag = "y%d_%d" % (c, tiles[0])
-            if c >= last - 1 and tiles == (2, 3):
-                y = y_end[:, :, (c - last + 1) * n : (c - last + 2) * n]
-            else:
-                y = keep.tile([P, len(tiles), n], F32, name=tag, align_bytes=64, tag=tag)[:]
-            nc.scalar.activation(y, acc[:], GELU, bias=bias_of.get((c, tiles[0]), 0.0))
-            for u, t in enumerate(tiles):
-                results[c, t] = y[:, u, :]
+            return acc
 
-        planes_of_next = {0: (2, 3), 1: (3,), 2: (1, 2, 3), 3: (0, 1, 2, 3)}
-        planes_of_next_but_one = {0: (2,), 1: (0,)}
+        quantised = {}
+
+        def activate_vector(c, bank):
+            acc = products(c, (0, 1), bank, *quantised[c])
+            nc.scalar.activation(y_vector[:, :, span(c)], acc[:], GELU)
 
         def compute(c):
-            n = span(c)[1]
-            codes = keep.tile([P, n], U32, name="codes%d" % c, align_bytes=64, tag="y%d_0" % (c - 1))
-            scales = keep.tile([P, n], U8, name="scales%d" % c, align_bytes=64, tag="scales%d" % c)
+            codes = sbuf([P, width(c)], U32, "codes%d" % c, "a%d" % (c - 1))
+            scales = sbuf([P, width(c)], U8, "scales%d" % c)
             nc.vector.quantize_mx(
                 out=codes[:].bitcast(FP8X4), scales=scales[:], in_=grouped[c][:].rearrange("p s j -> p (s j)")
             )
-            banks = ["bank%d_%d" % (c % 2, b) for b in range(3)] if c < last else ["spare0", "spare1", "bank0_2"]
-            activate(c, (0,), banks[0], codes, scales)
-            activate(c, (1,), banks[1], codes, scales)
-            ahead = planes_of_next.get(c, ())
-            gather(c + 1, ahead)
-            activate(c, (2, 3), banks[1 if len(ahead) >= 2 else 2], codes, scales)
-            gather(c + 2, planes_of_next_but_one.get(c, ()))
+            for t, tag in ((2, "a"), (3, "b")):
+                acc = products(c, (t,), "bank%d_%d" % (c % 2, t - 2), codes, scales)
+                y_scalar[c, t] = sbuf([P, width(c)], F32, "y%d_%d" % (c, t), "%s%d" % (tag, c))
+                bias = gelu_of_zeros[:, 0:1] if (c, t) == (0, 2) else 0.0
+                nc.scalar.activation(y_scalar[c, t][:], acc[:, 0, :], GELU, bias=bias)
+            quantised[c] = codes, scales
+            if c < last - 1:
+                activate_vector(c, "bank%d_2" % (c % 2))
 
-        def scatter(c, t):
-            s0, n = span(c)
-            weights = gate_first[:, s0 : s0 + n] if s0 < 2 * C else gate_rest[:, s0 - 2 * C : s0 - 2 * C + n]
-            nc.vector.tensor_tensor(own_out[t][:].indirect(own_offsets(c)), results[c, t], weights, MULT)
-            if c == last:
-                nc.sync.dma_start(out[t * P : (t + 1) * P, :T], own_out[t][:])
+        def apply_gate(c):
+            for t in (2, 3):
+                nc.vector.tensor_tensor(gated[t][:, span(c)], y_scalar[c, t][:], gates[:, span(c)], MULT)
 
-        def far(unit, bank, buffer, queue):
+        own_out = {2: sbuf([P, T], F32, "own_out2")}
+
+        def scatter_scalar(t, slots):
+            nc.scalar.activation(own_out[t][:].indirect(own_offsets(slots)), gated[t][:, slots], COPY)
+
+        def scatter_vector(t, slots):
+            nc.vector.tensor_tensor(
+                own_out[t][:].indirect(own_offsets(slots)), y_vector[:, t, slots], gates[:, slots], MULT
+            )
+
+        def store_own(t, queue):
+            queue.dma_start(out[t * P : (t + 1) * P, :T], own_out[t][:])
+
+        def far(unit, bank, queue):
             g, t = divmod(unit, NT)
             acc = psum.tile([P, SHARE * C], F32, name="far_acc", tag=bank)
             for i in range(SHARE):
                 e = SHARE * g + i
                 multiply(acc[:, i * C : (i + 1) * C], e, t, far_codes[:, e * C : (e + 1) * C], far_scales[e])
-            z = keep.tile([P, SHARE * C], F32, name="z%d" % unit, align_bytes=64, tag=buffer or "z%d" % unit)
-            nc.scalar.activation(z[:], acc[:], GELU)
-            queue.dma_start(out[t * P : (t + 1) * P, T + g * SHARE * C : T + (g + 1) * SHARE * C], z[:])
+            z = far_out[:, unit, :]
+            nc.scalar.activation(z, acc[:], GELU)
+            queue.dma_start(out[t * P : (t + 1) * P, T + g * SHARE * C : T + (g + 1) * SHARE * C], z)
 
-        far_banks = {
-            2: (("bank0_0", None), ("bank0_1", None)),
-            3: (("bank1_0", None), ("bank0_0", "plane2"), ("bank0_1", "plane3")),
-            4: (("spare0", None), ("spare1", None), ("bank0_2", None)),
-        }
-
-        grouped[0] = turns.tile([P, C, PACK], BF16, name="grouped0", align_bytes=64, offset=FIRST_AT)
-        gather(0, (0, 1))
-        for j in (2, 3):
-            nc.vector.tensor_copy(grouped[0][:, :, j], x_f32[j][:].indirect(own_offsets(0)))
-        nc.vector.tensor_copy(x_bf16[3][:, FIRST_HALF], x_f32[3][:, FIRST_HALF])
-        gather(1, (0, 1))
-        gather(2, (0, 1))
-        nc.scalar.copy(x_bf16[3][:, SECOND_HALF], x_f32[3][:, SECOND_HALF])
+        gather(0)
         compute(0)
-        gather_far_bytes(EARLY, E - EARLY, LATE_AT)
+        gather(1)
+        for c in range(last):
+            apply_gate(c)
+            scatter_scalar(2, span(c))
+            compute(c + 1)
+            if c + 2 <= last:
+                gather(c + 2)
+            if c + 2 == last:
+                gather_far_bytes(EARLY, E - EARLY, "b%d" % (last - 3))
 
-        unit = 0
-        for c in range(len(CHUNKS)):
-            scatter(c, 0)
-            scatter(c, 1)
-            if c < last:
-                compute(c + 1)
-            for bank, buffer in far_banks.get(c + 1, ()):
-                far(unit, bank, buffer, nc.scalar if c + 1 == last else nc.sync)
-                unit += 1
-            scatter(c, 2)
-            if c < last - 1:
-                scatter(c, 3)
-        s0 = span(last - 1)[0]
-        nc.vector.tensor_tensor(
-            own_out[3][:].indirect(own_list[:, s0 // PER_COL :]), y_end[:, 1, :], gate_rest[:, s0 - 2 * C :], MULT
-        )
-        nc.sync.dma_start(out[3 * P :, :T], own_out[3][:])
+        thirds = slice(0, 3 * C), slice(3 * C, 6 * C), slice(6 * C, 8 * C)
+        own_out[1] = sbuf([P, T], F32, "own_out1", "b%d" % (last - 1))
+        scatter_vector(1, thirds[0])
+        apply_gate(last)
+        own_out[0] = sbuf([P, T], F32, "own_out0", "a%d" % last)
+        own_out[3] = sbuf([P, T], F32, "own_out3", "b%d" % last)
+        activate_vector(last - 1, "bank0_0")
+        scatter_vector(0, thirds[0])
+        scatter_vector(1, thirds[1])
+        scatter_vector(0, thirds[1])
+
+        far_out = sbuf([P, 2 * NT, SHARE * C], F32, "far_out", "b%d" % (last - 2))
+        far(0, "bank1_0", nc.sync)
+        far(1, "bank1_1", nc.sync)
+        far(2, "bank1_2", nc.sync)
+        far(3, "bank0_2", nc.sync)
+        scatter_scalar(2, span(last))
+        store_own(2, nc.sync)
+        far(4, "spare0", nc.sync)
+        scatter_scalar(3, slice(0, 2 * C))
+        far(5, "spare1", nc.sync)
+        far(6, "bank0_1", nc.sync)
+        activate_vector(last, "bank1_0")
+        for t in (1, 0):
+            scatter_vector(t, thirds[2])
+            store_own(t, nc.sync)
+        scatter_scalar(3, slice(2 * C, 5 * C))
+        far(7, "bank1_1", nc.scalar)
+        scatter_scalar(3, slice(5 * C, 8 * C))
+        store_own(3, nc.scalar)

@@ -155,15 +155,28 @@ def tile_moe_loc_lin_gelu_kernel(
 
         grouped = {}
 
+        picked = {}
+
+        def pair_window(h):
+            return pairs[h][:].rearrange("p t j -> p (t j)").bitcast(U32)
+
+        def grouped_words(c, dtype):
+            grouped[c] = sbuf([P, width(c), PACK], BF16, "grouped%d" % c)
+            return grouped[c][:].rearrange("p s j -> p (s j)").bitcast(dtype).rearrange("p (s h) -> p s h", h=2)
+
+        def gather_first():
+            offsets = own_offsets(span(0))
+            nc.vector.tensor_copy(grouped_words(0, U32)[:, :, 0], pair_window(0).indirect(offsets))
+            for j in range(2):
+                nc.vector.tensor_copy(grouped[0][:, :, 2 + j], x_f32[1][:, j, :].indirect(offsets))
+
         def gather(c):
-            grouped[c] = sbuf([P, width(c), PACK], BF16, "grouped%d" % c, "b%d" % (c - 2))
-            words = grouped[c][:].rearrange("p s j -> p (s j)").bitcast(U32).rearrange("p (s h) -> p s h", h=2)
-            for h in range(2 if c else 1):
-                window = pairs[h][:].rearrange("p t j -> p (t j)").bitcast(U32)
-                nc.vector.tensor_copy(words[:, :, h], window.indirect(own_offsets(span(c))))
-            if c == 0:
-                for j in range(2):
-                    nc.vector.tensor_copy(grouped[c][:, :, 2 + j], x_f32[1][:, j, :].indirect(own_offsets(span(c))))
+            picked[c] = sbuf([P, 2, width(c)], U32, "picked%d" % c, "b%d" % (c - 2))
+            for h in range(2):
+                nc.vector.tensor_copy(picked[c][:, h, :], pair_window(h).indirect(own_offsets(span(c))))
+
+        def weave(c):
+            nc.vector.tensor_copy(grouped_words(c, I32), picked[c][:].bitcast(I32).rearrange("p h s -> p s h"))
 
         y_vector = sbuf([P, 2, E * C], F32, "y_vector")
         gated = {t: sbuf([P, E * C], F32, "gated%d" % t) for t in (2, 3)}
@@ -179,9 +192,9 @@ def tile_moe_loc_lin_gelu_kernel(
 
         quantised = {}
 
-        def activate_vector(c, bank):
-            acc = products(c, (0, 1), bank, *quantised[c])
-            nc.scalar.activation(y_vector[:, :, span(c)], acc[:], GELU)
+        def activate_vector(c, tiles, bank):
+            acc = products(c, tiles, bank, *quantised[c])
+            nc.scalar.activation(y_vector[:, tiles[0] : tiles[-1] + 1, span(c)], acc[:], GELU)
 
         def compute(c):
             codes = sbuf([P, width(c)], U32, "codes%d" % c, "a%d" % (c - 1))
@@ -195,8 +208,8 @@ def tile_moe_loc_lin_gelu_kernel(
                 bias = gelu_of_zeros[:, 0:1] if (c, t) == (0, 2) else 0.0
                 nc.scalar.activation(y_scalar[c, t][:], acc[:, 0, :], GELU, bias=bias)
             quantised[c] = codes, scales
-            if c < last - 1:
-                activate_vector(c, "bank%d_2" % (c % 2))
+            if c < last:
+                activate_vector(c, (0, 1), "bank%d_2" % (c % 2))
 
         def apply_gate(c):
             for t in (2, 3):
@@ -215,55 +228,57 @@ def tile_moe_loc_lin_gelu_kernel(
         def store_own(t, queue):
             queue.dma_start(out[t * P : (t + 1) * P, :T], own_out[t][:])
 
-        def far(unit, bank, queue):
+        def far(unit, bank, queue, z):
             g, t = divmod(unit, NT)
             acc = psum.tile([P, SHARE * C], F32, name="far_acc", tag=bank)
             for i in range(SHARE):
                 e = SHARE * g + i
                 multiply(acc[:, i * C : (i + 1) * C], e, t, far_codes[:, e * C : (e + 1) * C], far_scales[e])
-            z = far_out[:, unit, :]
             nc.scalar.activation(z, acc[:], GELU)
             queue.dma_start(out[t * P : (t + 1) * P, T + g * SHARE * C : T + (g + 1) * SHARE * C], z)
 
-        gather(0)
+        first_far = sbuf([P, SHARE * C], F32, "first_far")
+        gather_first()
         compute(0)
         gather(1)
+        weave(1)
         for c in range(last):
             apply_gate(c)
             scatter_scalar(2, span(c))
             compute(c + 1)
             if c + 2 <= last:
                 gather(c + 2)
-            if c + 2 == last:
-                gather_far_bytes(EARLY, E - EARLY, "b%d" % (last - 3))
+                if c >= 1:
+                    gather_far_bytes(EARLY + 2 * (c - 1), 2, "grouped%d" % (c + 1))
+                weave(c + 2)
+            if c == 0:
+                far(0, "spare0", nc.sync, first_far[:])
 
-        thirds = slice(0, 3 * C), slice(3 * C, 6 * C), slice(6 * C, 8 * C)
+        first_half, second_half = slice(0, HALF), slice(HALF, T)
         own_out[1] = sbuf([P, T], F32, "own_out1", "b%d" % (last - 1))
-        scatter_vector(1, thirds[0])
+        scatter_vector(1, first_half)
         apply_gate(last)
         own_out[0] = sbuf([P, T], F32, "own_out0", "a%d" % last)
         own_out[3] = sbuf([P, T], F32, "own_out3", "b%d" % last)
-        activate_vector(last - 1, "bank0_0")
-        scatter_vector(0, thirds[0])
-        scatter_vector(1, thirds[1])
-        scatter_vector(0, thirds[1])
+        scatter_vector(0, first_half)
 
-        far_out = sbuf([P, 2 * NT, SHARE * C], F32, "far_out", "b%d" % (last - 2))
-        far(0, "bank1_0", nc.sync)
-        far(1, "bank1_1", nc.sync)
-        far(2, "bank1_2", nc.sync)
-        far(3, "bank0_2", nc.sync)
+        far_out = sbuf([P, 2 * NT - 1, SHARE * C], F32, "far_out", "grouped%d" % last)
+        far(1, "bank1_0", nc.sync, far_out[:, 0, :])
+        far(2, "bank1_1", nc.sync, far_out[:, 1, :])
+        far(3, "bank1_2", nc.sync, far_out[:, 2, :])
+        far(4, "bank0_2", nc.sync, far_out[:, 3, :])
+        activate_vector(last, (1,), "bank0_0")
+        scatter_vector(1, second_half)
+        store_own(1, nc.sync)
         scatter_scalar(2, span(last))
         store_own(2, nc.sync)
-        far(4, "spare0", nc.sync)
-        scatter_scalar(3, slice(0, 2 * C))
-        far(5, "spare1", nc.sync)
-        far(6, "bank0_1", nc.sync)
-        activate_vector(last, "bank1_0")
-        for t in (1, 0):
-            scatter_vector(t, thirds[2])
-            store_own(t, nc.sync)
-        scatter_scalar(3, slice(2 * C, 5 * C))
-        far(7, "bank1_1", nc.scalar)
-        scatter_scalar(3, slice(5 * C, 8 * C))
+        far(5, "spare1", nc.sync, far_out[:, 4, :])
+        scatter_scalar(3, slice(0, 3 * C))
+        far(6, "bank0_1", nc.sync, far_out[:, 5, :])
+        activate_vector(last, (0,), "bank1_0")
+        scatter_vector(0, second_half)
+        store_own(0, nc.sync)
+        scatter_scalar(3, slice(3 * C, 6 * C))
+        far(7, "spare0", nc.scalar, far_out[:, 6, :])
+        scatter_scalar(3, slice(6 * C, 8 * C))
         store_own(3, nc.scalar)

@@ -92,8 +92,9 @@ def tile_moe_loc_lin_gelu_kernel(
                 far_bytes[32 * quad : 32 * quad + 4, :].bitcast(I32),
                 x_scales[0, 4 * quad : 4 * quad + 4, :].bitcast(I32),
             )
-        load_x(1, 0)
-        load_x(1, 1)
+        nc.sync.dma_start(x_f32[1][:, 0, :], xo_planes[:, 2, :])
+        for cols in (slice(0, HALF), slice(HALF, T)):
+            nc.sync.dma_start(x_f32[1][:, 1, cols], xo_planes[:, 3, cols])
         load_w_scales(0)
         load_w(0, slice(N // 2, N))
         nc.sync.dma_start(gates[:, : 2 * C], gate[:, : 2 * C])
@@ -153,132 +154,132 @@ def tile_moe_loc_lin_gelu_kernel(
         def own_offsets(slots):
             return own_list[:, slots.start // PER_COL : slots.stop // PER_COL]
 
-        grouped = {}
+        picked = sbuf([P, 3, 2 * C], U32, "picked")
+        grouped = {0: picked[:, 0, :].bitcast(BF16)}
 
-        picked = {}
+        def gather_pairs(dst, c, h):
+            window = pairs[h][:].rearrange("p t j -> p (t j)").bitcast(U32)
+            nc.vector.tensor_copy(dst, window.indirect(own_offsets(span(c))))
 
-        def pair_window(h):
-            return pairs[h][:].rearrange("p t j -> p (t j)").bitcast(U32)
+        def gather_low(c):
+            gather_pairs(picked[:, c % 2, : width(c)], c, 0)
 
-        def grouped_words(c, dtype):
-            grouped[c] = sbuf([P, width(c), PACK], BF16, "grouped%d" % c)
-            return grouped[c][:].rearrange("p s j -> p (s j)").bitcast(dtype).rearrange("p (s h) -> p s h", h=2)
-
-        def gather_first():
-            offsets = own_offsets(span(0))
-            nc.vector.tensor_copy(grouped_words(0, U32)[:, :, 0], pair_window(0).indirect(offsets))
-            for j in range(2):
-                nc.vector.tensor_copy(grouped[0][:, :, 2 + j], x_f32[1][:, j, :].indirect(offsets))
-
-        def gather(c):
-            picked[c] = sbuf([P, 2, width(c)], U32, "picked%d" % c, "b%d" % (c - 2))
-            for h in range(2):
-                nc.vector.tensor_copy(picked[c][:, h, :], pair_window(h).indirect(own_offsets(span(c))))
+        def gather_high(c):
+            gather_pairs(picked[:, 2, : width(c)], c, 1)
 
         def weave(c):
-            nc.vector.tensor_copy(grouped_words(c, I32), picked[c][:].bitcast(I32).rearrange("p h s -> p s h"))
+            tile = sbuf([P, width(c), 2], I32, "grouped%d" % c)
+            rows = picked[:, c % 2 :: 2 - c % 2, : width(c)].bitcast(I32)
+            nc.vector.tensor_copy(tile[:], rows.rearrange("p h s -> p s h"))
+            grouped[c] = tile[:].rearrange("p s h -> p (s h)").bitcast(BF16)
 
-        y_vector = sbuf([P, 2, E * C], F32, "y_vector")
-        gated = {t: sbuf([P, E * C], F32, "gated%d" % t) for t in (2, 3)}
-        y_scalar = {}
+        y = sbuf([P, NT, E * C], F32, "y")
+        quantised = {}
 
-        def products(c, tiles, bank, codes, scales):
+        def quantise(c):
+            codes = sbuf([P, width(c)], U32, "codes%d" % c)
+            scales = sbuf([P, width(c)], U8, "scales%d" % c)
+            nc.vector.quantize_mx(out=codes[:].bitcast(FP8X4), scales=scales[:], in_=grouped[c])
+            quantised[c] = codes, scales
+
+        def activate(c, tiles, bank, bias=0.0):
+            codes, scales = quantised[c]
             acc = psum.tile([P, len(tiles), width(c)], F32, name="own_acc", tag=bank)
             for u, t in enumerate(tiles):
                 for i, e in enumerate(CHUNKS[c]):
                     slots = slice(i * C, (i + 1) * C)
                     multiply(acc[:, u, slots], e, t, codes[:, slots], scales[:, slots])
-            return acc
+            nc.scalar.activation(y[:, tiles[0] : tiles[-1] + 1, span(c)], acc[:], GELU, bias=bias)
 
-        quantised = {}
+        def apply_gate(dst, t, slots):
+            nc.gpsimd.tensor_tensor(dst, y[:, t, slots], gates[:, slots], MULT)
 
-        def activate_vector(c, tiles, bank):
-            acc = products(c, tiles, bank, *quantised[c])
-            nc.scalar.activation(y_vector[:, tiles[0] : tiles[-1] + 1, span(c)], acc[:], GELU)
+        own_out = [sbuf([P, T], F32, "own_out%d" % t) for t in range(NT - 1)] + [None]
 
-        def compute(c):
-            codes = sbuf([P, width(c)], U32, "codes%d" % c, "a%d" % (c - 1))
-            scales = sbuf([P, width(c)], U8, "scales%d" % c)
-            nc.vector.quantize_mx(
-                out=codes[:].bitcast(FP8X4), scales=scales[:], in_=grouped[c][:].rearrange("p s j -> p (s j)")
-            )
-            for t, tag in ((2, "a"), (3, "b")):
-                acc = products(c, (t,), "bank%d_%d" % (c % 2, t - 2), codes, scales)
-                y_scalar[c, t] = sbuf([P, width(c)], F32, "y%d_%d" % (c, t), "%s%d" % (tag, c))
-                bias = gelu_of_zeros[:, 0:1] if (c, t) == (0, 2) else 0.0
-                nc.scalar.activation(y_scalar[c, t][:], acc[:, 0, :], GELU, bias=bias)
-            quantised[c] = codes, scales
-            if c < last:
-                activate_vector(c, (0, 1), "bank%d_2" % (c % 2))
+        def scatter_scalar(t, slots, src):
+            nc.scalar.activation(own_out[t][:].indirect(own_offsets(slots)), src, COPY)
 
-        def apply_gate(c):
-            for t in (2, 3):
-                nc.vector.tensor_tensor(gated[t][:, span(c)], y_scalar[c, t][:], gates[:, span(c)], MULT)
-
-        own_out = {2: sbuf([P, T], F32, "own_out2")}
-
-        def scatter_scalar(t, slots):
-            nc.scalar.activation(own_out[t][:].indirect(own_offsets(slots)), gated[t][:, slots], COPY)
-
-        def scatter_vector(t, slots):
-            nc.vector.tensor_tensor(
-                own_out[t][:].indirect(own_offsets(slots)), y_vector[:, t, slots], gates[:, slots], MULT
-            )
+        def scatter_vector(t, slots, src):
+            nc.vector.tensor_copy(own_out[t][:].indirect(own_offsets(slots)), src)
 
         def store_own(t, queue):
             queue.dma_start(out[t * P : (t + 1) * P, :T], own_out[t][:])
 
-        def far(unit, bank, queue, z):
+        def far(unit, bank, queue):
             g, t = divmod(unit, NT)
             acc = psum.tile([P, SHARE * C], F32, name="far_acc", tag=bank)
             for i in range(SHARE):
                 e = SHARE * g + i
                 multiply(acc[:, i * C : (i + 1) * C], e, t, far_codes[:, e * C : (e + 1) * C], far_scales[e])
-            nc.scalar.activation(z, acc[:], GELU)
-            queue.dma_start(out[t * P : (t + 1) * P, T + g * SHARE * C : T + (g + 1) * SHARE * C], z)
+            z = sbuf([P, SHARE * C], F32, "z%d" % unit)
+            nc.scalar.activation(z[:], acc[:], GELU)
+            queue.dma_start(out[t * P : (t + 1) * P, T + g * SHARE * C : T + (g + 1) * SHARE * C], z[:])
 
-        first_far = sbuf([P, SHARE * C], F32, "first_far")
-        gather_first()
-        compute(0)
-        gather(1)
-        weave(1)
-        for c in range(last):
-            apply_gate(c)
-            scatter_scalar(2, span(c))
-            compute(c + 1)
-            if c + 2 <= last:
-                gather(c + 2)
-                if c >= 1:
-                    gather_far_bytes(EARLY + 2 * (c - 1), 2, "grouped%d" % (c + 1))
-                weave(c + 2)
-            if c == 0:
-                far(0, "spare0", nc.sync, first_far[:])
+        gather_pairs(picked[:, 0, :].rearrange("p (s h) -> p s h", h=2)[:, :, 0], 0, 0)
+        for j in range(2):
+            nc.vector.tensor_copy(
+                grouped[0].rearrange("p (s j) -> p s j", j=PACK)[:, :, 2 + j],
+                x_f32[1][:, j, :].indirect(own_offsets(span(0))),
+            )
+        gather_low(1)
+        quantise(0)
+        for c in range(1, last + 1):
+            gather_high(c)
+            if c < last:
+                gather_low(c + 1)
+            weave(c)
+            quantise(c)
+        gather_far_bytes(EARLY, E - EARLY, "pairs0")
+
+        def gated(t, slots, tag=None, dst=None):
+            if dst is None:
+                dst = sbuf([P, slots.stop - slots.start], F32, "gated%d_%d" % (t, slots.start), tag)[:]
+            apply_gate(dst, t, slots)
+            return dst
 
         first_half, second_half = slice(0, HALF), slice(HALF, T)
-        own_out[1] = sbuf([P, T], F32, "own_out1", "b%d" % (last - 1))
-        scatter_vector(1, first_half)
-        apply_gate(last)
-        own_out[0] = sbuf([P, T], F32, "own_out0", "a%d" % last)
-        own_out[3] = sbuf([P, T], F32, "own_out3", "b%d" % last)
-        scatter_vector(0, first_half)
-
-        far_out = sbuf([P, 2 * NT - 1, SHARE * C], F32, "far_out", "grouped%d" % last)
-        far(1, "bank1_0", nc.sync, far_out[:, 0, :])
-        far(2, "bank1_1", nc.sync, far_out[:, 1, :])
-        far(3, "bank1_2", nc.sync, far_out[:, 2, :])
-        far(4, "bank0_2", nc.sync, far_out[:, 3, :])
-        activate_vector(last, (1,), "bank0_0")
-        scatter_vector(1, second_half)
-        store_own(1, nc.sync)
-        scatter_scalar(2, span(last))
+        activate(0, (2,), "bank0_0", gelu_of_zeros[:, 0:1])
+        activate(0, (3,), "spare1")
+        activate(0, (0, 1), "bank0_1")
+        scatter_scalar(2, span(0), gated(2, span(0)))
+        activate(1, (2, 3), "bank1_0")
+        activate(1, (0, 1), "bank1_1")
+        head_of_3 = gated(3, span(0), "grouped1")
+        far(0, "spare0", nc.sync)
+        scatter_scalar(2, span(1), gated(2, span(1)))
+        activate(2, (2, 3), "bank0_0")
+        activate(2, (0, 1), "bank0_1")
+        half_of_1 = sbuf([P, HALF], F32, "half_of_1", "grouped2")
+        gated(1, slice(0, 2 * C), dst=half_of_1[:, : 2 * C])
+        far(1, "spare1", nc.sync)
+        far(2, "spare2", nc.sync)
+        far(3, "spare3", nc.sync)
+        activate(3, (2, 3), "bank1_0")
+        activate(3, (0, 1), "bank1_1")
+        scatter_scalar(2, span(2), gated(2, span(2), "grouped3"))
+        gated(1, span(2), dst=half_of_1[:, 2 * C :])
+        activate(4, (0, 1), "bank1_0")
+        activate(4, (2, 3), "bank0_0")
+        scatter_scalar(2, span(3), gated(2, span(3), "grouped4"))
+        own_out[3] = sbuf([P, T], F32, "own_out3", "pairs1")
+        scatter_vector(3, span(0), head_of_3)
+        scatter_vector(1, first_half, half_of_1[:])
+        all_of_0 = sbuf([P, T], F32, "all_of_0")
+        gated(0, slice(0, 5 * C), dst=all_of_0[:, : 5 * C])
+        scatter_vector(0, first_half, all_of_0[:, first_half])
+        far(4, "spare0", nc.sync)
+        far(5, "spare1", nc.sync)
+        far(6, "spare2", nc.sync)
+        scatter_scalar(3, slice(C, HALF), gated(3, slice(C, HALF), "codes4"))
+        scatter_scalar(2, span(4), gated(2, span(4)))
         store_own(2, nc.sync)
-        far(5, "spare1", nc.sync, far_out[:, 4, :])
-        scatter_scalar(3, slice(0, 3 * C))
-        far(6, "bank0_1", nc.sync, far_out[:, 5, :])
-        activate_vector(last, (0,), "bank1_0")
-        scatter_vector(0, second_half)
+        scatter_vector(1, second_half, gated(1, second_half))
+        store_own(1, nc.sync)
+        end_of_3 = gated(3, second_half)
+        gated(0, slice(5 * C, T), dst=all_of_0[:, 5 * C :])
+        scatter_vector(0, second_half, all_of_0[:, second_half])
         store_own(0, nc.sync)
-        scatter_scalar(3, slice(3 * C, 6 * C))
-        far(7, "spare0", nc.scalar, far_out[:, 6, :])
-        scatter_scalar(3, slice(6 * C, 8 * C))
+        scatter_scalar(3, span(3), end_of_3[:, : 2 * C])
+        far(7, "spare3", nc.scalar)
+        scatter_scalar(3, span(4), end_of_3[:, 2 * C :])
         store_own(3, nc.scalar)

@@ -26,6 +26,7 @@ HALF = T // 2
 
 CHUNKS = ((0,), (1,), (2, 3), (4, 5), (6, 7))
 EARLY = 4
+REGION = C + HALF * 4
 ON_SCALAR = 256
 
 
@@ -35,10 +36,14 @@ def tile_moe_loc_lin_gelu_kernel(
     nc = tc.nc
     with ExitStack() as ctx:
         keep = ctx.enter_context(tc.tile_pool(name="keep", bufs=1))
+        turns = ctx.enter_context(tc.tile_pool(name="turns", bufs=1))
         psum = ctx.enter_context(tc.psum_pool(name="psum", bufs=1))
 
         def sbuf(shape, dtype, name, tag=None):
             return keep.tile(shape, dtype, name=name, align_bytes=64, tag=tag or name)
+
+        def taking_turns(shape, dtype, name, c, at):
+            return turns.tile(shape, dtype, name=name, align_bytes=64, offset=(c - 1) * REGION + at)
 
         own_list = keep.tile([P, E * C // PER_COL], U16, name="own_list")
         far_list = keep.tile([P, E * C // PER_COL], U16, name="far_list")
@@ -101,10 +106,10 @@ def tile_moe_loc_lin_gelu_kernel(
         load_w(0, slice(0, N // 2))
         load_w(1, slice(0, N))
         load_w(2, slice(0, N))
-        nc.sync.dma_start(gates[:, 2 * C :], gate[:, 2 * C :])
         load_w_scales(1)
         load_w(3, slice(0, N))
         load_w(4, slice(0, N))
+        nc.sync.dma_start(gates[:, 2 * C :], gate[:, 2 * C :])
 
         def multiply(acc, e, t, codes, scales):
             cols = slice(t * P, (t + 1) * P)
@@ -127,14 +132,13 @@ def tile_moe_loc_lin_gelu_kernel(
                 offsets = far_list[:, (first + i0) * C // PER_COL : (first + i1) * C // PER_COL]
                 nc.vector.tensor_copy(dst[:, i0 * C : i1 * C], window.indirect(offsets))
 
-        def gather_far_bytes(first, count, tag):
-            tile = sbuf([P, count * C], U8, "far_scales%d" % first, tag)
+        def gather_far_bytes(first, count, tile):
             gather_far(tile, far_bytes[:], first, count)
             for i in range(count):
                 far_scales[first + i] = tile[:, i * C : (i + 1) * C]
 
         gather_far(far_codes, far_words[:].bitcast(U32), 0, E)
-        gather_far_bytes(0, EARLY, None)
+        gather_far_bytes(0, EARLY, sbuf([P, EARLY * C], U8, "far_scales"))
 
         for h in range(2):
             for s in range(2):
@@ -168,7 +172,7 @@ def tile_moe_loc_lin_gelu_kernel(
             gather_pairs(picked[:, 2, : width(c)], c, 1)
 
         def weave(c):
-            tile = sbuf([P, width(c), 2], I32, "grouped%d" % c)
+            tile = taking_turns([P, width(c), 2], I32, "grouped%d" % c, c, 0)
             rows = picked[:, c % 2 :: 2 - c % 2, : width(c)].bitcast(I32)
             nc.vector.tensor_copy(tile[:], rows.rearrange("p h s -> p s h"))
             grouped[c] = tile[:].rearrange("p s h -> p (s h)").bitcast(BF16)
@@ -205,15 +209,19 @@ def tile_moe_loc_lin_gelu_kernel(
         def store_own(t, queue):
             queue.dma_start(out[t * P : (t + 1) * P, :T], own_out[t][:])
 
+        out_tiles = out.rearrange("(t p) c -> p t c", p=P)
+
         def far(unit, bank, queue):
-            g, t = divmod(unit, NT)
-            acc = psum.tile([P, SHARE * C], F32, name="far_acc", tag=bank)
-            for i in range(SHARE):
-                e = SHARE * g + i
-                multiply(acc[:, i * C : (i + 1) * C], e, t, far_codes[:, e * C : (e + 1) * C], far_scales[e])
-            z = sbuf([P, SHARE * C], F32, "z%d" % unit)
+            g, h = divmod(unit, 2)
+            acc = psum.tile([P, 2, 2 * C], F32, name="far_acc", tag=bank)
+            for u in range(2):
+                for i in range(2):
+                    e = 2 * g + i
+                    codes = far_codes[:, e * C : (e + 1) * C]
+                    multiply(acc[:, u, i * C : (i + 1) * C], e, 2 * h + u, codes, far_scales[e])
+            z = sbuf([P, 2, 2 * C], F32, "z%d" % unit)
             nc.scalar.activation(z[:], acc[:], GELU)
-            queue.dma_start(out[t * P : (t + 1) * P, T + g * SHARE * C : T + (g + 1) * SHARE * C], z[:])
+            queue.dma_start(out_tiles[:, 2 * h : 2 * h + 2, T + 2 * g * C : T + 2 * (g + 1) * C], z[:])
 
         gather_pairs(picked[:, 0, :].rearrange("p (s h) -> p s h", h=2)[:, :, 0], 0, 0)
         for j in range(2):
@@ -228,58 +236,57 @@ def tile_moe_loc_lin_gelu_kernel(
             if c < last:
                 gather_low(c + 1)
             weave(c)
+            if c > 1:
+                e = EARLY + c - 2
+                gather_far_bytes(e, 1, taking_turns([P, C], U8, "far_scales%d" % e, c - 1, 0))
             quantise(c)
-        gather_far_bytes(EARLY, E - EARLY, "pairs0")
+        gather_far_bytes(E - 1, 1, sbuf([P, C], U8, "far_scales_last", "pairs0"))
 
-        def gated(t, slots, tag=None, dst=None):
-            if dst is None:
-                dst = sbuf([P, slots.stop - slots.start], F32, "gated%d_%d" % (t, slots.start), tag)[:]
-            apply_gate(dst, t, slots)
-            return dst
+        def gated(t, slots, after=None):
+            shape, name = [P, slots.stop - slots.start], "gated%d_%d" % (t, slots.start)
+            dst = sbuf(shape, F32, name) if after is None else taking_turns(shape, F32, name, after, C)
+            apply_gate(dst[:], t, slots)
+            return dst[:]
 
         first_half, second_half = slice(0, HALF), slice(HALF, T)
+        head, middle, end = slice(0, 2 * C), slice(2 * C, 5 * C), slice(5 * C, T)
         activate(0, (2,), "bank0_0", gelu_of_zeros[:, 0:1])
         activate(0, (3,), "spare1")
         activate(0, (0, 1), "bank0_1")
         scatter_scalar(2, span(0), gated(2, span(0)))
         activate(1, (2, 3), "bank1_0")
         activate(1, (0, 1), "bank1_1")
-        head_of_3 = gated(3, span(0), "grouped1")
         far(0, "spare0", nc.sync)
         scatter_scalar(2, span(1), gated(2, span(1)))
-        activate(2, (2, 3), "bank0_0")
+        head_of_3 = gated(3, head, 2)
         activate(2, (0, 1), "bank0_1")
-        half_of_1 = sbuf([P, HALF], F32, "half_of_1", "grouped2")
-        gated(1, slice(0, 2 * C), dst=half_of_1[:, : 2 * C])
+        activate(2, (2, 3), "bank0_0")
+        half_of_1 = gated(1, first_half, 3)
         far(1, "spare1", nc.sync)
         far(2, "spare2", nc.sync)
         far(3, "spare3", nc.sync)
         activate(3, (2, 3), "bank1_0")
         activate(3, (0, 1), "bank1_1")
-        scatter_scalar(2, span(2), gated(2, span(2), "grouped3"))
-        gated(1, span(2), dst=half_of_1[:, 2 * C :])
-        activate(4, (0, 1), "bank1_0")
-        activate(4, (2, 3), "bank0_0")
-        scatter_scalar(2, span(3), gated(2, span(3), "grouped4"))
-        own_out[3] = sbuf([P, T], F32, "own_out3", "pairs1")
-        scatter_vector(3, span(0), head_of_3)
-        scatter_vector(1, first_half, half_of_1[:])
-        all_of_0 = sbuf([P, T], F32, "all_of_0")
-        gated(0, slice(0, 5 * C), dst=all_of_0[:, : 5 * C])
-        scatter_vector(0, first_half, all_of_0[:, first_half])
         far(4, "spare0", nc.sync)
         far(5, "spare1", nc.sync)
         far(6, "spare2", nc.sync)
-        scatter_scalar(3, slice(C, HALF), gated(3, slice(C, HALF), "codes4"))
-        scatter_scalar(2, span(4), gated(2, span(4)))
-        store_own(2, nc.sync)
+        scatter_scalar(2, middle, gated(2, middle, 4))
+        own_out[3] = sbuf([P, T], F32, "own_out3", "picked")
+        scatter_vector(3, head, head_of_3)
+        scatter_vector(1, first_half, half_of_1)
+        all_of_0 = sbuf([P, T], F32, "all_of_0")
+        apply_gate(all_of_0[:, : end.start], 0, slice(0, end.start))
+        scatter_vector(0, first_half, all_of_0[:, first_half])
+        far(7, "spare3", nc.sync)
+        activate(4, (0, 1), "bank0_1")
+        activate(4, (2, 3), "bank0_0")
+        scatter_scalar(3, middle, gated(3, middle))
         scatter_vector(1, second_half, gated(1, second_half))
         store_own(1, nc.sync)
-        end_of_3 = gated(3, second_half)
-        gated(0, slice(5 * C, T), dst=all_of_0[:, 5 * C :])
+        scatter_scalar(2, end, gated(2, end))
+        store_own(2, nc.scalar)
+        scatter_scalar(3, end, gated(3, end))
+        store_own(3, nc.scalar)
+        apply_gate(all_of_0[:, end], 0, end)
         scatter_vector(0, second_half, all_of_0[:, second_half])
         store_own(0, nc.sync)
-        scatter_scalar(3, span(3), end_of_3[:, : 2 * C])
-        far(7, "spare3", nc.scalar)
-        scatter_scalar(3, span(4), end_of_3[:, 2 * C :])
-        store_own(3, nc.scalar)

@@ -27,6 +27,8 @@ HALF = T // 2
 CHUNKS = ((0,), (1,), (2, 3), (4, 5), (6, 7))
 EARLY = 4
 REGION = C + HALF * 4
+BETWEEN = 4 * REGION + T * 4
+LAST_ON_SCALAR = 384
 ON_SCALAR = 256
 
 
@@ -144,8 +146,9 @@ def tile_moe_loc_lin_gelu_kernel(
             for s in range(2):
                 src = x_f32[h][:, :, s * HALF : (s + 1) * HALF].rearrange("p j t -> p t j")
                 dst = pairs[h][:, s * HALF : (s + 1) * HALF, :]
-                nc.scalar.copy(dst[:, :ON_SCALAR, :], src[:, :ON_SCALAR, :])
-                nc.gpsimd.tensor_scalar(dst[:, ON_SCALAR:, :], src[:, ON_SCALAR:, :], 1.0, 0.0, MULT, ADD)
+                n = LAST_ON_SCALAR if (h, s) == (1, 1) else ON_SCALAR
+                nc.scalar.copy(dst[:, :n, :], src[:, :n, :])
+                nc.gpsimd.tensor_scalar(dst[:, n:, :], src[:, n:, :], 1.0, 0.0, MULT, ADD)
 
         last = len(CHUNKS) - 1
 
@@ -158,22 +161,23 @@ def tile_moe_loc_lin_gelu_kernel(
         def own_offsets(slots):
             return own_list[:, slots.start // PER_COL : slots.stop // PER_COL]
 
-        picked = sbuf([P, 3, 2 * C], U32, "picked")
-        grouped = {0: picked[:, 0, :].bitcast(BF16)}
+        first = turns.tile([P, C, PACK], BF16, name="grouped0", align_bytes=64, offset=BETWEEN - 64)
+        grouped = {0: first[:].rearrange("p s j -> p (s j)")}
+        picked = {1: sbuf([P, 2, 2 * C], U32, "picked_odd")}
 
         def gather_pairs(dst, c, h):
             window = pairs[h][:].rearrange("p t j -> p (t j)").bitcast(U32)
             nc.vector.tensor_copy(dst, window.indirect(own_offsets(span(c))))
 
         def gather_low(c):
-            gather_pairs(picked[:, c % 2, : width(c)], c, 0)
+            gather_pairs(picked[c % 2][:, 0, : width(c)], c, 0)
 
         def gather_high(c):
-            gather_pairs(picked[:, 2, : width(c)], c, 1)
+            gather_pairs(picked[c % 2][:, 1, : width(c)], c, 1)
 
         def weave(c):
             tile = taking_turns([P, width(c), 2], I32, "grouped%d" % c, c, 0)
-            rows = picked[:, c % 2 :: 2 - c % 2, : width(c)].bitcast(I32)
+            rows = picked[c % 2][:, :, : width(c)].bitcast(I32)
             nc.vector.tensor_copy(tile[:], rows.rearrange("p h s -> p s h"))
             grouped[c] = tile[:].rearrange("p s h -> p (s h)").bitcast(BF16)
 
@@ -198,7 +202,7 @@ def tile_moe_loc_lin_gelu_kernel(
         def apply_gate(dst, t, slots):
             nc.gpsimd.tensor_tensor(dst, y[:, t, slots], gates[:, slots], MULT)
 
-        own_out = [sbuf([P, T], F32, "own_out%d" % t) for t in range(NT - 1)] + [None]
+        own_out = [sbuf([P, T], F32, "own_out%d" % t) if t % 2 == 0 else None for t in range(NT)]
 
         def scatter_scalar(t, slots, src):
             nc.scalar.activation(own_out[t][:].indirect(own_offsets(slots)), src, COPY)
@@ -223,14 +227,15 @@ def tile_moe_loc_lin_gelu_kernel(
             nc.scalar.activation(z[:], acc[:], GELU)
             queue.dma_start(out_tiles[:, 2 * h : 2 * h + 2, T + 2 * g * C : T + 2 * (g + 1) * C], z[:])
 
-        gather_pairs(picked[:, 0, :].rearrange("p (s h) -> p s h", h=2)[:, :, 0], 0, 0)
+        gather_pairs(grouped[0].bitcast(U32).rearrange("p (s h) -> p s h", h=2)[:, :, 0], 0, 0)
         for j in range(2):
             nc.vector.tensor_copy(
-                grouped[0].rearrange("p (s j) -> p s j", j=PACK)[:, :, 2 + j],
+                first[:, :, 2 + j],
                 x_f32[1][:, j, :].indirect(own_offsets(span(0))),
             )
         gather_low(1)
         quantise(0)
+        picked[0] = turns.tile([P, 2, 2 * C], U32, name="picked_even", align_bytes=64, offset=BETWEEN - 64)
         for c in range(1, last + 1):
             gather_high(c)
             if c < last:
@@ -242,9 +247,9 @@ def tile_moe_loc_lin_gelu_kernel(
             quantise(c)
         gather_far_bytes(E - 1, 1, sbuf([P, C], U8, "far_scales_last", "pairs0"))
 
-        def gated(t, slots, after=None):
+        def gated(t, slots, after=None, at=C):
             shape, name = [P, slots.stop - slots.start], "gated%d_%d" % (t, slots.start)
-            dst = sbuf(shape, F32, name) if after is None else taking_turns(shape, F32, name, after, C)
+            dst = sbuf(shape, F32, name) if after is None else taking_turns(shape, F32, name, after, at)
             apply_gate(dst[:], t, slots)
             return dst[:]
 
@@ -254,15 +259,16 @@ def tile_moe_loc_lin_gelu_kernel(
         activate(0, (3,), "spare1")
         activate(0, (0, 1), "bank0_1")
         scatter_scalar(2, span(0), gated(2, span(0)))
+        far(0, "spare0", nc.sync)
         activate(1, (2, 3), "bank1_0")
         activate(1, (0, 1), "bank1_1")
-        far(0, "spare0", nc.sync)
+        far(1, "spare1", nc.sync)
         scatter_scalar(2, span(1), gated(2, span(1)))
-        head_of_3 = gated(3, head, 2)
+        head_of_1 = gated(1, head, 2)
+        head_of_3 = gated(3, head, 2, C + 2 * C * 4)
         activate(2, (0, 1), "bank0_1")
         activate(2, (2, 3), "bank0_0")
-        half_of_1 = gated(1, first_half, 3)
-        far(1, "spare1", nc.sync)
+        next_of_1 = gated(1, span(2), 3)
         far(2, "spare2", nc.sync)
         far(3, "spare3", nc.sync)
         activate(3, (2, 3), "bank1_0")
@@ -270,21 +276,23 @@ def tile_moe_loc_lin_gelu_kernel(
         far(4, "spare0", nc.sync)
         far(5, "spare1", nc.sync)
         far(6, "spare2", nc.sync)
-        scatter_scalar(2, middle, gated(2, middle, 4))
-        own_out[3] = sbuf([P, T], F32, "own_out3", "picked")
-        scatter_vector(3, head, head_of_3)
-        scatter_vector(1, first_half, half_of_1)
-        all_of_0 = sbuf([P, T], F32, "all_of_0")
-        apply_gate(all_of_0[:, : end.start], 0, slice(0, end.start))
-        scatter_vector(0, first_half, all_of_0[:, first_half])
         far(7, "spare3", nc.sync)
         activate(4, (0, 1), "bank0_1")
         activate(4, (2, 3), "bank0_0")
+        scatter_scalar(2, middle, gated(2, middle, 4))
+        own_out[1] = turns.tile([P, T], F32, name="own_out1", align_bytes=64, offset=BETWEEN - T * 4)
+        own_out[3] = turns.tile([P, T], F32, name="own_out3", align_bytes=64, offset=BETWEEN)
+        scatter_vector(1, head, head_of_1)
+        scatter_vector(3, head, head_of_3)
+        scatter_vector(1, span(2), next_of_1)
+        all_of_0 = sbuf([P, T], F32, "all_of_0")
+        apply_gate(all_of_0[:, : end.start], 0, slice(0, end.start))
+        scatter_vector(0, first_half, all_of_0[:, first_half])
         scatter_scalar(3, middle, gated(3, middle))
         scatter_vector(1, second_half, gated(1, second_half))
         store_own(1, nc.sync)
         scatter_scalar(2, end, gated(2, end))
-        store_own(2, nc.scalar)
+        store_own(2, nc.sync)
         scatter_scalar(3, end, gated(3, end))
         store_own(3, nc.scalar)
         apply_gate(all_of_0[:, end], 0, end)

@@ -27,7 +27,9 @@ HALF = T // 2
 CHUNKS = ((0,), (1,), (2, 3), (4, 5), (6, 7))
 EARLY = 4
 REGION = C + HALF * 4
-BETWEEN = 4 * REGION + T * 4
+BETWEEN = 5 * REGION + T * 4
+ROW_OF = {2: 0, 3: 1, 0: 2, 1: 3}
+CUT = HALF + 32
 LAST_ON_SCALAR = 384
 ON_SCALAR = 256
 
@@ -197,10 +199,11 @@ def tile_moe_loc_lin_gelu_kernel(
                 for i, e in enumerate(CHUNKS[c]):
                     slots = slice(i * C, (i + 1) * C)
                     multiply(acc[:, u, slots], e, t, codes[:, slots], scales[:, slots])
-            nc.scalar.activation(y[:, tiles[0] : tiles[-1] + 1, span(c)], acc[:], GELU, bias=bias)
+            row = ROW_OF[tiles[0]]
+            nc.scalar.activation(y[:, row : row + len(tiles), span(c)], acc[:], GELU, bias=bias)
 
         def apply_gate(dst, t, slots):
-            nc.gpsimd.tensor_tensor(dst, y[:, t, slots], gates[:, slots], MULT)
+            nc.gpsimd.tensor_tensor(dst, y[:, ROW_OF[t], slots], gates[:, slots], MULT)
 
         own_out = [sbuf([P, T], F32, "own_out%d" % t) if t % 2 == 0 else None for t in range(NT)]
 
@@ -256,20 +259,17 @@ def tile_moe_loc_lin_gelu_kernel(
         first_half, second_half = slice(0, HALF), slice(HALF, T)
         head, middle, end = slice(0, 2 * C), slice(2 * C, 5 * C), slice(5 * C, T)
         activate(0, (2,), "bank0_0", gelu_of_zeros[:, 0:1])
-        activate(0, (3,), "spare1")
-        activate(0, (0, 1), "bank0_1")
+        activate(0, (3, 0, 1), "bank0_1")
         scatter_scalar(2, span(0), gated(2, span(0)))
         far(0, "spare0", nc.sync)
-        activate(1, (2, 3), "bank1_0")
-        activate(1, (0, 1), "bank1_1")
+        activate(1, (2, 3, 0, 1), "bank1_0")
         far(1, "spare1", nc.sync)
-        scatter_scalar(2, span(1), gated(2, span(1)))
-        head_of_1 = gated(1, head, 2)
-        head_of_3 = gated(3, head, 2, C + 2 * C * 4)
+        far(2, "spare2", nc.sync)
+        scatter_scalar(2, span(1), gated(2, span(1), 2))
+        head_of_1 = gated(1, head, 2, C + C * 4)
         activate(2, (0, 1), "bank0_1")
         activate(2, (2, 3), "bank0_0")
         next_of_1 = gated(1, span(2), 3)
-        far(2, "spare2", nc.sync)
         far(3, "spare3", nc.sync)
         activate(3, (2, 3), "bank1_0")
         activate(3, (0, 1), "bank1_1")
@@ -279,14 +279,15 @@ def tile_moe_loc_lin_gelu_kernel(
         far(7, "spare3", nc.sync)
         activate(4, (0, 1), "bank0_1")
         activate(4, (2, 3), "bank0_0")
-        scatter_scalar(2, middle, gated(2, middle, 4))
+        head_of_3 = gated(3, head, 4, 0)
+        scatter_scalar(2, middle, gated(2, middle, 4, 2 * C * 4))
         own_out[1] = turns.tile([P, T], F32, name="own_out1", align_bytes=64, offset=BETWEEN - T * 4)
         own_out[3] = turns.tile([P, T], F32, name="own_out3", align_bytes=64, offset=BETWEEN)
         scatter_vector(1, head, head_of_1)
         scatter_vector(3, head, head_of_3)
         scatter_vector(1, span(2), next_of_1)
         all_of_0 = sbuf([P, T], F32, "all_of_0")
-        apply_gate(all_of_0[:, : end.start], 0, slice(0, end.start))
+        apply_gate(all_of_0[:, :CUT], 0, slice(0, CUT))
         scatter_vector(0, first_half, all_of_0[:, first_half])
         scatter_scalar(3, middle, gated(3, middle))
         scatter_vector(1, second_half, gated(1, second_half))
@@ -295,6 +296,6 @@ def tile_moe_loc_lin_gelu_kernel(
         store_own(2, nc.sync)
         scatter_scalar(3, end, gated(3, end))
         store_own(3, nc.scalar)
-        apply_gate(all_of_0[:, end], 0, end)
+        apply_gate(all_of_0[:, CUT:], 0, slice(CUT, T))
         scatter_vector(0, second_half, all_of_0[:, second_half])
         store_own(0, nc.sync)

@@ -23,15 +23,17 @@ NT = N // P
 PER_COL = 16
 SHARE = 4
 HALF = T // 2
+WORD = 4
 
 CHUNKS = ((0,), (1,), (2, 3), (4, 5), (6, 7))
 EARLY = 4
-REGION = C + HALF * 4
-BETWEEN = 5 * REGION + T * 4
+ROUNDED_BY_SCALAR, LAST_ROUNDED_BY_SCALAR = 256, 384
+TILE_3_ON_VECTOR = 320
+FIRST_OF_TILE_0 = HALF + 2 * PER_COL
 ROW_OF = {2: 0, 3: 1, 0: 2, 1: 3}
-CUT = HALF + 32
-LAST_ON_SCALAR = 384
-ON_SCALAR = 256
+REGION = C + HALF * WORD
+SEAM = 4 * REGION + T * WORD
+ACROSS_SEAM = SEAM - 64
 
 
 def tile_moe_loc_lin_gelu_kernel(
@@ -46,8 +48,11 @@ def tile_moe_loc_lin_gelu_kernel(
         def sbuf(shape, dtype, name, tag=None):
             return keep.tile(shape, dtype, name=name, align_bytes=64, tag=tag or name)
 
-        def taking_turns(shape, dtype, name, c, at):
-            return turns.tile(shape, dtype, name=name, align_bytes=64, offset=(c - 1) * REGION + at)
+        def placed(shape, dtype, name, offset):
+            return turns.tile(shape, dtype, name=name, align_bytes=64, offset=offset)
+
+        def region(c):
+            return (c - 1) * REGION
 
         own_list = keep.tile([P, E * C // PER_COL], U16, name="own_list")
         far_list = keep.tile([P, E * C // PER_COL], U16, name="far_list")
@@ -86,23 +91,19 @@ def tile_moe_loc_lin_gelu_kernel(
             nc.sync.dma_start(w_chunks[c][:, :, cols], src[:, :, cols])
 
         xo_planes = xo.rearrange("(p j) t -> p j t", j=PACK)
-
-        def load_x(h, s):
-            cols = slice(s * HALF, (s + 1) * HALF)
-            nc.sync.dma_start(x_f32[h][:, :, cols], xo_planes[:, 2 * h : 2 * h + 2, cols])
-
+        first_half, second_half = slice(0, HALF), slice(HALF, T)
         nc.sync.dma_start(far_words[:], x_words[0].rearrange("p t d -> p (t d)").bitcast(I32))
         nc.sync.dma_start(far_list[:], offs2)
-        load_x(0, 0)
+        nc.sync.dma_start(x_f32[0][:, :, first_half], xo_planes[:, 0:2, first_half])
         nc.sync.dma_start(own_list[:], offs)
-        load_x(0, 1)
+        nc.sync.dma_start(x_f32[0][:, :, second_half], xo_planes[:, 0:2, second_half])
         for quad in range(4):
             nc.sync.dma_start(
                 far_bytes[32 * quad : 32 * quad + 4, :].bitcast(I32),
                 x_scales[0, 4 * quad : 4 * quad + 4, :].bitcast(I32),
             )
         nc.sync.dma_start(x_f32[1][:, 0, :], xo_planes[:, 2, :])
-        for cols in (slice(0, HALF), slice(HALF, T)):
+        for cols in (first_half, second_half):
             nc.sync.dma_start(x_f32[1][:, 1, cols], xo_planes[:, 3, cols])
         load_w_scales(0)
         load_w(0, slice(N // 2, N))
@@ -145,10 +146,10 @@ def tile_moe_loc_lin_gelu_kernel(
         gather_far_bytes(0, EARLY, sbuf([P, EARLY * C], U8, "far_scales"))
 
         for h in range(2):
-            for s in range(2):
-                src = x_f32[h][:, :, s * HALF : (s + 1) * HALF].rearrange("p j t -> p t j")
-                dst = pairs[h][:, s * HALF : (s + 1) * HALF, :]
-                n = LAST_ON_SCALAR if (h, s) == (1, 1) else ON_SCALAR
+            for cols in (first_half, second_half):
+                src = x_f32[h][:, :, cols].rearrange("p j t -> p t j")
+                dst = pairs[h][:, cols, :]
+                n = LAST_ROUNDED_BY_SCALAR if (h, cols) == (1, second_half) else ROUNDED_BY_SCALAR
                 nc.scalar.copy(dst[:, :n, :], src[:, :n, :])
                 nc.gpsimd.tensor_scalar(dst[:, n:, :], src[:, n:, :], 1.0, 0.0, MULT, ADD)
 
@@ -163,22 +164,19 @@ def tile_moe_loc_lin_gelu_kernel(
         def own_offsets(slots):
             return own_list[:, slots.start // PER_COL : slots.stop // PER_COL]
 
-        first = turns.tile([P, C, PACK], BF16, name="grouped0", align_bytes=64, offset=BETWEEN - 64)
-        grouped = {0: first[:].rearrange("p s j -> p (s j)")}
+        grouped_0 = placed([P, C, PACK], BF16, "grouped0", ACROSS_SEAM)
+        grouped = {0: grouped_0[:].rearrange("p s j -> p (s j)")}
         picked = {1: sbuf([P, 2, 2 * C], U32, "picked_odd")}
 
-        def gather_pairs(dst, c, h):
+        def gather_words(dst, c, h):
             window = pairs[h][:].rearrange("p t j -> p (t j)").bitcast(U32)
             nc.vector.tensor_copy(dst, window.indirect(own_offsets(span(c))))
 
-        def gather_low(c):
-            gather_pairs(picked[c % 2][:, 0, : width(c)], c, 0)
-
-        def gather_high(c):
-            gather_pairs(picked[c % 2][:, 1, : width(c)], c, 1)
+        def gather_pair(c, h):
+            gather_words(picked[c % 2][:, h, : width(c)], c, h)
 
         def weave(c):
-            tile = taking_turns([P, width(c), 2], I32, "grouped%d" % c, c, 0)
+            tile = placed([P, width(c), 2], I32, "grouped%d" % c, region(c))
             rows = picked[c % 2][:, :, : width(c)].bitcast(I32)
             nc.vector.tensor_copy(tile[:], rows.rearrange("p h s -> p s h"))
             grouped[c] = tile[:].rearrange("p s h -> p (s h)").bitcast(BF16)
@@ -205,7 +203,7 @@ def tile_moe_loc_lin_gelu_kernel(
         def apply_gate(dst, t, slots):
             nc.gpsimd.tensor_tensor(dst, y[:, ROW_OF[t], slots], gates[:, slots], MULT)
 
-        own_out = [sbuf([P, T], F32, "own_out%d" % t) if t % 2 == 0 else None for t in range(NT)]
+        own_out = {t: sbuf([P, T], F32, "own_out%d" % t) for t in (0, 2)}
 
         def scatter_scalar(t, slots, src):
             nc.scalar.activation(own_out[t][:].indirect(own_offsets(slots)), src, COPY)
@@ -218,9 +216,9 @@ def tile_moe_loc_lin_gelu_kernel(
 
         out_tiles = out.rearrange("(t p) c -> p t c", p=P)
 
-        def far(unit, bank, queue):
+        def far(unit):
             g, h = divmod(unit, 2)
-            acc = psum.tile([P, 2, 2 * C], F32, name="far_acc", tag=bank)
+            acc = psum.tile([P, 2, 2 * C], F32, name="far_acc", tag="far%d" % (unit % 4))
             for u in range(2):
                 for i in range(2):
                     e = 2 * g + i
@@ -228,74 +226,71 @@ def tile_moe_loc_lin_gelu_kernel(
                     multiply(acc[:, u, i * C : (i + 1) * C], e, 2 * h + u, codes, far_scales[e])
             z = sbuf([P, 2, 2 * C], F32, "z%d" % unit)
             nc.scalar.activation(z[:], acc[:], GELU)
-            queue.dma_start(out_tiles[:, 2 * h : 2 * h + 2, T + 2 * g * C : T + 2 * (g + 1) * C], z[:])
+            nc.sync.dma_start(out_tiles[:, 2 * h : 2 * h + 2, T + 2 * g * C : T + 2 * (g + 1) * C], z[:])
 
-        gather_pairs(grouped[0].bitcast(U32).rearrange("p (s h) -> p s h", h=2)[:, :, 0], 0, 0)
+        gather_words(grouped[0].bitcast(U32).rearrange("p (s h) -> p s h", h=2)[:, :, 0], 0, 0)
         for j in range(2):
-            nc.vector.tensor_copy(
-                first[:, :, 2 + j],
-                x_f32[1][:, j, :].indirect(own_offsets(span(0))),
-            )
-        gather_low(1)
+            nc.vector.tensor_copy(grouped_0[:, :, 2 + j], x_f32[1][:, j, :].indirect(own_offsets(span(0))))
+        gather_pair(1, 0)
         quantise(0)
-        picked[0] = turns.tile([P, 2, 2 * C], U32, name="picked_even", align_bytes=64, offset=BETWEEN - 64)
+        picked[0] = placed([P, 2, 2 * C], U32, "picked_even", ACROSS_SEAM)
         for c in range(1, last + 1):
-            gather_high(c)
+            gather_pair(c, 1)
             if c < last:
-                gather_low(c + 1)
+                gather_pair(c + 1, 0)
             weave(c)
             if c > 1:
                 e = EARLY + c - 2
-                gather_far_bytes(e, 1, taking_turns([P, C], U8, "far_scales%d" % e, c - 1, 0))
+                gather_far_bytes(e, 1, placed([P, C], U8, "far_scales%d" % e, region(c - 1)))
             quantise(c)
         gather_far_bytes(E - 1, 1, sbuf([P, C], U8, "far_scales_last", "pairs0"))
 
-        def gated(t, slots, after=None, at=C):
+        def gated(t, slots, offset=None):
             shape, name = [P, slots.stop - slots.start], "gated%d_%d" % (t, slots.start)
-            dst = sbuf(shape, F32, name) if after is None else taking_turns(shape, F32, name, after, at)
+            dst = sbuf(shape, F32, name) if offset is None else placed(shape, F32, name, offset)
             apply_gate(dst[:], t, slots)
             return dst[:]
 
-        first_half, second_half = slice(0, HALF), slice(HALF, T)
-        head, middle, end = slice(0, 2 * C), slice(2 * C, 5 * C), slice(5 * C, T)
-        activate(0, (2,), "bank0_0", gelu_of_zeros[:, 0:1])
-        activate(0, (3, 0, 1), "bank0_1")
+        small_chunks = slice(0, 2 * C)
+        middle_of_2, end_of_2 = slice(2 * C, 5 * C), slice(5 * C, T)
+        halfway = (TILE_3_ON_VECTOR + T) // 2
+        start_of_3, middle_of_3, end_of_3 = slice(0, TILE_3_ON_VECTOR), slice(TILE_3_ON_VECTOR, halfway), slice(halfway, T)
+        rest_of_1 = slice(2 * C, T)
+
+        activate(0, (2,), "even0", gelu_of_zeros[:, 0:1])
+        activate(0, (3, 0, 1), "even1")
         scatter_scalar(2, span(0), gated(2, span(0)))
-        far(0, "spare0", nc.sync)
-        activate(1, (2, 3, 0, 1), "bank1_0")
-        far(1, "spare1", nc.sync)
-        far(2, "spare2", nc.sync)
-        scatter_scalar(2, span(1), gated(2, span(1), 2))
-        head_of_1 = gated(1, head, 2, C + C * 4)
-        activate(2, (0, 1), "bank0_1")
-        activate(2, (2, 3), "bank0_0")
-        next_of_1 = gated(1, span(2), 3)
-        far(3, "spare3", nc.sync)
-        activate(3, (2, 3), "bank1_0")
-        activate(3, (0, 1), "bank1_1")
-        far(4, "spare0", nc.sync)
-        far(5, "spare1", nc.sync)
-        far(6, "spare2", nc.sync)
-        far(7, "spare3", nc.sync)
-        activate(4, (0, 1), "bank0_1")
-        activate(4, (2, 3), "bank0_0")
-        head_of_3 = gated(3, head, 4, 0)
-        scatter_scalar(2, middle, gated(2, middle, 4, 2 * C * 4))
-        own_out[1] = turns.tile([P, T], F32, name="own_out1", align_bytes=64, offset=BETWEEN - T * 4)
-        own_out[3] = turns.tile([P, T], F32, name="own_out3", align_bytes=64, offset=BETWEEN)
-        scatter_vector(1, head, head_of_1)
-        scatter_vector(3, head, head_of_3)
-        scatter_vector(1, span(2), next_of_1)
-        all_of_0 = sbuf([P, T], F32, "all_of_0")
-        apply_gate(all_of_0[:, :CUT], 0, slice(0, CUT))
-        scatter_vector(0, first_half, all_of_0[:, first_half])
-        scatter_scalar(3, middle, gated(3, middle))
-        scatter_vector(1, second_half, gated(1, second_half))
+        far(0)
+        activate(1, (2, 3, 0, 1), "odd0")
+        far(1)
+        far(2)
+        scatter_scalar(2, span(1), gated(2, span(1), region(2) + C))
+        first_of_1 = gated(1, small_chunks, region(2) + C + C * WORD)
+        activate(2, (2, 3), "even0")
+        activate(2, (0, 1), "even1")
+        first_of_3 = gated(3, start_of_3, region(3) + C)
+        far(3)
+        activate(3, (2, 3), "odd0")
+        activate(3, (0, 1), "odd1")
+        for unit in range(4, E):
+            far(unit)
+        activate(4, (0, 1), "even1")
+        activate(4, (2, 3), "even0")
+        scatter_scalar(2, middle_of_2, gated(2, middle_of_2, region(4) + C))
+        own_out[1] = placed([P, T], F32, "own_out1", SEAM - T * WORD)
+        own_out[3] = placed([P, T], F32, "own_out3", SEAM)
+        scatter_vector(3, start_of_3, first_of_3)
+        scatter_vector(1, small_chunks, first_of_1)
+        gated_0 = sbuf([P, T], F32, "gated0")
+        apply_gate(gated_0[:, :FIRST_OF_TILE_0], 0, slice(0, FIRST_OF_TILE_0))
+        scatter_vector(0, first_half, gated_0[:, first_half])
+        scatter_scalar(3, middle_of_3, gated(3, middle_of_3))
+        scatter_vector(1, rest_of_1, gated(1, rest_of_1))
         store_own(1, nc.sync)
-        scatter_scalar(2, end, gated(2, end))
+        scatter_scalar(2, end_of_2, gated(2, end_of_2))
         store_own(2, nc.sync)
-        scatter_scalar(3, end, gated(3, end))
+        scatter_scalar(3, end_of_3, gated(3, end_of_3))
         store_own(3, nc.scalar)
-        apply_gate(all_of_0[:, CUT:], 0, slice(CUT, T))
-        scatter_vector(0, second_half, all_of_0[:, second_half])
+        apply_gate(gated_0[:, FIRST_OF_TILE_0:], 0, slice(FIRST_OF_TILE_0, T))
+        scatter_vector(0, second_half, gated_0[:, second_half])
         store_own(0, nc.sync)

@@ -23,17 +23,12 @@ NT = N // P
 PER_COL = 16
 SHARE = 4
 HALF = T // 2
-WORD = 4
 
-CHUNKS = ((0,), (1,), (2, 3), (4, 5), (6, 7))
-EARLY = 4
-ROUNDED_BY_SCALAR, LAST_ROUNDED_BY_SCALAR = 256, 384
-TILE_3_ON_VECTOR = 320
-FIRST_OF_TILE_0 = HALF + 2 * PER_COL
-ROW_OF = {2: 0, 3: 1, 0: 2, 1: 3}
-REGION = C + HALF * WORD
-SEAM = 4 * REGION + T * WORD
-ACROSS_SEAM = SEAM - 64
+CHUNKS = ((0,), (1, 2, 3), (4, 5, 6, 7))
+TILE_ORDER = (3, 1, 0, 2)
+FAR_EARLY, FAR_LATE = (1, 2, 3), (4, 5, 6, 7)
+WINDOW = 4 * T
+TILE_3_ON_VECTOR = 512
 
 
 def tile_moe_loc_lin_gelu_kernel(
@@ -45,23 +40,22 @@ def tile_moe_loc_lin_gelu_kernel(
         turns = ctx.enter_context(tc.tile_pool(name="turns", bufs=1))
         psum = ctx.enter_context(tc.psum_pool(name="psum", bufs=1))
 
-        def sbuf(shape, dtype, name, tag=None):
-            return keep.tile(shape, dtype, name=name, align_bytes=64, tag=tag or name)
-
-        def placed(shape, dtype, name, offset):
-            return turns.tile(shape, dtype, name=name, align_bytes=64, offset=offset)
-
-        def region(c):
-            return (c - 1) * REGION
+        def sbuf(shape, dtype, name, place=None):
+            if place is None:
+                return keep.tile(shape, dtype, name=name, align_bytes=64)
+            return turns.tile(shape, dtype, name=name, align_bytes=64, offset=place * WINDOW)
 
         own_list = keep.tile([P, E * C // PER_COL], U16, name="own_list")
         far_list = keep.tile([P, E * C // PER_COL], U16, name="far_list")
         far_words = sbuf([P, Q], I32, "far_words")
         far_bytes = sbuf([P, Q], U8, "far_bytes")
         w_scale_tiles = [sbuf([P, N], U8, "w_scales%d" % g) for g in range(E // SHARE)]
-        x_f32 = [sbuf([P, 2, T], F32, "x_f32_%d" % h) for h in range(2)]
-        pairs = [sbuf([P, T, 2], BF16, "pairs%d" % h) for h in range(2)]
+        raw = [sbuf([P, T], F32, "raw%d" % j) for j in range(2)]
+        raw_23 = sbuf([P, 2, T], F32, "raw_23")
+        planes = [sbuf([P, T], BF16, "plane%d" % j) for j in range(2)]
+        pair_23 = sbuf([P, T, 2], BF16, "pair_23")
         gates = sbuf([P, E * C], F32, "gates")
+        w_of = [sbuf([P, N], I32, "w_codes%d" % e) for e in range(E)]
 
         nc.vector.memset(far_bytes[:].bitcast(I32), 0)
         for tile in w_scale_tiles:
@@ -79,42 +73,37 @@ def tile_moe_loc_lin_gelu_kernel(
                     w_scales[SHARE * g : SHARE * (g + 1), 0, 4 * quad : 4 * quad + 4, :].bitcast(I32),
                 )
 
-        w_chunks, w_of = [], {}
-        for experts in CHUNKS:
-            tile = sbuf([P, len(experts), N], I32, "w_codes%d" % experts[0])
-            w_chunks.append(tile)
-            for i, e in enumerate(experts):
-                w_of[e] = tile[:, i, :]
+        def load_w(e):
+            nc.sync.dma_start(w_of[e][:], w_words[e, 0].rearrange("p n d -> p (n d)").bitcast(I32))
 
-        def load_w(c, cols):
-            src = w_words[CHUNKS[c][0] : CHUNKS[c][-1] + 1, 0].rearrange("e p n d -> p e (n d)").bitcast(I32)
-            nc.sync.dma_start(w_chunks[c][:, :, cols], src[:, :, cols])
+        def load_gates(cols):
+            nc.sync.dma_start(gates[:, cols], gate[:, cols])
 
         xo_planes = xo.rearrange("(p j) t -> p j t", j=PACK)
         first_half, second_half = slice(0, HALF), slice(HALF, T)
         nc.sync.dma_start(far_words[:], x_words[0].rearrange("p t d -> p (t d)").bitcast(I32))
         nc.sync.dma_start(far_list[:], offs2)
-        nc.sync.dma_start(x_f32[0][:, :, first_half], xo_planes[:, 0:2, first_half])
+        nc.sync.dma_start(raw[0][:], xo_planes[:, 0, :])
         nc.sync.dma_start(own_list[:], offs)
-        nc.sync.dma_start(x_f32[0][:, :, second_half], xo_planes[:, 0:2, second_half])
         for quad in range(4):
+            if quad == 2:
+                nc.sync.dma_start(raw[1][:], xo_planes[:, 1, :])
             nc.sync.dma_start(
                 far_bytes[32 * quad : 32 * quad + 4, :].bitcast(I32),
                 x_scales[0, 4 * quad : 4 * quad + 4, :].bitcast(I32),
             )
-        nc.sync.dma_start(x_f32[1][:, 0, :], xo_planes[:, 2, :])
         for cols in (first_half, second_half):
-            nc.sync.dma_start(x_f32[1][:, 1, cols], xo_planes[:, 3, cols])
+            nc.sync.dma_start(raw_23[:, :, cols], xo_planes[:, 2:4, cols])
         load_w_scales(0)
-        load_w(0, slice(N // 2, N))
-        nc.sync.dma_start(gates[:, : 2 * C], gate[:, : 2 * C])
-        load_w(0, slice(0, N // 2))
-        load_w(1, slice(0, N))
-        load_w(2, slice(0, N))
+        load_w(0)
+        load_gates(slice(0, C))
+        for e in FAR_EARLY:
+            load_w(e)
+        load_gates(slice(C, HALF))
         load_w_scales(1)
-        load_w(3, slice(0, N))
-        load_w(4, slice(0, N))
-        nc.sync.dma_start(gates[:, 2 * C :], gate[:, 2 * C :])
+        for e in FAR_LATE:
+            load_w(e)
+        load_gates(second_half)
 
         def multiply(acc, e, t, codes, scales):
             cols = slice(t * P, (t + 1) * P)
@@ -128,32 +117,22 @@ def tile_moe_loc_lin_gelu_kernel(
                 stop=True,
             )
 
-        far_codes = sbuf([P, E * C], U32, "far_codes")
-        far_scales = {}
+        held = FAR_EARLY[-1] // 2
+        far_scales = [sbuf([P, 2 * C], U8, "far_scales%d" % g, 1 if g == held else None) for g in range(E // 2)]
+        far_codes = [sbuf([P, 2 * C], U32, "far_codes%d" % g, 0 if g == held else None) for g in range(E // 2)]
+        for dst, window in ((far_codes, far_words[:].bitcast(U32)), (far_scales, far_bytes[:])):
+            for g in range(E // 2):
+                offsets = far_list[:, 2 * g * C // PER_COL : 2 * (g + 1) * C // PER_COL]
+                nc.vector.tensor_copy(dst[g][:], window.indirect(offsets))
 
-        def gather_far(dst, window, first, count):
-            for i0 in range(0, count, 2):
-                i1 = min(i0 + 2, count)
-                offsets = far_list[:, (first + i0) * C // PER_COL : (first + i1) * C // PER_COL]
-                nc.vector.tensor_copy(dst[:, i0 * C : i1 * C], window.indirect(offsets))
+        def round_gpsimd(dst, src):
+            nc.gpsimd.tensor_scalar(dst, src, 1.0, 0.0, MULT, ADD)
 
-        def gather_far_bytes(first, count, tile):
-            gather_far(tile, far_bytes[:], first, count)
-            for i in range(count):
-                far_scales[first + i] = tile[:, i * C : (i + 1) * C]
-
-        gather_far(far_codes, far_words[:].bitcast(U32), 0, E)
-        gather_far_bytes(0, EARLY, sbuf([P, EARLY * C], U8, "far_scales"))
-
-        for h in range(2):
-            for cols in (first_half, second_half):
-                src = x_f32[h][:, :, cols].rearrange("p j t -> p t j")
-                dst = pairs[h][:, cols, :]
-                n = LAST_ROUNDED_BY_SCALAR if (h, cols) == (1, second_half) else ROUNDED_BY_SCALAR
-                nc.scalar.copy(dst[:, :n, :], src[:, :n, :])
-                nc.gpsimd.tensor_scalar(dst[:, n:, :], src[:, n:, :], 1.0, 0.0, MULT, ADD)
-
-        last = len(CHUNKS) - 1
+        nc.scalar.copy(planes[0][:, first_half], raw[0][:, first_half])
+        round_gpsimd(planes[0][:, second_half], raw[0][:, second_half])
+        round_gpsimd(planes[1][:], raw[1][:])
+        for cols in (first_half, second_half):
+            round_gpsimd(pair_23[:, cols, :], raw_23[:, :, cols].rearrange("p j t -> p t j"))
 
         def span(c):
             return slice(CHUNKS[c][0] * C, (CHUNKS[c][-1] + 1) * C)
@@ -164,133 +143,128 @@ def tile_moe_loc_lin_gelu_kernel(
         def own_offsets(slots):
             return own_list[:, slots.start // PER_COL : slots.stop // PER_COL]
 
-        grouped_0 = placed([P, C, PACK], BF16, "grouped0", ACROSS_SEAM)
+        grouped_0 = sbuf([P, C, PACK], BF16, "grouped0")
+        picked = {c: sbuf([P, 2, width(c)], U32, "picked%d" % c) for c in (1, 2)}
+        for j in range(2):
+            for c in range(len(CHUNKS)):
+                if c == 0:
+                    dst = grouped_0[:, :, j]
+                else:
+                    dst = picked[c][:, 0, :].bitcast(BF16).rearrange("p (s j) -> p s j", j=2)[:, :, j]
+                nc.scalar.activation(dst, planes[j][:].indirect(own_offsets(span(c))), COPY)
+
+        for j in range(2):
+            nc.vector.tensor_copy(grouped_0[:, :, 2 + j], raw_23[:, j, :].indirect(own_offsets(span(0))))
+
         grouped = {0: grouped_0[:].rearrange("p s j -> p (s j)")}
-        picked = {1: sbuf([P, 2, 2 * C], U32, "picked_odd")}
-
-        def gather_words(dst, c, h):
-            window = pairs[h][:].rearrange("p t j -> p (t j)").bitcast(U32)
-            nc.vector.tensor_copy(dst, window.indirect(own_offsets(span(c))))
-
-        def gather_pair(c, h):
-            gather_words(picked[c % 2][:, h, : width(c)], c, h)
-
-        def weave(c):
-            tile = placed([P, width(c), 2], I32, "grouped%d" % c, region(c))
-            rows = picked[c % 2][:, :, : width(c)].bitcast(I32)
-            nc.vector.tensor_copy(tile[:], rows.rearrange("p h s -> p s h"))
-            grouped[c] = tile[:].rearrange("p s h -> p (s h)").bitcast(BF16)
-
-        y = sbuf([P, NT, E * C], F32, "y")
         quantised = {}
 
         def quantise(c):
-            codes = sbuf([P, width(c)], U32, "codes%d" % c)
+            codes = sbuf([P, width(c)], U32, "codes%d" % c, c - 1 if c else None)
             scales = sbuf([P, width(c)], U8, "scales%d" % c)
             nc.vector.quantize_mx(out=codes[:].bitcast(FP8X4), scales=scales[:], in_=grouped[c])
             quantised[c] = codes, scales
 
-        def activate(c, tiles, bank, bias=0.0):
+        def weave(c):
+            tile = sbuf([P, width(c), 2], I32, "grouped%d" % c, c + 1)
+            nc.vector.tensor_copy(tile[:], picked[c][:].bitcast(I32).rearrange("p h s -> p s h"))
+            grouped[c] = tile[:].rearrange("p s h -> p (s h)").bitcast(BF16)
+
+        quantise(0)
+        window_23 = pair_23[:].rearrange("p t j -> p (t j)").bitcast(U32)
+        for c in (1, 2):
+            nc.vector.tensor_copy(picked[c][:, 1, :], window_23.indirect(own_offsets(span(c))))
+        for step in (weave, quantise):
+            for c in (1, 2):
+                step(c)
+
+        y = sbuf([P, NT, E * C], F32, "y")
+        out_tiles = out.rearrange("(t p) c -> p t c", p=P)
+        z = [sbuf([P, NT, 2 * C], F32, "z%d" % g) for g in range(E // 2)]
+
+        def far(e, bank, bias=0.0):
+            acc = psum.tile([P, NT, C], F32, name="far_acc", tag="bank%d" % bank)
+            g, i = divmod(e, 2)
+            slots = slice(i * C, (i + 1) * C)
+            for t in range(NT):
+                multiply(acc[:, t, :], e, t, far_codes[g][:, slots], far_scales[g][:, slots])
+            nc.scalar.activation(z[g][:, :, i * C : (i + 1) * C], acc[:], GELU, bias=bias)
+            if i == 1:
+                nc.sync.dma_start(out_tiles[:, :, T + 2 * g * C : T + 2 * (g + 1) * C], z[g][:])
+
+        def activate_first(bank):
+            codes, scales = quantised[0]
+            acc = psum.tile([P, NT, C], F32, name="first_acc", tag="bank%d" % bank)
+            for t in range(NT):
+                multiply(acc[:, t, :], 0, t, codes[:], scales[:])
+            nc.scalar.activation(y[:, :, span(0)], acc[:], GELU)
+
+        def activate(c, t, bank):
             codes, scales = quantised[c]
-            acc = psum.tile([P, len(tiles), width(c)], F32, name="own_acc", tag=bank)
-            for u, t in enumerate(tiles):
-                for i, e in enumerate(CHUNKS[c]):
-                    slots = slice(i * C, (i + 1) * C)
-                    multiply(acc[:, u, slots], e, t, codes[:, slots], scales[:, slots])
-            row = ROW_OF[tiles[0]]
-            nc.scalar.activation(y[:, row : row + len(tiles), span(c)], acc[:], GELU, bias=bias)
+            acc = psum.tile([P, width(c)], F32, name="own_acc", tag="bank%d" % bank)
+            for i, e in enumerate(CHUNKS[c]):
+                slots = slice(i * C, (i + 1) * C)
+                multiply(acc[:, slots], e, t, codes[:, slots], scales[:, slots])
+            nc.scalar.activation(y[:, t, span(c)], acc[:], GELU)
 
-        def apply_gate(dst, t, slots):
-            nc.gpsimd.tensor_tensor(dst, y[:, ROW_OF[t], slots], gates[:, slots], MULT)
+        far(0, 0, gelu_of_zeros[:, 0:1])
+        activate_first(5)
+        for e, bank in zip(FAR_EARLY, (1, 2, 3)):
+            far(e, bank)
+        for t, bank in zip(TILE_ORDER, (4, 6, 7, 0)):
+            activate(1, t, bank)
+        activate(2, 1, 5)
+        for e, bank in zip(FAR_LATE, (4, 6, 7, 0)):
+            far(e, bank)
+        for t, bank in zip((3, 2, 0), (1, 2, 3)):
+            activate(2, t, bank)
 
-        own_out = {t: sbuf([P, T], F32, "own_out%d" % t) for t in (0, 2)}
+        gated = [sbuf([P, T], F32, "gated%d" % t, 1 if t == 2 else None) for t in range(NT)]
+        own_out = [sbuf([P, T], F32, "own_out%d" % t, {3: 2, 1: 3}.get(t)) for t in range(NT)]
 
-        def scatter_scalar(t, slots, src):
-            nc.scalar.activation(own_out[t][:].indirect(own_offsets(slots)), src, COPY)
+        def apply_gate(t, lo, hi):
+            nc.gpsimd.tensor_tensor(gated[t][:, lo:hi], y[:, t, lo:hi], gates[:, lo:hi], MULT)
 
-        def scatter_vector(t, slots, src):
-            nc.vector.tensor_copy(own_out[t][:].indirect(own_offsets(slots)), src)
+        def scatter_scalar(t, lo, hi):
+            nc.scalar.activation(own_out[t][:].indirect(own_offsets(slice(lo, hi))), gated[t][:, lo:hi], COPY)
+
+        def scatter_vector(t, lo, hi):
+            nc.vector.tensor_copy(own_out[t][:].indirect(own_offsets(slice(lo, hi))), gated[t][:, lo:hi])
 
         def store_own(t, queue):
             queue.dma_start(out[t * P : (t + 1) * P, :T], own_out[t][:])
 
-        out_tiles = out.rearrange("(t p) c -> p t c", p=P)
+        split = TILE_3_ON_VECTOR
+        halfway = (split + T) // 2
+        for t, lo, hi in (
+            (3, 0, C),
+            (1, 0, C),
+            (3, C, split),
+            (1, C, 3 * C),
+            (0, 0, 2 * C),
+            (2, 0, 3 * C),
+            (1, 3 * C, T),
+            (3, split, halfway),
+            (2, 3 * C, 6 * C),
+            (0, 2 * C, T),
+            (3, halfway, T),
+            (2, 6 * C, T),
+        ):
+            apply_gate(t, lo, hi)
 
-        def far(unit):
-            g, h = divmod(unit, 2)
-            acc = psum.tile([P, 2, 2 * C], F32, name="far_acc", tag="far%d" % (unit % 4))
-            for u in range(2):
-                for i in range(2):
-                    e = 2 * g + i
-                    codes = far_codes[:, e * C : (e + 1) * C]
-                    multiply(acc[:, u, i * C : (i + 1) * C], e, 2 * h + u, codes, far_scales[e])
-            z = sbuf([P, 2, 2 * C], F32, "z%d" % unit)
-            nc.scalar.activation(z[:], acc[:], GELU)
-            nc.sync.dma_start(out_tiles[:, 2 * h : 2 * h + 2, T + 2 * g * C : T + 2 * (g + 1) * C], z[:])
-
-        gather_words(grouped[0].bitcast(U32).rearrange("p (s h) -> p s h", h=2)[:, :, 0], 0, 0)
-        for j in range(2):
-            nc.vector.tensor_copy(grouped_0[:, :, 2 + j], x_f32[1][:, j, :].indirect(own_offsets(span(0))))
-        gather_pair(1, 0)
-        quantise(0)
-        picked[0] = placed([P, 2, 2 * C], U32, "picked_even", ACROSS_SEAM)
-        for c in range(1, last + 1):
-            gather_pair(c, 1)
-            if c < last:
-                gather_pair(c + 1, 0)
-            weave(c)
-            if c > 1:
-                e = EARLY + c - 2
-                gather_far_bytes(e, 1, placed([P, C], U8, "far_scales%d" % e, region(c - 1)))
-            quantise(c)
-        gather_far_bytes(E - 1, 1, sbuf([P, C], U8, "far_scales_last", "pairs0"))
-
-        def gated(t, slots, offset=None):
-            shape, name = [P, slots.stop - slots.start], "gated%d_%d" % (t, slots.start)
-            dst = sbuf(shape, F32, name) if offset is None else placed(shape, F32, name, offset)
-            apply_gate(dst[:], t, slots)
-            return dst[:]
-
-        small_chunks = slice(0, 2 * C)
-        middle_of_2, end_of_2 = slice(2 * C, 5 * C), slice(5 * C, T)
-        halfway = (TILE_3_ON_VECTOR + T) // 2
-        start_of_3, middle_of_3, end_of_3 = slice(0, TILE_3_ON_VECTOR), slice(TILE_3_ON_VECTOR, halfway), slice(halfway, T)
-        rest_of_1 = slice(2 * C, T)
-
-        activate(0, (2,), "even0", gelu_of_zeros[:, 0:1])
-        activate(0, (3, 0, 1), "even1")
-        scatter_scalar(2, span(0), gated(2, span(0)))
-        far(0)
-        activate(1, (2, 3, 0, 1), "odd0")
-        far(1)
-        far(2)
-        scatter_scalar(2, span(1), gated(2, span(1), region(2) + C))
-        first_of_1 = gated(1, small_chunks, region(2) + C + C * WORD)
-        activate(2, (2, 3), "even0")
-        activate(2, (0, 1), "even1")
-        first_of_3 = gated(3, start_of_3, region(3) + C)
-        far(3)
-        activate(3, (2, 3), "odd0")
-        activate(3, (0, 1), "odd1")
-        for unit in range(4, E):
-            far(unit)
-        activate(4, (0, 1), "even1")
-        activate(4, (2, 3), "even0")
-        scatter_scalar(2, middle_of_2, gated(2, middle_of_2, region(4) + C))
-        own_out[1] = placed([P, T], F32, "own_out1", SEAM - T * WORD)
-        own_out[3] = placed([P, T], F32, "own_out3", SEAM)
-        scatter_vector(3, start_of_3, first_of_3)
-        scatter_vector(1, small_chunks, first_of_1)
-        gated_0 = sbuf([P, T], F32, "gated0")
-        apply_gate(gated_0[:, :FIRST_OF_TILE_0], 0, slice(0, FIRST_OF_TILE_0))
-        scatter_vector(0, first_half, gated_0[:, first_half])
-        scatter_scalar(3, middle_of_3, gated(3, middle_of_3))
-        scatter_vector(1, rest_of_1, gated(1, rest_of_1))
+        scatter_vector(3, 0, C)
+        scatter_vector(1, 0, C)
+        scatter_vector(3, C, split)
+        scatter_vector(1, C, 3 * C)
+        scatter_scalar(2, 0, 3 * C)
+        scatter_vector(0, 0, 2 * C)
+        scatter_scalar(3, split, halfway)
+        scatter_vector(1, 3 * C, T)
         store_own(1, nc.sync)
-        scatter_scalar(2, end_of_2, gated(2, end_of_2))
-        store_own(2, nc.sync)
-        scatter_scalar(3, end_of_3, gated(3, end_of_3))
-        store_own(3, nc.scalar)
-        apply_gate(gated_0[:, FIRST_OF_TILE_0:], 0, slice(FIRST_OF_TILE_0, T))
-        scatter_vector(0, second_half, gated_0[:, second_half])
+        scatter_scalar(2, 3 * C, 6 * C)
+        scatter_scalar(3, halfway, T)
+        store_own(3, nc.sync)
+        scatter_scalar(2, 6 * C, T)
+        store_own(2, nc.scalar)
+        scatter_vector(0, 2 * C, T)
         store_own(0, nc.sync)

@@ -28,7 +28,8 @@ CHUNKS = ((0,), (1, 2, 3), (4, 5, 6, 7))
 TILE_ORDER = (3, 1, 0, 2)
 FAR_EARLY, FAR_LATE = (1, 2, 3), (4, 5, 6, 7)
 WINDOW = 4 * T
-TILE_3_ON_VECTOR = 512
+TILE_3_ON_VECTOR = 448
+CUTS_OF_2 = (C, 448, 736)
 
 
 def tile_moe_loc_lin_gelu_kernel(
@@ -83,10 +84,11 @@ def tile_moe_loc_lin_gelu_kernel(
         first_half, second_half = slice(0, HALF), slice(HALF, T)
         nc.sync.dma_start(far_words[:], x_words[0].rearrange("p t d -> p (t d)").bitcast(I32))
         nc.sync.dma_start(far_list[:], offs2)
-        nc.sync.dma_start(raw[0][:], xo_planes[:, 0, :])
+        for cols in (first_half, second_half):
+            nc.sync.dma_start(raw[0][:, cols], xo_planes[:, 0, cols])
         nc.sync.dma_start(own_list[:], offs)
         for quad in range(4):
-            if quad == 2:
+            if quad == 1:
                 nc.sync.dma_start(raw[1][:], xo_planes[:, 1, :])
             nc.sync.dma_start(
                 far_bytes[32 * quad : 32 * quad + 4, :].bitcast(I32),
@@ -128,10 +130,12 @@ def tile_moe_loc_lin_gelu_kernel(
         def round_gpsimd(dst, src):
             nc.gpsimd.tensor_scalar(dst, src, 1.0, 0.0, MULT, ADD)
 
-        nc.scalar.copy(planes[0][:, first_half], raw[0][:, first_half])
-        round_gpsimd(planes[0][:, second_half], raw[0][:, second_half])
+        last_quarter = slice(T - T // 4, T)
+        for cols in (first_half, slice(HALF, last_quarter.start)):
+            nc.scalar.copy(planes[0][:, cols], raw[0][:, cols])
+        round_gpsimd(planes[0][:, last_quarter], raw[0][:, last_quarter])
         round_gpsimd(planes[1][:], raw[1][:])
-        for cols in (first_half, second_half):
+        for cols in (first_half, slice(HALF, last_quarter.start)):
             round_gpsimd(pair_23[:, cols, :], raw_23[:, :, cols].rearrange("p j t -> p t j"))
 
         def span(c):
@@ -155,6 +159,8 @@ def tile_moe_loc_lin_gelu_kernel(
 
         for j in range(2):
             nc.vector.tensor_copy(grouped_0[:, :, 2 + j], raw_23[:, j, :].indirect(own_offsets(span(0))))
+
+        nc.vector.tensor_copy(pair_23[:, last_quarter, :], raw_23[:, :, last_quarter].rearrange("p j t -> p t j"))
 
         grouped = {0: grouped_0[:].rearrange("p s j -> p (s j)")}
         quantised = {}
@@ -182,13 +188,13 @@ def tile_moe_loc_lin_gelu_kernel(
         out_tiles = out.rearrange("(t p) c -> p t c", p=P)
         z = [sbuf([P, NT, 2 * C], F32, "z%d" % g) for g in range(E // 2)]
 
-        def far(e, bank, bias=0.0):
+        def far(e, bank):
             acc = psum.tile([P, NT, C], F32, name="far_acc", tag="bank%d" % bank)
             g, i = divmod(e, 2)
             slots = slice(i * C, (i + 1) * C)
             for t in range(NT):
                 multiply(acc[:, t, :], e, t, far_codes[g][:, slots], far_scales[g][:, slots])
-            nc.scalar.activation(z[g][:, :, i * C : (i + 1) * C], acc[:], GELU, bias=bias)
+            nc.scalar.activation(z[g][:, :, i * C : (i + 1) * C], acc[:], GELU)
             if i == 1:
                 nc.sync.dma_start(out_tiles[:, :, T + 2 * g * C : T + 2 * (g + 1) * C], z[g][:])
 
@@ -197,7 +203,7 @@ def tile_moe_loc_lin_gelu_kernel(
             acc = psum.tile([P, NT, C], F32, name="first_acc", tag="bank%d" % bank)
             for t in range(NT):
                 multiply(acc[:, t, :], 0, t, codes[:], scales[:])
-            nc.scalar.activation(y[:, :, span(0)], acc[:], GELU)
+            nc.scalar.activation(y[:, :, span(0)], acc[:], GELU, bias=gelu_of_zeros[:, 0:1])
 
         def activate(c, t, bank):
             codes, scales = quantised[c]
@@ -207,8 +213,8 @@ def tile_moe_loc_lin_gelu_kernel(
                 multiply(acc[:, slots], e, t, codes[:, slots], scales[:, slots])
             nc.scalar.activation(y[:, t, span(c)], acc[:], GELU)
 
-        far(0, 0, gelu_of_zeros[:, 0:1])
         activate_first(5)
+        far(0, 0)
         for e, bank in zip(FAR_EARLY, (1, 2, 3)):
             far(e, bank)
         for t, bank in zip(TILE_ORDER, (4, 6, 7, 0)):
@@ -220,7 +226,8 @@ def tile_moe_loc_lin_gelu_kernel(
             activate(2, t, bank)
 
         gated = [sbuf([P, T], F32, "gated%d" % t, 1 if t == 2 else None) for t in range(NT)]
-        own_out = [sbuf([P, T], F32, "own_out%d" % t, {3: 2, 1: 3}.get(t)) for t in range(NT)]
+        first_of_2 = sbuf([P, C], F32, "first_of_2")
+        own_out = [sbuf([P, T], F32, "own_out%d" % t, {3: 2, 1: 3, 2: 0}.get(t)) for t in range(NT)]
 
         def apply_gate(t, lo, hi):
             nc.gpsimd.tensor_tensor(gated[t][:, lo:hi], y[:, t, lo:hi], gates[:, lo:hi], MULT)
@@ -239,32 +246,38 @@ def tile_moe_loc_lin_gelu_kernel(
         for t, lo, hi in (
             (3, 0, C),
             (1, 0, C),
+        ):
+            apply_gate(t, lo, hi)
+        nc.gpsimd.tensor_tensor(first_of_2[:], y[:, 2, :C], gates[:, :C], MULT)
+        a, b, c = CUTS_OF_2
+        for t, lo, hi in (
             (3, C, split),
             (1, C, 3 * C),
             (0, 0, 2 * C),
-            (2, 0, 3 * C),
+            (2, a, b),
             (1, 3 * C, T),
             (3, split, halfway),
-            (2, 3 * C, 6 * C),
+            (2, b, c),
             (0, 2 * C, T),
             (3, halfway, T),
-            (2, 6 * C, T),
+            (2, c, T),
         ):
             apply_gate(t, lo, hi)
 
         scatter_vector(3, 0, C)
         scatter_vector(1, 0, C)
+        nc.vector.tensor_copy(own_out[2][:].indirect(own_offsets(span(0))), first_of_2[:])
         scatter_vector(3, C, split)
         scatter_vector(1, C, 3 * C)
-        scatter_scalar(2, 0, 3 * C)
+        scatter_scalar(2, a, b)
         scatter_vector(0, 0, 2 * C)
         scatter_scalar(3, split, halfway)
         scatter_vector(1, 3 * C, T)
         store_own(1, nc.sync)
-        scatter_scalar(2, 3 * C, 6 * C)
+        scatter_scalar(2, b, c)
         scatter_scalar(3, halfway, T)
         store_own(3, nc.sync)
-        scatter_scalar(2, 6 * C, T)
+        scatter_scalar(2, c, T)
         store_own(2, nc.scalar)
         scatter_vector(0, 2 * C, T)
         store_own(0, nc.sync)

@@ -28,7 +28,13 @@ CHUNKS = ((0,), (1, 2, 3), (4, 5, 6, 7))
 TILE_ORDER = (3, 1, 0, 2)
 FAR_EARLY, FAR_LATE = (1, 2, 3), (4, 5, 6, 7)
 WINDOW = 4 * T
-TILE_3_ON_VECTOR = 448
+PLACE = {
+    "far_codes1": 0, "codes1": 0, "own_out2": 0,
+    "far_scales1": WINDOW, "codes2": WINDOW, "gated2_128": WINDOW,
+    "grouped1": 2 * WINDOW, "own_out3": 2 * WINDOW,
+    "grouped2": 3 * WINDOW, "gated2_0": 3 * WINDOW, "own_out1": 3 * WINDOW + WINDOW // 2,
+}
+TILE_3_ON_VECTOR = 384
 CUTS_OF_2 = (C, 448, 736)
 
 
@@ -41,10 +47,10 @@ def tile_moe_loc_lin_gelu_kernel(
         turns = ctx.enter_context(tc.tile_pool(name="turns", bufs=1))
         psum = ctx.enter_context(tc.psum_pool(name="psum", bufs=1))
 
-        def sbuf(shape, dtype, name, place=None):
-            if place is None:
-                return keep.tile(shape, dtype, name=name, align_bytes=64)
-            return turns.tile(shape, dtype, name=name, align_bytes=64, offset=place * WINDOW)
+        def sbuf(shape, dtype, name):
+            if name in PLACE:
+                return turns.tile(shape, dtype, name=name, align_bytes=64, offset=PLACE[name])
+            return keep.tile(shape, dtype, name=name, align_bytes=64)
 
         own_list = keep.tile([P, E * C // PER_COL], U16, name="own_list")
         far_list = keep.tile([P, E * C // PER_COL], U16, name="far_list")
@@ -119,9 +125,8 @@ def tile_moe_loc_lin_gelu_kernel(
                 stop=True,
             )
 
-        held = FAR_EARLY[-1] // 2
-        far_scales = [sbuf([P, 2 * C], U8, "far_scales%d" % g, 1 if g == held else None) for g in range(E // 2)]
-        far_codes = [sbuf([P, 2 * C], U32, "far_codes%d" % g, 0 if g == held else None) for g in range(E // 2)]
+        far_scales = [sbuf([P, 2 * C], U8, "far_scales%d" % g) for g in range(E // 2)]
+        far_codes = [sbuf([P, 2 * C], U32, "far_codes%d" % g) for g in range(E // 2)]
         for dst, window in ((far_codes, far_words[:].bitcast(U32)), (far_scales, far_bytes[:])):
             for g in range(E // 2):
                 offsets = far_list[:, 2 * g * C // PER_COL : 2 * (g + 1) * C // PER_COL]
@@ -166,13 +171,13 @@ def tile_moe_loc_lin_gelu_kernel(
         quantised = {}
 
         def quantise(c):
-            codes = sbuf([P, width(c)], U32, "codes%d" % c, c - 1 if c else None)
+            codes = sbuf([P, width(c)], U32, "codes%d" % c)
             scales = sbuf([P, width(c)], U8, "scales%d" % c)
             nc.vector.quantize_mx(out=codes[:].bitcast(FP8X4), scales=scales[:], in_=grouped[c])
             quantised[c] = codes, scales
 
         def weave(c):
-            tile = sbuf([P, width(c), 2], I32, "grouped%d" % c, c + 1)
+            tile = sbuf([P, width(c), 2], I32, "grouped%d" % c)
             nc.vector.tensor_copy(tile[:], picked[c][:].bitcast(I32).rearrange("p h s -> p s h"))
             grouped[c] = tile[:].rearrange("p s h -> p (s h)").bitcast(BF16)
 
@@ -213,6 +218,29 @@ def tile_moe_loc_lin_gelu_kernel(
                 multiply(acc[:, slots], e, t, codes[:, slots], scales[:, slots])
             nc.scalar.activation(y[:, t, span(c)], acc[:], GELU)
 
+        own_out = [sbuf([P, T], F32, "own_out%d" % t) for t in range(NT)]
+        gated = {}
+
+        def apply_gate(t, lo, hi):
+            gated[t, lo] = sbuf([P, hi - lo], F32, "gated%d_%d" % (t, lo))
+            nc.gpsimd.tensor_tensor(gated[t, lo][:], y[:, t, lo:hi], gates[:, lo:hi], MULT)
+
+        def window(t, lo):
+            return own_out[t][:].indirect(own_offsets(slice(lo, lo + gated[t, lo].shape[1])))
+
+        def scatter_scalar(t, lo):
+            nc.scalar.activation(window(t, lo), gated[t, lo][:], COPY)
+
+        def scatter_vector(t, lo):
+            nc.vector.tensor_copy(window(t, lo), gated[t, lo][:])
+
+        def store_own(t, queue):
+            queue.dma_start(out[t * P : (t + 1) * P, :T], own_out[t][:])
+
+        split = TILE_3_ON_VECTOR
+        halfway = (split + T) // 2
+        a, b, c = CUTS_OF_2
+
         activate_first(5)
         far(0, 0)
         for e, bank in zip(FAR_EARLY, (1, 2, 3)):
@@ -225,32 +253,10 @@ def tile_moe_loc_lin_gelu_kernel(
         for t, bank in zip((3, 2, 0), (1, 2, 3)):
             activate(2, t, bank)
 
-        gated = [sbuf([P, T], F32, "gated%d" % t, 1 if t == 2 else None) for t in range(NT)]
-        first_of_2 = sbuf([P, C], F32, "first_of_2")
-        own_out = [sbuf([P, T], F32, "own_out%d" % t, {3: 2, 1: 3, 2: 0}.get(t)) for t in range(NT)]
-
-        def apply_gate(t, lo, hi):
-            nc.gpsimd.tensor_tensor(gated[t][:, lo:hi], y[:, t, lo:hi], gates[:, lo:hi], MULT)
-
-        def scatter_scalar(t, lo, hi):
-            nc.scalar.activation(own_out[t][:].indirect(own_offsets(slice(lo, hi))), gated[t][:, lo:hi], COPY)
-
-        def scatter_vector(t, lo, hi):
-            nc.vector.tensor_copy(own_out[t][:].indirect(own_offsets(slice(lo, hi))), gated[t][:, lo:hi])
-
-        def store_own(t, queue):
-            queue.dma_start(out[t * P : (t + 1) * P, :T], own_out[t][:])
-
-        split = TILE_3_ON_VECTOR
-        halfway = (split + T) // 2
         for t, lo, hi in (
             (3, 0, C),
             (1, 0, C),
-        ):
-            apply_gate(t, lo, hi)
-        nc.gpsimd.tensor_tensor(first_of_2[:], y[:, 2, :C], gates[:, :C], MULT)
-        a, b, c = CUTS_OF_2
-        for t, lo, hi in (
+            (2, 0, C),
             (3, C, split),
             (1, C, 3 * C),
             (0, 0, 2 * C),
@@ -264,20 +270,20 @@ def tile_moe_loc_lin_gelu_kernel(
         ):
             apply_gate(t, lo, hi)
 
-        scatter_vector(3, 0, C)
-        scatter_vector(1, 0, C)
-        nc.vector.tensor_copy(own_out[2][:].indirect(own_offsets(span(0))), first_of_2[:])
-        scatter_vector(3, C, split)
-        scatter_vector(1, C, 3 * C)
-        scatter_scalar(2, a, b)
-        scatter_vector(0, 0, 2 * C)
-        scatter_scalar(3, split, halfway)
-        scatter_vector(1, 3 * C, T)
+        scatter_vector(3, 0)
+        scatter_vector(1, 0)
+        scatter_vector(2, 0)
+        scatter_vector(3, C)
+        scatter_vector(1, C)
+        scatter_scalar(2, a)
+        scatter_vector(0, 0)
+        scatter_scalar(3, split)
+        scatter_vector(1, 3 * C)
         store_own(1, nc.sync)
-        scatter_scalar(2, b, c)
-        scatter_scalar(3, halfway, T)
+        scatter_scalar(2, b)
+        scatter_scalar(3, halfway)
         store_own(3, nc.sync)
-        scatter_scalar(2, c, T)
+        scatter_scalar(2, c)
         store_own(2, nc.scalar)
-        scatter_vector(0, 2 * C, T)
+        scatter_vector(0, 2 * C)
         store_own(0, nc.sync)

@@ -26,16 +26,15 @@ HALF = T // 2
 
 CHUNKS = ((0,), (1, 2, 3), (4, 5, 6, 7))
 TILE_ORDER = (3, 1, 0, 2)
-FAR_EARLY, FAR_LATE = (1, 2, 3), (4, 5, 6, 7)
 WINDOW = 4 * T
 PLACE = {
-    "far_codes1": 0, "codes1": 0, "own_out2": 0,
-    "far_scales1": WINDOW, "codes2": WINDOW, "gated2_128": WINDOW,
+    "far_codes2": 0, "codes1": 0,
+    "far_scales2": WINDOW, "codes2": WINDOW, "gated2_0": WINDOW,
     "grouped1": 2 * WINDOW, "own_out3": 2 * WINDOW,
-    "grouped2": 3 * WINDOW, "gated2_0": 3 * WINDOW, "own_out1": 3 * WINDOW + WINDOW // 2,
+    "grouped2": 3 * WINDOW, "own_out1": 3 * WINDOW,
 }
-TILE_3_ON_VECTOR = 384
-CUTS_OF_2 = (C, 448, 736)
+TILE_3_ON_VECTOR = 416
+CUTS_OF_2 = (0, 384, 704)
 
 
 def tile_moe_loc_lin_gelu_kernel(
@@ -102,15 +101,13 @@ def tile_moe_loc_lin_gelu_kernel(
             )
         for cols in (first_half, second_half):
             nc.sync.dma_start(raw_23[:, :, cols], xo_planes[:, 2:4, cols])
-        load_w_scales(0)
-        load_w(0)
         load_gates(slice(0, C))
-        for e in FAR_EARLY:
+        load_w_scales(0)
+        for e in range(E):
+            if e == SHARE:
+                load_w_scales(1)
             load_w(e)
         load_gates(slice(C, HALF))
-        load_w_scales(1)
-        for e in FAR_LATE:
-            load_w(e)
         load_gates(second_half)
 
         def multiply(acc, e, t, codes, scales):
@@ -140,7 +137,7 @@ def tile_moe_loc_lin_gelu_kernel(
             nc.scalar.copy(planes[0][:, cols], raw[0][:, cols])
         round_gpsimd(planes[0][:, last_quarter], raw[0][:, last_quarter])
         round_gpsimd(planes[1][:], raw[1][:])
-        for cols in (first_half, slice(HALF, last_quarter.start)):
+        for cols in (first_half, second_half):
             round_gpsimd(pair_23[:, cols, :], raw_23[:, :, cols].rearrange("p j t -> p t j"))
 
         def span(c):
@@ -155,17 +152,12 @@ def tile_moe_loc_lin_gelu_kernel(
         grouped_0 = sbuf([P, C, PACK], BF16, "grouped0")
         picked = {c: sbuf([P, 2, width(c)], U32, "picked%d" % c) for c in (1, 2)}
         for j in range(2):
-            for c in range(len(CHUNKS)):
-                if c == 0:
-                    dst = grouped_0[:, :, j]
-                else:
-                    dst = picked[c][:, 0, :].bitcast(BF16).rearrange("p (s j) -> p s j", j=2)[:, :, j]
+            for c in (1, 2):
+                dst = picked[c][:, 0, :].bitcast(BF16).rearrange("p (s j) -> p s j", j=2)[:, :, j]
                 nc.scalar.activation(dst, planes[j][:].indirect(own_offsets(span(c))), COPY)
 
-        for j in range(2):
-            nc.vector.tensor_copy(grouped_0[:, :, 2 + j], raw_23[:, j, :].indirect(own_offsets(span(0))))
-
-        nc.vector.tensor_copy(pair_23[:, last_quarter, :], raw_23[:, :, last_quarter].rearrange("p j t -> p t j"))
+        for j, plane in enumerate((raw[0][:], raw[1][:], raw_23[:, 0, :], raw_23[:, 1, :])):
+            nc.vector.tensor_copy(grouped_0[:, :, j], plane.indirect(own_offsets(span(0))))
 
         grouped = {0: grouped_0[:].rearrange("p s j -> p (s j)")}
         quantised = {}
@@ -199,7 +191,7 @@ def tile_moe_loc_lin_gelu_kernel(
             slots = slice(i * C, (i + 1) * C)
             for t in range(NT):
                 multiply(acc[:, t, :], e, t, far_codes[g][:, slots], far_scales[g][:, slots])
-            nc.scalar.activation(z[g][:, :, i * C : (i + 1) * C], acc[:], GELU)
+            nc.scalar.activation(z[g][:, :, i * C : (i + 1) * C], acc[:], GELU, bias=gelu_of_zeros[:, 0:1] if e == 0 else 0.0)
             if i == 1:
                 nc.sync.dma_start(out_tiles[:, :, T + 2 * g * C : T + 2 * (g + 1) * C], z[g][:])
 
@@ -208,7 +200,7 @@ def tile_moe_loc_lin_gelu_kernel(
             acc = psum.tile([P, NT, C], F32, name="first_acc", tag="bank%d" % bank)
             for t in range(NT):
                 multiply(acc[:, t, :], 0, t, codes[:], scales[:])
-            nc.scalar.activation(y[:, :, span(0)], acc[:], GELU, bias=gelu_of_zeros[:, 0:1])
+            nc.scalar.activation(y[:, :, span(0)], acc[:], GELU)
 
         def activate(c, t, bank):
             codes, scales = quantised[c]
@@ -238,25 +230,21 @@ def tile_moe_loc_lin_gelu_kernel(
             queue.dma_start(out[t * P : (t + 1) * P, :T], own_out[t][:])
 
         split = TILE_3_ON_VECTOR
-        halfway = (split + T) // 2
+        halfway = CUTS_OF_2[2]
         a, b, c = CUTS_OF_2
 
-        activate_first(5)
-        far(0, 0)
-        for e, bank in zip(FAR_EARLY, (1, 2, 3)):
-            far(e, bank)
-        for t, bank in zip(TILE_ORDER, (4, 6, 7, 0)):
+        for e in range(E):
+            if e == 3:
+                activate_first(1)
+            far(e, e)
+        for t, bank in zip(TILE_ORDER, (0, 2, 3, 1)):
             activate(1, t, bank)
-        activate(2, 1, 5)
-        for e, bank in zip(FAR_LATE, (4, 6, 7, 0)):
-            far(e, bank)
-        for t, bank in zip((3, 2, 0), (1, 2, 3)):
+        for t, bank in zip((1, 3, 2, 0), (4, 5, 6, 7)):
             activate(2, t, bank)
 
         for t, lo, hi in (
             (3, 0, C),
             (1, 0, C),
-            (2, 0, C),
             (3, C, split),
             (1, C, 3 * C),
             (0, 0, 2 * C),
@@ -272,7 +260,6 @@ def tile_moe_loc_lin_gelu_kernel(
 
         scatter_vector(3, 0)
         scatter_vector(1, 0)
-        scatter_vector(2, 0)
         scatter_vector(3, C)
         scatter_vector(1, C)
         scatter_scalar(2, a)

@@ -27,14 +27,21 @@ HALF = T // 2
 CHUNKS = ((0,), (1, 2, 3), (4, 5, 6, 7))
 TILE_ORDER = (3, 1, 0, 2)
 WINDOW = 4 * T
-PLACE = {
-    "far_codes2": 0, "codes1": 0,
-    "far_scales2": WINDOW, "codes2": WINDOW, "gated2_0": WINDOW,
-    "grouped1": 2 * WINDOW, "own_out3": 2 * WINDOW,
-    "grouped2": 3 * WINDOW, "own_out1": 3 * WINDOW,
+LOW = {
+    "own_out1": 0, "own_out0": WINDOW, "grouped2": WINDOW - 64,
+    "gated0_0": 2 * WINDOW, "gated0_128": 2 * WINDOW + 4 * C, "gated0_256": 2 * WINDOW + 8 * C,
+    "gated1_0": 3 * WINDOW, "gated1_128": 3 * WINDOW + 4 * C, "gated1_384": 3 * WINDOW + 12 * C,
+    "gated3_0": 4 * WINDOW, "gated3_128": 4 * WINDOW + 4 * C, "gated2_0": 5 * WINDOW,
+    "pair_23": 6 * WINDOW, "raw_23": 7 * WINDOW, "far_words": 9 * WINDOW, "far_bytes": 9 * WINDOW + WINDOW // 2,
 }
-TILE_3_ON_VECTOR = 416
-CUTS_OF_2 = (0, 384, 704)
+HIGH = {
+    "far_scales2": 0, "codes2": 0, "gated2_128": 0,
+    "grouped1": WINDOW, "own_out3": WINDOW,
+    "far_codes2": 2 * WINDOW, "codes1": 2 * WINDOW, "own_out2": 2 * WINDOW,
+    "plane0": 3 * WINDOW, "plane1": 3 * WINDOW + WINDOW // 2,
+}
+TILE_3_ON_VECTOR = 352
+CUTS_OF_2 = (C, 448, 736)
 
 
 def tile_moe_loc_lin_gelu_kernel(
@@ -42,13 +49,15 @@ def tile_moe_loc_lin_gelu_kernel(
 ):
     nc = tc.nc
     with ExitStack() as ctx:
+        low = ctx.enter_context(tc.tile_pool(name="low", bufs=1))
         keep = ctx.enter_context(tc.tile_pool(name="keep", bufs=1))
-        turns = ctx.enter_context(tc.tile_pool(name="turns", bufs=1))
+        high = ctx.enter_context(tc.tile_pool(name="high", bufs=1))
         psum = ctx.enter_context(tc.psum_pool(name="psum", bufs=1))
 
         def sbuf(shape, dtype, name):
-            if name in PLACE:
-                return turns.tile(shape, dtype, name=name, align_bytes=64, offset=PLACE[name])
+            for pool, places in ((low, LOW), (high, HIGH)):
+                if name in places:
+                    return pool.tile(shape, dtype, name=name, align_bytes=64, offset=places[name])
             return keep.tile(shape, dtype, name=name, align_bytes=64)
 
         own_list = keep.tile([P, E * C // PER_COL], U16, name="own_list")
@@ -137,7 +146,7 @@ def tile_moe_loc_lin_gelu_kernel(
             nc.scalar.copy(planes[0][:, cols], raw[0][:, cols])
         round_gpsimd(planes[0][:, last_quarter], raw[0][:, last_quarter])
         round_gpsimd(planes[1][:], raw[1][:])
-        for cols in (first_half, second_half):
+        for cols in (first_half, slice(HALF, last_quarter.start)):
             round_gpsimd(pair_23[:, cols, :], raw_23[:, :, cols].rearrange("p j t -> p t j"))
 
         def span(c):
@@ -150,14 +159,18 @@ def tile_moe_loc_lin_gelu_kernel(
             return own_list[:, slots.start // PER_COL : slots.stop // PER_COL]
 
         grouped_0 = sbuf([P, C, PACK], BF16, "grouped0")
-        picked = {c: sbuf([P, 2, width(c)], U32, "picked%d" % c) for c in (1, 2)}
+        picked = {c: sbuf([P, 2 if c else 1, width(c)], U32, "picked%d" % c) for c in range(len(CHUNKS))}
         for j in range(2):
-            for c in (1, 2):
+            for c in range(len(CHUNKS)):
                 dst = picked[c][:, 0, :].bitcast(BF16).rearrange("p (s j) -> p s j", j=2)[:, :, j]
                 nc.scalar.activation(dst, planes[j][:].indirect(own_offsets(span(c))), COPY)
 
-        for j, plane in enumerate((raw[0][:], raw[1][:], raw_23[:, 0, :], raw_23[:, 1, :])):
+        words_0 = grouped_0[:].rearrange("p s j -> p (s j)").bitcast(I32).rearrange("p (s h) -> p s h", h=2)
+        nc.vector.tensor_copy(words_0[:, :, 0], picked[0][:, 0, :].bitcast(I32))
+        for j, plane in enumerate((raw_23[:, 0, :], raw_23[:, 1, :]), 2):
             nc.vector.tensor_copy(grouped_0[:, :, j], plane.indirect(own_offsets(span(0))))
+
+        nc.vector.tensor_copy(pair_23[:, last_quarter, :], raw_23[:, :, last_quarter].rearrange("p j t -> p t j"))
 
         grouped = {0: grouped_0[:].rearrange("p s j -> p (s j)")}
         quantised = {}
@@ -230,7 +243,7 @@ def tile_moe_loc_lin_gelu_kernel(
             queue.dma_start(out[t * P : (t + 1) * P, :T], own_out[t][:])
 
         split = TILE_3_ON_VECTOR
-        halfway = CUTS_OF_2[2]
+        halfway = 704
         a, b, c = CUTS_OF_2
 
         for e in range(E):
@@ -245,9 +258,11 @@ def tile_moe_loc_lin_gelu_kernel(
         for t, lo, hi in (
             (3, 0, C),
             (1, 0, C),
+            (0, 0, C),
+            (2, 0, C),
             (3, C, split),
             (1, C, 3 * C),
-            (0, 0, 2 * C),
+            (0, C, 2 * C),
             (2, a, b),
             (1, 3 * C, T),
             (3, split, halfway),
@@ -260,10 +275,12 @@ def tile_moe_loc_lin_gelu_kernel(
 
         scatter_vector(3, 0)
         scatter_vector(1, 0)
+        scatter_vector(0, 0)
+        scatter_vector(2, 0)
         scatter_vector(3, C)
         scatter_vector(1, C)
         scatter_scalar(2, a)
-        scatter_vector(0, 0)
+        scatter_vector(0, C)
         scatter_scalar(3, split)
         scatter_vector(1, 3 * C)
         store_own(1, nc.sync)

@@ -25,6 +25,7 @@ SHARE = 4
 HALF = T // 2
 
 CHUNKS = ((0,), (1, 2, 3), (4, 5, 6, 7))
+FAR_ORDER = (0, 2, 3, 4, 5, 6, 1, 7)
 TILE_ORDER = (3, 1, 0, 2)
 WINDOW = 4 * T
 LOW = {
@@ -35,12 +36,12 @@ LOW = {
     "pair_23": 6 * WINDOW, "raw_23": 7 * WINDOW, "far_words": 9 * WINDOW, "far_bytes": 9 * WINDOW + WINDOW // 2,
 }
 HIGH = {
-    "far_scales2": 0, "codes2": 0, "gated2_128": 0,
+    "codes2": 0, "gated2_128": 0,
     "grouped1": WINDOW, "own_out3": WINDOW,
-    "far_codes2": 2 * WINDOW, "codes1": 2 * WINDOW, "own_out2": 2 * WINDOW,
+    "codes1": 2 * WINDOW, "own_out2": 2 * WINDOW,
     "plane0": 3 * WINDOW, "plane1": 3 * WINDOW + WINDOW // 2,
 }
-TILE_3_ON_VECTOR = 352
+TILE_3_ON_VECTOR = 320
 CUTS_OF_2 = (C, 448, 736)
 
 
@@ -112,7 +113,7 @@ def tile_moe_loc_lin_gelu_kernel(
             nc.sync.dma_start(raw_23[:, :, cols], xo_planes[:, 2:4, cols])
         load_gates(slice(0, C))
         load_w_scales(0)
-        for e in range(E):
+        for e in FAR_ORDER:
             if e == SHARE:
                 load_w_scales(1)
             load_w(e)
@@ -218,7 +219,8 @@ def tile_moe_loc_lin_gelu_kernel(
         def activate(c, t, bank):
             codes, scales = quantised[c]
             acc = psum.tile([P, width(c)], F32, name="own_acc", tag="bank%d" % bank)
-            for i, e in enumerate(CHUNKS[c]):
+            for e in sorted(CHUNKS[c], key=FAR_ORDER.index, reverse=True):
+                i = e - CHUNKS[c][0]
                 slots = slice(i * C, (i + 1) * C)
                 multiply(acc[:, slots], e, t, codes[:, slots], scales[:, slots])
             nc.scalar.activation(y[:, t, span(c)], acc[:], GELU)
@@ -243,13 +245,13 @@ def tile_moe_loc_lin_gelu_kernel(
             queue.dma_start(out[t * P : (t + 1) * P, :T], own_out[t][:])
 
         split = TILE_3_ON_VECTOR
-        halfway = 704
+        halfway = (split + T) // 2
         a, b, c = CUTS_OF_2
 
-        for e in range(E):
-            if e == 3:
+        for bank, e in enumerate(FAR_ORDER):
+            if bank == 3:
                 activate_first(1)
-            far(e, e)
+            far(e, bank)
         for t, bank in zip(TILE_ORDER, (0, 2, 3, 1)):
             activate(1, t, bank)
         for t, bank in zip((1, 3, 2, 0), (4, 5, 6, 7)):

@@ -29,10 +29,11 @@ FAR_ORDER = (0, 2, 3, 4, 5, 6, 1, 7)
 TILE_ORDER = (3, 1, 0, 2)
 WINDOW = 4 * T
 LOW = {
-    "own_out1": 0, "own_out0": WINDOW, "grouped2": WINDOW - 64,
-    "gated0_0": 2 * WINDOW, "gated0_128": 2 * WINDOW + 4 * C, "gated0_256": 2 * WINDOW + 8 * C,
-    "gated1_0": 3 * WINDOW, "gated1_128": 3 * WINDOW + 4 * C, "gated1_384": 3 * WINDOW + 12 * C,
-    "gated3_0": 4 * WINDOW, "gated3_128": 4 * WINDOW + 4 * C, "gated2_0": 5 * WINDOW,
+    "own_out1": 0, "grouped2": WINDOW - 64, "gated0_0": WINDOW, "gated2_0": WINDOW + 4 * C,
+    "own_out0": 2 * WINDOW - 128,
+    "gated0_128": 3 * WINDOW, "gated0_256": 3 * WINDOW + 4 * C,
+    "gated1_0": 4 * WINDOW, "gated1_128": 4 * WINDOW + 4 * C, "gated1_384": 4 * WINDOW + 12 * C,
+    "gated3_0": 5 * WINDOW, "gated3_128": 5 * WINDOW + 4 * C,
     "pair_23": 6 * WINDOW, "raw_23": 7 * WINDOW, "far_words": 9 * WINDOW, "far_bytes": 9 * WINDOW + WINDOW // 2,
 }
 HIGH = {
@@ -249,10 +250,10 @@ def tile_moe_loc_lin_gelu_kernel(
         a, b, c = CUTS_OF_2
 
         for bank, e in enumerate(FAR_ORDER):
-            if bank == 3:
-                activate_first(1)
+            if bank == 2:
+                activate_first(0)
             far(e, bank)
-        for t, bank in zip(TILE_ORDER, (0, 2, 3, 1)):
+        for t, bank in zip(TILE_ORDER, (1, 2, 3, 0)):
             activate(1, t, bank)
         for t, bank in zip((1, 3, 2, 0), (4, 5, 6, 7)):
             activate(2, t, bank)

@@ -148,8 +148,7 @@ def tile_moe_loc_lin_gelu_kernel(
             nc.scalar.copy(planes[0][:, cols], raw[0][:, cols])
         round_gpsimd(planes[0][:, last_quarter], raw[0][:, last_quarter])
         round_gpsimd(planes[1][:], raw[1][:])
-        for cols in (first_half, slice(HALF, last_quarter.start)):
-            round_gpsimd(pair_23[:, cols, :], raw_23[:, :, cols].rearrange("p j t -> p t j"))
+        round_gpsimd(pair_23[:, first_half, :], raw_23[:, :, first_half].rearrange("p j t -> p t j"))
 
         def span(c):
             return slice(CHUNKS[c][0] * C, (CHUNKS[c][-1] + 1) * C)
@@ -161,18 +160,19 @@ def tile_moe_loc_lin_gelu_kernel(
             return own_list[:, slots.start // PER_COL : slots.stop // PER_COL]
 
         grouped_0 = sbuf([P, C, PACK], BF16, "grouped0")
-        picked = {c: sbuf([P, 2 if c else 1, width(c)], U32, "picked%d" % c) for c in range(len(CHUNKS))}
+        picked = {c: sbuf([P, 2, width(c)], U32, "picked%d" % c) for c in (1, 2)}
         for j in range(2):
             for c in range(len(CHUNKS)):
-                dst = picked[c][:, 0, :].bitcast(BF16).rearrange("p (s j) -> p s j", j=2)[:, :, j]
+                if c == 0:
+                    dst = grouped_0[:, :, j]
+                else:
+                    dst = picked[c][:, 0, :].bitcast(BF16).rearrange("p (s j) -> p s j", j=2)[:, :, j]
                 nc.scalar.activation(dst, planes[j][:].indirect(own_offsets(span(c))), COPY)
 
-        words_0 = grouped_0[:].rearrange("p s j -> p (s j)").bitcast(I32).rearrange("p (s h) -> p s h", h=2)
-        nc.vector.tensor_copy(words_0[:, :, 0], picked[0][:, 0, :].bitcast(I32))
         for j, plane in enumerate((raw_23[:, 0, :], raw_23[:, 1, :]), 2):
             nc.vector.tensor_copy(grouped_0[:, :, j], plane.indirect(own_offsets(span(0))))
 
-        nc.vector.tensor_copy(pair_23[:, last_quarter, :], raw_23[:, :, last_quarter].rearrange("p j t -> p t j"))
+        nc.vector.tensor_copy(pair_23[:, second_half, :], raw_23[:, :, second_half].rearrange("p j t -> p t j"))
 
         grouped = {0: grouped_0[:].rearrange("p s j -> p (s j)")}
         quantised = {}

@@ -23,27 +23,45 @@ NT = N // P
 PER_COL = 16
 SHARE = 4
 HALF = T // 2
+WORD = 4
+ALIGN = 64
 
 CHUNKS = ((0,), (1, 2, 3), (4, 5, 6, 7))
 FAR_ORDER = (0, 2, 3, 4, 5, 6, 1, 7)
-TILE_ORDER = (3, 1, 0, 2)
-WINDOW = 4 * T
+TILE_BANKS = {1: ((3, 1), (1, 2), (0, 3), (2, 0)), 2: ((1, 4), (3, 5), (2, 6), (0, 7))}
+TILE_3_ON_VECTOR = 320
+CUTS_OF_2 = (448, 736)
+CUT_OF_3 = 672
+
+ROW = T * WORD
 LOW = {
-    "own_out1": 0, "grouped2": WINDOW - 64, "gated0_0": WINDOW, "gated2_0": WINDOW + 4 * C,
-    "own_out0": 2 * WINDOW - 128,
-    "gated0_128": 3 * WINDOW, "gated0_256": 3 * WINDOW + 4 * C,
-    "gated1_0": 4 * WINDOW, "gated1_128": 4 * WINDOW + 4 * C, "gated1_384": 4 * WINDOW + 12 * C,
-    "gated3_0": 5 * WINDOW, "gated3_128": 5 * WINDOW + 4 * C,
-    "pair_23": 6 * WINDOW, "raw_23": 7 * WINDOW, "far_words": 9 * WINDOW, "far_bytes": 9 * WINDOW + WINDOW // 2,
+    "own_out1": 0,
+    "grouped2": ROW - ALIGN,
+    "gated0_0": ROW,
+    "gated2_0": ROW + C * WORD,
+    "own_out0": 2 * ROW - 2 * ALIGN,
+    "gated0_128": 3 * ROW,
+    "gated0_256": 3 * ROW + C * WORD,
+    "gated1_0": 4 * ROW,
+    "gated1_128": 4 * ROW + C * WORD,
+    "gated1_384": 4 * ROW + 3 * C * WORD,
+    "gated3_0": 5 * ROW,
+    "gated3_128": 5 * ROW + C * WORD,
+    "pair_23": 6 * ROW,
+    "raw_23": 7 * ROW,
+    "far_words": 9 * ROW,
+    "far_bytes": 9 * ROW + Q * WORD,
 }
 HIGH = {
-    "codes2": 0, "gated2_128": 0,
-    "grouped1": WINDOW, "own_out3": WINDOW,
-    "codes1": 2 * WINDOW, "own_out2": 2 * WINDOW,
-    "plane0": 3 * WINDOW, "plane1": 3 * WINDOW + WINDOW // 2,
+    "codes2": 0,
+    "gated2_128": 0,
+    "grouped1": ROW,
+    "own_out3": ROW,
+    "codes1": 2 * ROW,
+    "own_out2": 2 * ROW,
+    "plane0": 3 * ROW,
+    "plane1": 3 * ROW + ROW // 2,
 }
-TILE_3_ON_VECTOR = 320
-CUTS_OF_2 = (C, 448, 736)
 
 
 def tile_moe_loc_lin_gelu_kernel(
@@ -59,8 +77,8 @@ def tile_moe_loc_lin_gelu_kernel(
         def sbuf(shape, dtype, name):
             for pool, places in ((low, LOW), (high, HIGH)):
                 if name in places:
-                    return pool.tile(shape, dtype, name=name, align_bytes=64, offset=places[name])
-            return keep.tile(shape, dtype, name=name, align_bytes=64)
+                    return pool.tile(shape, dtype, name=name, align_bytes=ALIGN, offset=places[name])
+            return keep.tile(shape, dtype, name=name, align_bytes=ALIGN)
 
         own_list = keep.tile([P, E * C // PER_COL], U16, name="own_list")
         far_list = keep.tile([P, E * C // PER_COL], U16, name="far_list")
@@ -83,6 +101,12 @@ def tile_moe_loc_lin_gelu_kernel(
         nc.vector.memset(zeros[:], 0.0)
         nc.scalar.activation(gelu_of_zeros[:], zeros[:], GELU)
 
+        def load_far_bytes(quad):
+            nc.sync.dma_start(
+                far_bytes[32 * quad : 32 * quad + 4, :].bitcast(I32),
+                x_scales[0, 4 * quad : 4 * quad + 4, :].bitcast(I32),
+            )
+
         def load_w_scales(g):
             for quad in range(4):
                 nc.sync.dma_start(
@@ -103,20 +127,16 @@ def tile_moe_loc_lin_gelu_kernel(
         for cols in (first_half, second_half):
             nc.sync.dma_start(raw[0][:, cols], xo_planes[:, 0, cols])
         nc.sync.dma_start(own_list[:], offs)
-        for quad in range(4):
-            if quad == 1:
-                nc.sync.dma_start(raw[1][:], xo_planes[:, 1, :])
-            nc.sync.dma_start(
-                far_bytes[32 * quad : 32 * quad + 4, :].bitcast(I32),
-                x_scales[0, 4 * quad : 4 * quad + 4, :].bitcast(I32),
-            )
+        load_far_bytes(0)
+        nc.sync.dma_start(raw[1][:], xo_planes[:, 1, :])
+        for quad in range(1, 4):
+            load_far_bytes(quad)
         for cols in (first_half, second_half):
             nc.sync.dma_start(raw_23[:, :, cols], xo_planes[:, 2:4, cols])
         load_gates(slice(0, C))
-        load_w_scales(0)
         for e in FAR_ORDER:
-            if e == SHARE:
-                load_w_scales(1)
+            if e % SHARE == 0:
+                load_w_scales(e // SHARE)
             load_w(e)
         load_gates(slice(C, HALF))
         load_gates(second_half)
@@ -135,10 +155,10 @@ def tile_moe_loc_lin_gelu_kernel(
 
         far_scales = [sbuf([P, 2 * C], U8, "far_scales%d" % g) for g in range(E // 2)]
         far_codes = [sbuf([P, 2 * C], U32, "far_codes%d" % g) for g in range(E // 2)]
-        for dst, window in ((far_codes, far_words[:].bitcast(U32)), (far_scales, far_bytes[:])):
+        for tiles, table in ((far_codes, far_words[:].bitcast(U32)), (far_scales, far_bytes[:])):
             for g in range(E // 2):
                 offsets = far_list[:, 2 * g * C // PER_COL : 2 * (g + 1) * C // PER_COL]
-                nc.vector.tensor_copy(dst[g][:], window.indirect(offsets))
+                nc.vector.tensor_copy(tiles[g][:], table.indirect(offsets))
 
         def round_gpsimd(dst, src):
             nc.gpsimd.tensor_scalar(dst, src, 1.0, 0.0, MULT, ADD)
@@ -148,7 +168,8 @@ def tile_moe_loc_lin_gelu_kernel(
             nc.scalar.copy(planes[0][:, cols], raw[0][:, cols])
         round_gpsimd(planes[0][:, last_quarter], raw[0][:, last_quarter])
         round_gpsimd(planes[1][:], raw[1][:])
-        round_gpsimd(pair_23[:, first_half, :], raw_23[:, :, first_half].rearrange("p j t -> p t j"))
+        raw_pairs = raw_23[:].rearrange("p j t -> p t j")
+        round_gpsimd(pair_23[:, first_half, :], raw_pairs[:, first_half, :])
 
         def span(c):
             return slice(CHUNKS[c][0] * C, (CHUNKS[c][-1] + 1) * C)
@@ -161,18 +182,16 @@ def tile_moe_loc_lin_gelu_kernel(
 
         grouped_0 = sbuf([P, C, PACK], BF16, "grouped0")
         picked = {c: sbuf([P, 2, width(c)], U32, "picked%d" % c) for c in (1, 2)}
+        first_pairs = {0: grouped_0[:, :, :2]}
+        for c in (1, 2):
+            first_pairs[c] = picked[c][:, 0, :].bitcast(BF16).rearrange("p (s j) -> p s j", j=2)
         for j in range(2):
             for c in range(len(CHUNKS)):
-                if c == 0:
-                    dst = grouped_0[:, :, j]
-                else:
-                    dst = picked[c][:, 0, :].bitcast(BF16).rearrange("p (s j) -> p s j", j=2)[:, :, j]
-                nc.scalar.activation(dst, planes[j][:].indirect(own_offsets(span(c))), COPY)
+                nc.scalar.activation(first_pairs[c][:, :, j], planes[j][:].indirect(own_offsets(span(c))), COPY)
 
-        for j, plane in enumerate((raw_23[:, 0, :], raw_23[:, 1, :]), 2):
-            nc.vector.tensor_copy(grouped_0[:, :, j], plane.indirect(own_offsets(span(0))))
-
-        nc.vector.tensor_copy(pair_23[:, second_half, :], raw_23[:, :, second_half].rearrange("p j t -> p t j"))
+        for j in range(2):
+            nc.vector.tensor_copy(grouped_0[:, :, 2 + j], raw_23[:, j, :].indirect(own_offsets(span(0))))
+        nc.vector.tensor_copy(pair_23[:, second_half, :], raw_pairs[:, second_half, :])
 
         grouped = {0: grouped_0[:].rearrange("p s j -> p (s j)")}
         quantised = {}
@@ -189,9 +208,9 @@ def tile_moe_loc_lin_gelu_kernel(
             grouped[c] = tile[:].rearrange("p s h -> p (s h)").bitcast(BF16)
 
         quantise(0)
-        window_23 = pair_23[:].rearrange("p t j -> p (t j)").bitcast(U32)
+        words_23 = pair_23[:].rearrange("p t j -> p (t j)").bitcast(U32)
         for c in (1, 2):
-            nc.vector.tensor_copy(picked[c][:, 1, :], window_23.indirect(own_offsets(span(c))))
+            nc.vector.tensor_copy(picked[c][:, 1, :], words_23.indirect(own_offsets(span(c))))
         for step in (weave, quantise):
             for c in (1, 2):
                 step(c)
@@ -200,13 +219,13 @@ def tile_moe_loc_lin_gelu_kernel(
         out_tiles = out.rearrange("(t p) c -> p t c", p=P)
         z = [sbuf([P, NT, 2 * C], F32, "z%d" % g) for g in range(E // 2)]
 
-        def far(e, bank):
+        def far(e, bank, bias=0.0):
             acc = psum.tile([P, NT, C], F32, name="far_acc", tag="bank%d" % bank)
             g, i = divmod(e, 2)
             slots = slice(i * C, (i + 1) * C)
             for t in range(NT):
                 multiply(acc[:, t, :], e, t, far_codes[g][:, slots], far_scales[g][:, slots])
-            nc.scalar.activation(z[g][:, :, i * C : (i + 1) * C], acc[:], GELU, bias=gelu_of_zeros[:, 0:1] if e == 0 else 0.0)
+            nc.scalar.activation(z[g][:, :, i * C : (i + 1) * C], acc[:], GELU, bias=bias)
             if i == 1:
                 nc.sync.dma_start(out_tiles[:, :, T + 2 * g * C : T + 2 * (g + 1) * C], z[g][:])
 
@@ -214,15 +233,15 @@ def tile_moe_loc_lin_gelu_kernel(
             codes, scales = quantised[0]
             acc = psum.tile([P, NT, C], F32, name="first_acc", tag="bank%d" % bank)
             for t in range(NT):
-                multiply(acc[:, t, :], 0, t, codes[:], scales[:])
+                multiply(acc[:, t, :], CHUNKS[0][0], t, codes[:], scales[:])
             nc.scalar.activation(y[:, :, span(0)], acc[:], GELU)
 
         def activate(c, t, bank):
             codes, scales = quantised[c]
             acc = psum.tile([P, width(c)], F32, name="own_acc", tag="bank%d" % bank)
             for e in sorted(CHUNKS[c], key=FAR_ORDER.index, reverse=True):
-                i = e - CHUNKS[c][0]
-                slots = slice(i * C, (i + 1) * C)
+                place = e - CHUNKS[c][0]
+                slots = slice(place * C, (place + 1) * C)
                 multiply(acc[:, slots], e, t, codes[:, slots], scales[:, slots])
             nc.scalar.activation(y[:, t, span(c)], acc[:], GELU)
 
@@ -245,52 +264,44 @@ def tile_moe_loc_lin_gelu_kernel(
         def store_own(t, queue):
             queue.dma_start(out[t * P : (t + 1) * P, :T], own_out[t][:])
 
-        split = TILE_3_ON_VECTOR
-        halfway = (split + T) // 2
-        a, b, c = CUTS_OF_2
+        far(FAR_ORDER[0], 0, gelu_of_zeros[:, 0:1])
+        activate_first(E - 1)
+        for bank in range(1, E):
+            far(FAR_ORDER[bank], bank)
+        for c in (1, 2):
+            for t, bank in TILE_BANKS[c]:
+                activate(c, t, bank)
 
-        for bank, e in enumerate(FAR_ORDER):
-            if bank == 2:
-                activate_first(0)
-            far(e, bank)
-        for t, bank in zip(TILE_ORDER, (1, 2, 3, 0)):
-            activate(1, t, bank)
-        for t, bank in zip((1, 3, 2, 0), (4, 5, 6, 7)):
-            activate(2, t, bank)
-
+        middle_of_2, end_of_2 = CUTS_OF_2
+        for t in (3, 1, 0, 2):
+            apply_gate(t, 0, C)
         for t, lo, hi in (
-            (3, 0, C),
-            (1, 0, C),
-            (0, 0, C),
-            (2, 0, C),
-            (3, C, split),
+            (3, C, TILE_3_ON_VECTOR),
             (1, C, 3 * C),
             (0, C, 2 * C),
-            (2, a, b),
+            (2, C, middle_of_2),
             (1, 3 * C, T),
-            (3, split, halfway),
-            (2, b, c),
+            (3, TILE_3_ON_VECTOR, CUT_OF_3),
+            (2, middle_of_2, end_of_2),
             (0, 2 * C, T),
-            (3, halfway, T),
-            (2, c, T),
+            (3, CUT_OF_3, T),
+            (2, end_of_2, T),
         ):
             apply_gate(t, lo, hi)
 
-        scatter_vector(3, 0)
-        scatter_vector(1, 0)
-        scatter_vector(0, 0)
-        scatter_vector(2, 0)
+        for t in (3, 1, 0, 2):
+            scatter_vector(t, 0)
         scatter_vector(3, C)
         scatter_vector(1, C)
-        scatter_scalar(2, a)
+        scatter_scalar(2, C)
         scatter_vector(0, C)
-        scatter_scalar(3, split)
+        scatter_scalar(3, TILE_3_ON_VECTOR)
         scatter_vector(1, 3 * C)
         store_own(1, nc.sync)
-        scatter_scalar(2, b)
-        scatter_scalar(3, halfway)
+        scatter_scalar(2, middle_of_2)
+        scatter_scalar(3, CUT_OF_3)
         store_own(3, nc.sync)
-        scatter_scalar(2, c)
+        scatter_scalar(2, end_of_2)
         store_own(2, nc.scalar)
         scatter_vector(0, 2 * C)
         store_own(0, nc.sync)

from contextlib import ExitStack

import concourse.mybir as mybir

K, T, Q, E, C, N = 512, 1024, 512, 8, 128, 512
FLOPS = 2 * K * N * 2 * E * C

F32 = mybir.dt.float32
BF16 = mybir.dt.bfloat16
I32 = mybir.dt.int32
U32 = mybir.dt.uint32
U16 = mybir.dt.uint16
U8 = mybir.dt.uint8
FP8X4 = mybir.dt.float8_e4m3fn_x4
GELU = mybir.ActivationFunctionType.Gelu_apprx_tanh
COPY = mybir.ActivationFunctionType.Copy
MULT = mybir.AluOpType.mult
ADD = mybir.AluOpType.add

P = 128
PACK = 4
NT = N // P
PER_COL = 16
SHARE = 4
HALF = T // 2
WORD = 4
ALIGN = 64

CHUNKS = ((0,), (1, 2, 3), (4, 5, 6, 7))
FAR_ORDER = (0, 2, 3, 4, 5, 6, 1, 7)
TILE_BANKS = {1: ((3, 1), (1, 2), (0, 3), (2, 0)), 2: ((1, 4), (3, 5), (2, 6), (0, 7))}
TILE_3_ON_VECTOR = 320
CUTS_OF_2 = (448, 736)
CUT_OF_3 = 672

ROW = T * WORD
LOW = {
    "own_out1": 0,
    "grouped2": ROW - ALIGN,
    "gated0_0": ROW,
    "gated2_0": ROW + C * WORD,
    "own_out0": 2 * ROW - 2 * ALIGN,
    "gated0_128": 3 * ROW,
    "gated0_256": 3 * ROW + C * WORD,
    "gated1_0": 4 * ROW,
    "gated1_128": 4 * ROW + C * WORD,
    "gated1_384": 4 * ROW + 3 * C * WORD,
    "gated3_0": 5 * ROW,
    "gated3_128": 5 * ROW + C * WORD,
    "pair_23": 6 * ROW,
    "raw_23": 7 * ROW,
    "far_words": 9 * ROW,
    "far_bytes": 9 * ROW + Q * WORD,
}
HIGH = {
    "codes2": 0,
    "gated2_128": 0,
    "grouped1": ROW,
    "own_out3": ROW,
    "codes1": 2 * ROW,
    "own_out2": 2 * ROW,
    "plane0": 3 * ROW,
    "plane1": 3 * ROW + ROW // 2,
}


def tile_moe_loc_lin_gelu_kernel(
    tc, x_words, x_scales, xo, w_words, w_scales, gate, offs, offs2, out
):
    nc = tc.nc
    with ExitStack() as ctx:
        low = ctx.enter_context(tc.tile_pool(name="low", bufs=1))
        keep = ctx.enter_context(tc.tile_pool(name="keep", bufs=1))
        high = ctx.enter_context(tc.tile_pool(name="high", bufs=1))
        psum = ctx.enter_context(tc.psum_pool(name="psum", bufs=1))

        def sbuf(shape, dtype, name):
            for pool, places in ((low, LOW), (high, HIGH)):
                if name in places:
                    return pool.tile(shape, dtype, name=name, align_bytes=ALIGN, offset=places[name])
            return keep.tile(shape, dtype, name=name, align_bytes=ALIGN)

        own_list = keep.tile([P, E * C // PER_COL], U16, name="own_list")
        far_list = keep.tile([P, E * C // PER_COL], U16, name="far_list")
        far_words = sbuf([P, Q], I32, "far_words")
        far_bytes = sbuf([P, Q], U8, "far_bytes")
        w_scale_tiles = [sbuf([P, N], U8, "w_scales%d" % g) for g in range(E // SHARE)]
        raw = [sbuf([P, T], F32, "raw%d" % j) for j in range(2)]
        raw_23 = sbuf([P, 2, T], F32, "raw_23")
        planes = [sbuf([P, T], BF16, "plane%d" % j) for j in range(2)]
        pair_23 = sbuf([P, T, 2], BF16, "pair_23")
        gates = sbuf([P, E * C], F32, "gates")
        w_of = [sbuf([P, N], I32, "w_codes%d" % e) for e in range(E)]

        nc.vector.memset(far_bytes[:].bitcast(I32), 0)
        for tile in w_scale_tiles:
            nc.vector.memset(tile[:].bitcast(I32), 0)

        zeros = sbuf([P, 16], F32, "zeros")
        gelu_of_zeros = sbuf([P, 16], F32, "gelu_of_zeros")
        nc.vector.memset(zeros[:], 0.0)
        nc.scalar.activation(gelu_of_zeros[:], zeros[:], GELU)

        def load_far_bytes(quad):
            nc.sync.dma_start(
                far_bytes[32 * quad : 32 * quad + 4, :].bitcast(I32),
                x_scales[0, 4 * quad : 4 * quad + 4, :].bitcast(I32),
            )

        def load_w_scales(g):
            for quad in range(4):
                nc.sync.dma_start(
                    w_scale_tiles[g][32 * quad : 32 * quad + 4 * SHARE, :].bitcast(I32),
                    w_scales[SHARE * g : SHARE * (g + 1), 0, 4 * quad : 4 * quad + 4, :].bitcast(I32),
                )

        def load_w(e):
            nc.sync.dma_start(w_of[e][:], w_words[e, 0].rearrange("p n d -> p (n d)").bitcast(I32))

        def load_gates(cols):
            nc.sync.dma_start(gates[:, cols], gate[:, cols])

        xo_planes = xo.rearrange("(p j) t -> p j t", j=PACK)
        first_half, second_half = slice(0, HALF), slice(HALF, T)
        nc.sync.dma_start(far_words[:], x_words[0].rearrange("p t d -> p (t d)").bitcast(I32))
        nc.sync.dma_start(far_list[:], offs2)
        for cols in (first_half, second_half):
            nc.sync.dma_start(raw[0][:, cols], xo_planes[:, 0, cols])
        nc.sync.dma_start(own_list[:], offs)
        load_far_bytes(0)
        nc.sync.dma_start(raw[1][:], xo_planes[:, 1, :])
        for quad in range(1, 4):
            load_far_bytes(quad)
        for cols in (first_half, second_half):
            nc.sync.dma_start(raw_23[:, :, cols], xo_planes[:, 2:4, cols])
        load_gates(slice(0, C))
        for e in FAR_ORDER:
            if e % SHARE == 0:
                load_w_scales(e // SHARE)
            load_w(e)
        load_gates(slice(C, HALF))
        load_gates(second_half)

        def multiply(acc, e, t, codes, scales):
            cols = slice(t * P, (t + 1) * P)
            nc.tensor.matmul_mx(
                out=acc,
                lhsT=w_of[e][:, cols].bitcast(FP8X4),
                lhsT_scale=w_scale_tiles[e // SHARE][4 * (e % SHARE) :, cols],
                rhs=codes.bitcast(FP8X4),
                rhs_scale=scales,
                start=True,
                stop=True,
            )

        far_scales = [sbuf([P, 2 * C], U8, "far_scales%d" % g) for g in range(E // 2)]
        far_codes = [sbuf([P, 2 * C], U32, "far_codes%d" % g) for g in range(E // 2)]
        for tiles, table in ((far_codes, far_words[:].bitcast(U32)), (far_scales, far_bytes[:])):
            for g in range(E // 2):
                offsets = far_list[:, 2 * g * C // PER_COL : 2 * (g + 1) * C // PER_COL]
                nc.vector.tensor_copy(tiles[g][:], table.indirect(offsets))

        def round_gpsimd(dst, src):
            nc.gpsimd.tensor_scalar(dst, src, 1.0, 0.0, MULT, ADD)

        last_quarter = slice(T - T // 4, T)
        for cols in (first_half, slice(HALF, last_quarter.start)):
            nc.scalar.copy(planes[0][:, cols], raw[0][:, cols])
        round_gpsimd(planes[0][:, last_quarter], raw[0][:, last_quarter])
        round_gpsimd(planes[1][:], raw[1][:])
        raw_pairs = raw_23[:].rearrange("p j t -> p t j")
        round_gpsimd(pair_23[:, first_half, :], raw_pairs[:, first_half, :])

        def span(c):
            return slice(CHUNKS[c][0] * C, (CHUNKS[c][-1] + 1) * C)

        def width(c):
            return len(CHUNKS[c]) * C

        def own_offsets(slots):
            return own_list[:, slots.start // PER_COL : slots.stop // PER_COL]

        grouped_0 = sbuf([P, C, PACK], BF16, "grouped0")
        picked = {c: sbuf([P, 2, width(c)], U32, "picked%d" % c) for c in (1, 2)}
        first_pairs = {0: grouped_0[:, :, :2]}
        for c in (1, 2):
            first_pairs[c] = picked[c][:, 0, :].bitcast(BF16).rearrange("p (s j) -> p s j", j=2)
        for j in range(2):
            for c in range(len(CHUNKS)):
                nc.scalar.activation(first_pairs[c][:, :, j], planes[j][:].indirect(own_offsets(span(c))), COPY)

        for j in range(2):
            nc.vector.tensor_copy(grouped_0[:, :, 2 + j], raw_23[:, j, :].indirect(own_offsets(span(0))))
        nc.vector.tensor_copy(pair_23[:, second_half, :], raw_pairs[:, second_half, :])

        grouped = {0: grouped_0[:].rearrange("p s j -> p (s j)")}
        quantised = {}

        def quantise(c):
            codes = sbuf([P, width(c)], U32, "codes%d" % c)
            scales = sbuf([P, width(c)], U8, "scales%d" % c)
            nc.vector.quantize_mx(out=codes[:].bitcast(FP8X4), scales=scales[:], in_=grouped[c])
            quantised[c] = codes, scales

        def weave(c):
            tile = sbuf([P, width(c), 2], I32, "grouped%d" % c)
            nc.vector.tensor_copy(tile[:], picked[c][:].bitcast(I32).rearrange("p h s -> p s h"))
            grouped[c] = tile[:].rearrange("p s h -> p (s h)").bitcast(BF16)

        quantise(0)
        words_23 = pair_23[:].rearrange("p t j -> p (t j)").bitcast(U32)
        for c in (1, 2):
            nc.vector.tensor_copy(picked[c][:, 1, :], words_23.indirect(own_offsets(span(c))))
        for step in (weave, quantise):
            for c in (1, 2):
                step(c)

        y = sbuf([P, NT, E * C], F32, "y")
        out_tiles = out.rearrange("(t p) c -> p t c", p=P)
        z = [sbuf([P, NT, 2 * C], F32, "z%d" % g) for g in range(E // 2)]

        def far(e, bank, bias=0.0):
            acc = psum.tile([P, NT, C], F32, name="far_acc", tag="bank%d" % bank)
            g, i = divmod(e, 2)
            slots = slice(i * C, (i + 1) * C)
            for t in range(NT):
                multiply(acc[:, t, :], e, t, far_codes[g][:, slots], far_scales[g][:, slots])
            nc.scalar.activation(z[g][:, :, i * C : (i + 1) * C], acc[:], GELU, bias=bias)
            if i == 1:
                nc.sync.dma_start(out_tiles[:, :, T + 2 * g * C : T + 2 * (g + 1) * C], z[g][:])

        def activate_first(bank):
            codes, scales = quantised[0]
            acc = psum.tile([P, NT, C], F32, name="first_acc", tag="bank%d" % bank)
            for t in range(NT):
                multiply(acc[:, t, :], CHUNKS[0][0], t, codes[:], scales[:])
            nc.scalar.activation(y[:, :, span(0)], acc[:], GELU)

        def activate(c, t, bank):
            codes, scales = quantised[c]
            acc = psum.tile([P, width(c)], F32, name="own_acc", tag="bank%d" % bank)
            for e in sorted(CHUNKS[c], key=FAR_ORDER.index, reverse=True):
                place = e - CHUNKS[c][0]
                slots = slice(place * C, (place + 1) * C)
                multiply(acc[:, slots], e, t, codes[:, slots], scales[:, slots])
            nc.scalar.activation(y[:, t, span(c)], acc[:], GELU)

        own_out = [sbuf([P, T], F32, "own_out%d" % t) for t in range(NT)]
        gated = {}

        def apply_gate(t, lo, hi):
            gated[t, lo] = sbuf([P, hi - lo], F32, "gated%d_%d" % (t, lo))
            nc.gpsimd.tensor_tensor(gated[t, lo][:], y[:, t, lo:hi], gates[:, lo:hi], MULT)

        def window(t, lo):
            return own_out[t][:].indirect(own_offsets(slice(lo, lo + gated[t, lo].shape[1])))

        def scatter_scalar(t, lo):
            nc.scalar.activation(window(t, lo), gated[t, lo][:], COPY)

        def scatter_vector(t, lo):
            nc.vector.tensor_copy(window(t, lo), gated[t, lo][:])

        def store_own(t, queue):
            queue.dma_start(out[t * P : (t + 1) * P, :T], own_out[t][:])

        far(FAR_ORDER[0], 0, gelu_of_zeros[:, 0:1])
        activate_first(E - 1)
        for bank in range(1, E):
            far(FAR_ORDER[bank], bank)
        for c in (1, 2):
            for t, bank in TILE_BANKS[c]:
                activate(c, t, bank)

        middle_of_2, end_of_2 = CUTS_OF_2
        for t in (3, 1, 0, 2):
            apply_gate(t, 0, C)
        for t, lo, hi in (
            (3, C, TILE_3_ON_VECTOR),
            (1, C, 3 * C),
            (0, C, 2 * C),
            (2, C, middle_of_2),
            (1, 3 * C, T),
            (3, TILE_3_ON_VECTOR, CUT_OF_3),
            (2, middle_of_2, end_of_2),
            (0, 2 * C, T),
            (3, CUT_OF_3, T),
            (2, end_of_2, T),
        ):
            apply_gate(t, lo, hi)

        for t in (3, 1, 0, 2):
            scatter_vector(t, 0)
        scatter_vector(3, C)
        scatter_vector(1, C)
        scatter_scalar(2, C)
        scatter_vector(0, C)
        scatter_scalar(3, TILE_3_ON_VECTOR)
        scatter_vector(1, 3 * C)
        store_own(1, nc.sync)
        scatter_scalar(2, middle_of_2)
        scatter_scalar(3, CUT_OF_3)
        store_own(3, nc.sync)
        scatter_scalar(2, end_of_2)
        store_own(2, nc.scalar)
        scatter_vector(0, 2 * C)
        store_own(0, nc.sync)
